import numpy as np, ml_dtypes
CORES = [9,25,41,57]
N = 4
BF = ml_dtypes.bfloat16
def gentries(a):
    return np.ascontiguousarray(a.reshape(8, 16, -1).transpose(0, 2, 1)).reshape(8, -1)
def gtable(e):
    e = np.asarray(e); return np.ascontiguousarray(e.reshape(8, -1, 16).transpose(0, 2, 1)).reshape(128, -1).astype(np.int32)
V, R, L, S = 4096, 256, 4, 2
def trees(rng, deep):
    T = N * 8; ar = np.arange(T); P = V // 2 - 1; i = np.arange(P)[:, None]
    pair = 2 * (np.argsort(rng.random((T, P)), axis=1) + 1); side = rng.integers(0, 2, (P, T))
    pick = np.where(rng.random((P, T)) < deep, i, np.minimum((rng.random((P, T)) * (i + 1)).astype(np.int64), i))
    kid = np.full((T, V), -1, np.int64); up = np.zeros((T, V), np.int64); leaf = np.zeros((T, P + 1), np.int64); cnt = np.ones((T, V), np.int64)
    for t in range(P):
        j = pick[t]; n = leaf[ar, j]; k = pair[:, t]; b = side[t]
        kid[ar, n] = k; up[ar, k] = n; up[ar, k + 1] = n
        leaf[ar, j] = k + b; leaf[ar, t + 1] = k + 1 - b
    for t in range(P - 1, -1, -1):
        k = pair[:, t]; cnt[ar, up[ar, k]] = cnt[ar, k] + cnt[ar, k + 1]
    return kid, up, cnt
def quads(rng, kid, cnt, top, drop):
    T = N * 8; Q = 4 * R; ar = np.arange(T)[:, None]; ar3 = ar[:, :, None]
    ok = cnt >= 4; order = np.argsort(~ok, axis=1, kind="stable"); num = np.sum(ok, axis=1)[:, None]
    x = order[ar, np.minimum((rng.random((T, Q)) * num).astype(np.int64), num - 1)]
    c = np.full((T, Q, 4), -1, np.int64); c[:, :, 0] = np.where(rng.random((T, Q)) < top, 0, x)
    for w in (1, 2, 3):
        k = kid[ar3, np.maximum(c, 0)]
        t = np.argmax(np.where((c >= 0) & (k >= 0), rng.random(c.shape), -1.0), axis=2)[..., None]
        k = np.take_along_axis(k, t, 2); np.put_along_axis(c, t, k, 2); c[:, :, w] = k[..., 0] + 1
    m = rng.random((T, Q, 1)) < drop
    for w in range(4):
        k = kid[ar3, c]; go = m & (k >= 0) & (rng.random(c.shape) < 0.3)
        c = np.where(go, k + rng.integers(0, 2, c.shape), c)
    return np.take_along_axis(c, np.argsort(rng.random(c.shape), axis=2), 2)
def parts(rng, deep=0.2, top=0.15, drop=0.5):
    kid, up, cnt = trees(rng, deep)
    return {"s": rng.integers(0, 256, (N, 8, 16, V)), "m": rng.integers(0, 256, (N, 8, 16, V)), "kid": kid, "up": up,
            "a": rng.integers(0, 256, (N, 8, 16, R)), "a0": rng.integers(0, 256, (N, 8, 16, R)), "lk": rng.integers(0, R, (N, 8, L, R)), "cut0": quads(rng, kid, cnt, top, drop)}
def pack(d):
    q = {}
    for k in ("s", "m", "kid", "up", "a", "a0", "lk", "cut0"):
        v = d[k]
        if k in ("kid", "up"): q[k] = np.ascontiguousarray(v.reshape(N, 8, V)).astype(np.int32)
        elif k in ("lk", "cut0"): q[k] = np.stack([gtable(x) for x in v.reshape(N, 8, -1)])
        else: q[k] = np.ascontiguousarray(v.reshape(N, 128, -1)).astype(np.float32).astype(BF)
    return q
def setup_inputs(rng):
    return pack(parts(rng))
def setup_inputs_ties(rng):
    d = parts(rng, 0.2, 0.3, 0.4)
    d["a"] = rng.integers(1, 3, (N, 8, 16, R)); d["a0"] = rng.integers(1, 3, (N, 8, 16, R))
    d["s"] = np.repeat(rng.integers(0, 3, (N, 8, 1, V)) * rng.choice(np.array([1, 7, 100]), (N, 8, 1, 1)), 16, axis=2)
    d["s"][:, 3] = 7; d["s"][:, 5] = np.where(rng.random((N, 16, V)) < 0.5, 1, 2)
    return pack(d)
def setup_inputs_deep(rng):
    T = N * 8; Q = 4 * R; deep = rng.choice(np.array([0.0, 0.9, 1.0]), (1, T)); deep[0, 0] = 1.0; deep[0, T - 1] = 0.0
    d = parts(rng, deep, 0.05, 0.3); n = np.arange(V)[None, :]
    leaf = np.argsort(np.where((d["kid"] < 0) & (n != 1), n, V + n), axis=1)[:, :V // 2]
    at = rng.integers(0, V // 2 - 3, (T, Q)); at[:, 0] = 0; at[:, 1] = V // 2 - 4
    m = rng.random((T, Q)) < 0.4; m[:, :2] = True
    four = leaf[np.arange(T)[:, None, None], at[:, :, None] + np.arange(4)]
    four = np.take_along_axis(four, np.argsort(rng.random(four.shape), axis=2), 2)
    d["cut0"] = np.where(m[:, :, None], four, d["cut0"])
    return pack(d)
def top_end(rng, d, g):
    ar = np.arange(N); c = d["cut0"].reshape(N, 8, R, 4, 4).copy(); k = d["kid"].reshape(N, 8, V)[:, g]; u = d["up"].reshape(N, 8, V)[:, g]
    q = c[:, g].reshape(N, 4 * R, 4); sib = np.any(q[..., None, :] == (q ^ 1)[..., :, None], axis=3)
    q = np.take_along_axis(q, np.argsort(~sib, axis=2, kind="stable"), 2)
    inner = k[ar[:, None, None], q] >= 0; good = (np.sum(sib, axis=2) == 2) & inner[..., 2] & inner[..., 3]
    p = q[ar, np.argmax(good, axis=1)]
    c[:, g] = q.reshape(N, R, 4, 4); c[:, g, ::2, 0] = p[:, None, :]; d["cut0"] = c
    j = rng.integers(0, 16, (N, V))
    j[ar, p[:, 0]] = 2; j[ar, p[:, 1]] = 2; j[ar, u[ar, p[:, 0]]] = 2; j[ar, p[:, 2]] = 1; j[ar, p[:, 3]] = 1
    d["s"][:, g] = 255 - (np.arange(16)[None, :, None] == j[:, None, :]).astype(np.int64)
    d["a"][:, g] = rng.integers(254, 256, (N, 16, R)); d["a"][:, g, 12:] = 255; d["a"][:, g, 1, ::2] = 254; d["a"][:, g, 2, ::2] = 255
    d["a0"][:, g] = rng.integers(0, 2, (N, 16, R))
def setup_inputs_ends(rng):
    d = parts(rng)
    for k in ("s", "m", "a", "a0"):
        e = rng.random(d[k].shape); d[k] = np.where(e < 0.4, 255, np.where(e < 0.7, 0, d[k]))
    for k in ("s", "m", "a"): d[k][:, 0] = 255
    d["a"][:, 1, :, ::2] = 0; d["s"][:, 2] = 0
    d["lk"][:, ::2] = rng.choice(np.array([0, R - 1]), (N, 4, L, R))
    top_end(rng, d, 7)
    return pack(d)
def setup_inputs_alike(rng):
    d = parts(rng, 0.0, 1.0, 0.2)
    d["lk"][:, 1::2] = rng.integers(0, R, (N, 4, 1, 1))
    c = d["cut0"].reshape(N, 8, R, 16).copy(); c[:, ::2] = c[:, ::2, :1].copy(); d["cut0"] = c
    d["a"][:, :4] = np.repeat(d["a"][:, :4, :, :R // 16], 16, axis=3); d["a0"][:, 2:6, :, :R // 2] = d["a"][:, 2:6, :, :R // 2]
    return pack(d)
def setup_inputs_spread(rng):
    d = parts(rng)
    for k in ("s", "m", "a", "a0"):
        n = d[k].shape[3]; d[k] = np.floor(np.exp2(8 * rng.random((N, 8, 1, n))) * rng.random((N, 8, 16, n))).astype(np.int64)
    return pack(d)
def check_inputs(d):
    bad = []
    for k in ("s", "m", "a", "a0"):
        x = np.asarray(d[k]).astype(np.float32)
        if not np.all((x >= 0) & (x <= 255) & (x == np.floor(x))): bad.append("numbers of " + k)
    if np.min(d["lk"]) < 0 or np.max(d["lk"]) > R - 1: bad.append("range of lk")
    if np.min(d["cut0"]) < 2 or np.max(d["cut0"]) > V - 1: bad.append("range of cut0")
    T = N * 8; kid = np.asarray(d["kid"]).astype(np.int64).reshape(T, V); up = np.asarray(d["up"]).astype(np.int64).reshape(T, V)
    if np.min(kid) < -1 or np.max(kid) > V - 1 or np.min(up) < 0 or np.max(up) > V - 1: return bad + ["range of the trees"]
    ar = np.arange(T)[:, None]; n = np.arange(V)[None, :]
    ok = np.all(up[:, :2] == 0) and np.all(kid[:, 1] == -1) and np.all((kid == -1) | ((kid >= 2) & (kid % 2 == 0)))
    ok = ok and np.all(kid[ar, up][:, 2:] == (n - n % 2)[:, 2:]) and np.all(up[:, 0::2] == up[:, 1::2])
    ok = ok and np.all((kid < 0) | (up[ar, np.maximum(kid, 0)] == n))
    jump = [up]; dep = np.where(n == 0, 0, 1) + np.zeros((T, 1), np.int64); K = V.bit_length()
    for k in range(K):
        dep = dep + dep[ar, jump[-1]]; jump.append(jump[-1][ar, jump[-1]])
    if not ok or np.any(jump[-1]): return bad + ["trees"]
    if "range of cut0" in bad: return bad
    c = np.stack([gentries(np.asarray(x)) for x in d["cut0"]]).astype(np.int64).reshape(T, 4 * R, 4); wrong = False
    for i in range(4):
        for j in range(i):
            x, y = c[:, :, i], c[:, :, j]; dx, dy = dep[ar, x], dep[ar, y]
            low = np.where(dx >= dy, x, y); high = np.where(dx >= dy, y, x); dif = np.abs(dx - dy)
            for k in range(K): low = np.where(((dif >> k) & 1) > 0, jump[k][ar, low], low)
            wrong = wrong or bool(np.any(low == high))
    if wrong: bad.append("quads of cut0")
    return bad
def reference(s, m, kid, up, a, a0, lk, cut0):
    def rows(x, n): return np.ascontiguousarray(x.astype(np.float32).astype(np.int64).reshape(N, 8, 16, n).transpose(0, 1, 3, 2))
    sv, mv, av, ka = rows(s, V), rows(m, V), rows(a, R), rows(a0, R)
    kd, pu = kid.astype(np.int64), up.astype(np.int64)
    lv = np.stack([gentries(x) for x in lk]).astype(np.int64).reshape(N, 8, L, R)
    cut = np.stack([gentries(x) for x in cut0]).astype(np.int64).reshape(N, 8, R, 4, 4)
    G3 = np.arange(8)[:, None, None]; G4 = G3[..., None]; E = np.zeros((N, 8, R, 16), np.int64)
    def at(x, i): return np.take_along_axis(x, i, 3)
    for h in range(N):
        newcut = []; newa = []
        for r in range(N):
            b = (r - h) % N; x = av[b]; w = lv[b]
            dist = np.sum(np.abs(x[:, None] - ka[r][G3, w]).reshape(8, L, R, 4, 4), axis=4)
            best = np.argmin(dist, axis=1)
            own = w[G3, best, np.arange(R)[None, :, None]]
            c = cut[r][G3, own, np.arange(4)[None, None, :]]
            xx = x[:, :, None, None, :]
            for step in range(S):
                k = kd[r][G4, c]; p = pu[r][G4, c]
                err = np.where(k >= 0, np.sum(sv[r][G4, c] * xx, axis=4), -1)
                cost = np.sum(sv[r][G4, p] * xx, axis=4)
                i = np.argmax(err, axis=3)[..., None]; free = np.arange(4) != i
                mate = (c[..., None, :] == (c ^ 1)[..., :, None]) & free[..., None, :] & free[..., :, None]
                pair = np.any(mate, axis=4); j = np.argmax(pair, axis=3)[..., None]
                j2 = np.argmax(np.take_along_axis(mate, j[..., None], 3)[..., 0, :], axis=3)[..., None]
                go = np.any(pair, axis=3)[..., None] & (at(cost, j) < at(err, i)); left = at(k, i)
                new = c.copy()
                np.put_along_axis(new, i, left, 3); np.put_along_axis(new, j, at(p, j), 3); np.put_along_axis(new, j2, left + 1, 3)
                c = np.where(go, new, c)
            E[b] += x * np.sum(mv[r][G4, c], axis=(2, 3))
            newcut.append(c); newa.append(x)
        cut = np.stack(newcut); ka = np.stack(newa)
    return {"ye": np.ascontiguousarray(E.transpose(0, 1, 3, 2)).reshape(N, 128, R).astype(np.float32), "yc": np.stack([gtable(x.reshape(8, -1)) for x in cut]).astype(np.float32)}

@@ -1,0 +1,539 @@
+from concourse.bass import DstId, RemoteDMATransfer
+from concourse.mybir import AluOpType, ActivationFunctionType
+
+OP = AluOpType
+AF = ActivationFunctionType
+BIG = 8388608.0
+
+_W = {}
+_n = [0]
+for _k in "ups yd16 lab lbk kes o prk prl prr lt s1 s2 n0 n1 n2".split():
+    _W[_k] = (_n[0], 128); _n[0] += 128
+for _k in "eq peq xa na mab nab w1 w0 sab t1 tl tr u1 u2 u3 y1 y2 y3 mk lbf z zc".split():
+    _W[_k] = (_n[0], 64); _n[0] += 64
+for _k in ("pa pb ga gb ka kb ja jb pa2 pb2 lj ljp upu sib hasp mx mn ljm ljq ls lp mxm mn1 aa bb dz zr1 dab dr "
+           "fk0 fk2 fk3 d0 d1 kl kr mxu g1a k2 sl g1 gs b1 b2 bbb m0 e1 e2 e3 go2 m1").split():
+    _W[_k] = (_n[0], 32); _n[0] += 32
+
+SCRATCH = {
+    "kl": ("sbuf", [128, 256], "int32"), "ul": ("sbuf", [128, 256], "int32"),
+    "ytk": ("sbuf", [128, 256], "int32"), "ytu": ("sbuf", [128, 256], "int32"),
+    "xk": ("sbuf", [128, 256], "float32"), "xu": ("sbuf", [128, 256], "float32"),
+    "zk": ("sbuf", [128, 256], "float32"), "zu": ("sbuf", [128, 256], "float32"),
+    "lstk": ("sbuf", [128, 256], "uint16"), "lstu": ("sbuf", [128, 256], "uint16"),
+    "u1i": ("sbuf", [128, 256], "int32"),
+    "di": ("sbuf", [128, 1536], "int32"), "db": ("sbuf", [128, 2048], "bfloat16"),
+    "pn": ("sbuf", [128, 256], "int32"), "pc3": ("sbuf", [128, 2], "int32"), "adc": ("sbuf", [128, 1], "float32"),
+    "pcf": ("sbuf", [128, 1], "float32"),
+    "lki": ("sbuf", [128, 64], "int32"), "a0b": ("sbuf", [128, 256], "bfloat16"),
+    "swin": ("sbuf", [128, 4096], "bfloat16"), "mwin": ("sbuf", [128, 4096], "bfloat16"),
+    "cwin": ("sbuf", [128, 4096], "bfloat16"), "meta": ("sbuf", [128, 4096], "bfloat16"), "bt": ("sbuf", [128, 4096], "bfloat16"),
+    "ax0": ("sbuf", [128, 4096], "bfloat16"), "ax1": ("sbuf", [128, 4096], "bfloat16"),
+    "p0": ("sbuf", [128, 2048], "float32"), "p1": ("sbuf", [128, 2048], "float32"),
+    "gm0": ("sbuf", [128, 2048], "bfloat16"), "gm1": ("sbuf", [128, 2048], "bfloat16"),
+    "mg0": ("sbuf", [128, 2048], "bfloat16"), "mg1": ("sbuf", [128, 2048], "bfloat16"),
+    "df": ("sbuf", [128, 1024], "bfloat16"), "dabs": ("sbuf", [128, 1024], "bfloat16"),
+    "kd": ("sbuf", [128, 1024], "float32"), "kmn": ("sbuf", [128, 768], "float32"),
+    "mk0": ("sbuf", [128, 1024], "bfloat16"),
+    "xc": ("sbuf", [128, 256], "int32"), "xh": ("sbuf", [128, 256], "int32"), "xy": ("sbuf", [128, 256], "float32"),
+    "xw": ("sbuf", [128, 704], "float32"), "xo": ("sbuf", [128, 256], "float32"),
+    "y": ("sbuf", [128, 256], "float32"), "yn": ("sbuf", [128, 256], "float32"),
+    "pr": ("sbuf", [128, 1024], "float32"), "a2": ("sbuf", [128, 512], "float32"),
+    "cl": ("sbuf", [128, 256], "uint16"), "l2": ("sbuf", [128, 256], "uint16"), "ml": ("sbuf", [128, 256], "uint16"),
+    "w0": ("sbuf", [128, _n[0]], "float32"), "w1": ("sbuf", [128, _n[0]], "float32"),
+    "wi0": ("sbuf", [128, 128], "int32"), "wi1": ("sbuf", [128, 128], "int32"),
+    "idf": ("sbuf", [128, 128], "float32"), "idb": ("sbuf", [128, 128], "bfloat16"), "zz": ("sbuf", [128, 128], "float32"),
+    "b4": ("sbuf", [128, 32], "float32"), "bqb": ("sbuf", [128, 128], "bfloat16"),
+    "wt": ("sbuf", [128, 512], "float32"), "w4": ("sbuf", [128, 8], "float32"),
+    "wm": ("sbuf", [128, 56], "float32"), "wmb": ("sbuf", [128, 56], "bfloat16"),
+    "cf": ("sbuf", [128, 256], "float32"), "lby": ("sbuf", [128, 256], "float32"), "eqt": ("sbuf", [128, 1024], "float32"),
+    "ypt": ("sbuf", [128, 1024], "float32"), "ycs": ("sbuf", [128, 256], "float32"),
+    "acc": ("sbuf", [128, 512], "float32"), "fin": ("sbuf", [128, 256], "float32"), "yes": ("sbuf", [128, 256], "float32"),
+}
+for _k in range(8): SCRATCH["dg%d" % _k] = ("dram", [8, 4096], "bfloat16")
+for _k in range(4):
+    SCRATCH["ra%d" % _k] = ("sbuf", [128, 256], "bfloat16")
+    SCRATCH["rl%d" % _k] = ("sbuf", [128, 64], "uint16")
+    SCRATCH["rm%d" % _k] = ("sbuf", [128, 1024], "bfloat16")
+    SCRATCH["rE%d" % _k] = ("sbuf", [128, 256], "float32")
+    SCRATCH["ms%d" % _k] = ("sbuf", [128, 256], "float32")
+for _k in ("pA", "pM", "pN", "pL"):
+    for _h in "01": SCRATCH[_k + _h] = ("psum", [128, 512], "float32")
+
+_DS = ["dk", "du", "da", "dl", "da0", "dyk", "dyu", "dxc", "dss", "dmm", "ddg", "dcw", "dm1", "dm2", "dy0", "dyc", "dye0", "dye1"]
+SEMAPHORES = ["sv", "ss", "sp", "sg", "rl"] + _DS + ["aA%d" % k for k in range(4)] + ["aL%d" % k for k in range(4)] \
+    + ["aM%d" % k for k in range(4)] + ["aE1", "aE2", "aE3a", "aE3b"]
+
+
+def rank_program(g, core, T, topo):
+    me = T.rank_of(core)
+    if me is None:
+        return
+    cores = list(T.cores); N = len(cores)
+    peers = [c for c in cores if c != core]
+    Q = {"V": g.vector, "S": g.scalar, "P": g.tensor, "G": g, "Y": g.sync}
+    SEM = {"V": "sv", "S": "ss", "P": "sp", "G": "sg"}
+    cnt = {}; known = {e: {} for e in Q}; snap = {}; lastw = {}; reads = {}; bank = {}
+
+    def need(e, evs):
+        best = {}
+        for s, v in evs: best[s] = max(best.get(s, 0), v)
+        for s in sorted(best, key=lambda k: (k in ("sv", "ss", "sp", "sg"), k)):
+            v = best[s]; kn = known[e]
+            if kn.get(s, 0) >= v: continue
+            Q[e].wait_ge(T.sem[s], v)
+            for s2, v2 in snap.get((s, v), {}).items():
+                if kn.get(s2, 0) < v2: kn[s2] = v2
+            kn[s] = v
+
+    def deps(e, r, w, b, asyn=False):
+        evs = []
+        for t in r:
+            if t in lastw: evs.append(lastw[t])
+        for t in w:
+            if t in lastw: evs.append(lastw[t])
+            for e2, ev in reads.get(t, {}).items():
+                if e2 != e or asyn: evs.append(ev)
+        for t in b:
+            for e2, ev in bank.get(t, {}).items():
+                if e2 != e: evs.append(ev)
+        need(e, evs)
+
+    def done(e, key, ev, r, w, b):
+        snap[ev] = dict(known[e])
+        for t in r: reads.setdefault(t, {})[key] = ev
+        for t in w:
+            lastw[t] = ev; reads[t] = {}
+        for t in b: bank.setdefault(t, {})[key] = ev
+
+    def op(e, calls, r=(), w=(), b=()):
+        deps(e, r, w, b)
+        s = SEM[e]
+        for c in (calls if isinstance(calls, list) else [calls]):
+            c().then_inc(T.sem[s], 1); cnt[s] = cnt.get(s, 0) + 1
+        done(e, e, (s, cnt[s]), r, w, b)
+
+    def dmag(e, pairs, sem, r=(), w=()):
+        deps(e, r, w, (), True)
+        for o, i in pairs:
+            Q[e].dma_start(out=o, in_=i).then_inc(T.sem[sem], 16)
+        cnt[sem] = 16 * len(pairs)
+        done(e, "dma" + sem, (sem, cnt[sem]), r, w, ())
+
+    def send(src, name, dsts, rsem, r):
+        deps("G", r, (), ())
+        eng = topo.engines(core, dsts[0][0])
+        ids = []
+        for c, _x in dsts:
+            a = topo.addr(c); ids.append(DstId(rid=a[0], pnc=a[1]))
+        g.remote_dma_fused([RemoteDMATransfer(dst_ids=ids, dma_engine_mask=topo.mask(core, dsts[0][0]), remote_sem=T.sem[rsem],
+                                              srcs=[src], dsts=[d for _c, d in dsts])], local_sem=T.sem.rl)
+        cnt["rl"] = cnt.get("rl", 0) + len(eng)
+
+    def v(n, h, st=0, step=1):
+        o, w = _W[n]; return T["w%d" % h][:, o + st:o + w:step]
+
+    def vb(n, h, a, b):
+        o, w = _W[n]; return T["w%d" % h][:, o + a:o + b]
+
+    def tk(s, h): return [x + str(h) for x in s.split()]
+
+    def tt(o, a, b, f, h, w, r, bk=""):
+        op("V", lambda: g.vector.tensor_tensor(out=o, in0=a, in1=b, op=f), tk(r, h), tk(w, h), tk(bk, h))
+
+    def ts(o, a, s1, s2, f0, f1, r, w, b=()):
+        if f1 is None: op("V", lambda: g.vector.tensor_scalar(out=o, in0=a, scalar1=s1, scalar2=None, op0=f0), r, w, b)
+        else: op("V", lambda: g.vector.tensor_scalar(out=o, in0=a, scalar1=s1, scalar2=s2, op0=f0, op1=f1), r, w, b)
+
+    def cp(o, a, r, w, b=()):
+        op("V", lambda: g.vector.tensor_copy(out=o, in_=a), r, w, b)
+
+    def act(o, a, f, r, w, b=(), bias=0.0, scale=1.0):
+        op("S", lambda: g.scalar.activation(out=o, in_=a, func=f, bias=bias, scale=scale), r, w, b)
+
+    def ms(o, c, w):
+        op("V", lambda: g.vector.memset(o, c), (), w)
+
+    def mm(o, l, r_, st, sp):
+        return lambda: g.tensor.matmul(out=o, lhsT=l, rhs=r_, start=st, stop=sp)
+
+    RA = "ra%d" % me; RL = "rl%d" % me; RM = "rm%d" % me
+    ne = len(topo.engines(core, peers[0]))
+    for k in range(N):
+        if k != me:
+            lastw["ra%d" % k] = ("aA%d" % k, ne); lastw["rl%d" % k] = ("aL%d" % k, ne); lastw["rm%d" % k] = ("aM%d" % k, ne)
+    lastw["rE1"] = ("aE1", ne); lastw["rE2"] = ("aE2", ne); lastw["rE3h0"] = ("aE3a", ne); lastw["rE3h1"] = ("aE3b", ne)
+
+    dmag("Y", [(T.kl[:, :], T.kid[:, :])], "dk", (), ["kl"])
+    dmag("S", [(T[RA][:, :], T.a[:, :])], "da", (), [RA])
+    dmag("S", [(T.lki[:, :], T.lk[:, :])], "dl", (), ["lki"])
+    dmag("S", [(T.a0b[:, :], T.a0[:, :])], "da0", (), ["a0b"])
+    dmag("Y", [(T.ul[:, :], T.up[:, :])], "du", (), ["ul"])
+    dmag("Y", [(T.ytk[:, 128 * k:128 * k + 128], T.kid[k::2, :]) for k in (0, 1)], "dyk", (), ["ytk"])
+    dmag("Y", [(T.ytu[:, 128 * k:128 * k + 128], T.up[k::2, :]) for k in (0, 1)], "dyu", (), ["ytu"])
+    dmag("S", [(T.xc[:, t * 64:t * 64 + 64], T.cut0[t::4, :]) for t in range(4)], "dxc", (), ["xc"])
+    dmag("S", [(T.swin[:, :], T.s[:, :])], "dss", (), ["swin"])
+
+    ms(T.b4[:, :], 1.0, ["b4"]); ms(T.zz[:, :], 0.0, ["zz"]); ms(T.wm[:, :], 0.0, ["wm"]); ms(T.w4[:, :], 4.0, ["w4"])
+    ms(T.cwin[:, 4080:4096], 0.0, ["cwin"]); ms(T.wt[:, :], 0.0, ["wt"])
+
+    def sel(buf, tok, pat, base, cm, cmp_, fill, src=None, stok=None):
+        op("G", lambda: g.affine_select(out=buf, in_=buf if src is None else src, pattern=pat, compare_op=cmp_, fill=fill, base=base,
+                                        channel_multiplier=cm), [tok] if stok is None else [stok], [tok])
+    op("G", lambda: g.iota(T.pn[:, :], [[0, 256]], 0, 1), (), ["pn"])
+    op("G", lambda: g.iota(T.di[:, 1024:1280], [[1, 256]], 0, 0), (), ["di4"])
+    sel(T.b4[:, :], "b4", [[-4, 32]], 0, 1, OP.is_ge, 0.0)
+    sel(T.b4[:, :], "b4", [[4, 32]], 3, -1, OP.is_ge, 0.0)
+
+    cp(T[RL][:, :], T.lki[:, :], ["lki"], [RL])
+    send(T[RA][:, :], RA, [(c, T[RA][:, :]) for c in peers], "aA%d" % me, [RA])
+    send(T[RL][:, :], RL, [(c, T[RL][:, :]) for c in peers], "aL%d" % me, [RL])
+
+    sel(T.idf[:, :], "idf", [[-1, 128]], 0, 1, OP.not_equal, 1.0, T.zz[:, :], "zz")
+    sel(T.w4[:, :], "w4", [[-16, 8]], 0, 1, OP.is_ge, 0.0)
+    sel(T.w4[:, :], "w4", [[16, 8]], 15, -1, OP.is_ge, 0.0)
+    TERMS = [(0, 0, 2.0), (0, 1, 512.0), (1, 9, 1.0), (1, 10, 256.0), (2, 11, 1.0), (2, 12, 256.0), (3, 13, 16.0), (3, 14, 4096.0),
+             (4, 3, 2.0), (4, 4, 512.0), (4, 5, BIG), (5, 6, 2.0), (5, 7, 512.0), (5, 8, BIG), (6, 13, 16.0), (6, 14, 4096.0), (6, 2, BIG)]
+    for o_ in range(7):
+        for oo, i_, w_ in TERMS:
+            if oo == o_: sel(T.wm[:, oo * 8:oo * 8 + 8], "wm", [[-16, 8]], -i_, 1, OP.not_equal, w_)
+
+    def spread_g(b, ax, rows):
+        for r in rows:
+            op("G", lambda: g.affine_select(out=T[ax][:, r::16], in_=T["ra%d" % b][:, :], pattern=[[0, 256]], compare_op=OP.is_gt, fill=0.0,
+                                            base=1, channel_multiplier=0), ["ra%d" % b], [ax + "r%d" % r])
+    spread_g(me, "ax0", range(8, 16))
+    for r in range(8):
+        act(T.ax0[:, r::16], T[RA][:, :], AF.Copy, [RA], ["ax0r%d" % r])
+
+    ts(T.di[:, 0:256], T.kl[:, :], 1, 255, OP.arith_shift_right, OP.bitwise_and, ["kl"], ["di0"])
+    ts(T.di[:, 256:512], T.kl[:, :], 9, None, OP.arith_shift_right, None, ["kl"], ["di1"])
+    ts(T.db[:, 1536:1792], T.kl[:, :], 0, None, OP.is_lt, None, ["kl"], ["db6"])
+    ts(T.db[:, 1792:2048], T.kl[:, :], 0, None, OP.is_ge, None, ["kl"], ["db7"])
+    ts(T.u1i[:, :], T.ul[:, :], 1, None, OP.add, None, ["ul"], ["u1i"])
+    ts(T.di[:, 1280:1536], T.pn[:, :], 15, None, OP.bitwise_and, None, ["pn"], ["di5"])
+    ts(T.di[:, 512:768], T.u1i[:, :], 255, None, OP.bitwise_and, None, ["u1i"], ["di2"])
+    ts(T.di[:, 768:1024], T.u1i[:, :], 8, None, OP.arith_shift_right, None, ["u1i"], ["di3"])
+    cp(T.db[:, 0:1536], T.di[:, :], ["di%d" % k for k in range(6)], ["db0"])
+    dmag("Y", [(T["dg%d" % k][:, :], T.db[:, 256 * k:256 * k + 256]) for k in range(8)], "ddg", ["db0", "db6", "db7"], ["dg"])
+    C = T.cwin
+    prs = [(C[i::16, :], T["dg%d" % k][:, :]) for i, k in ((0, 0), (1, 1), (2, 6), (3, 0), (4, 1), (5, 7), (9, 2), (10, 3), (11, 2), (12, 3),
+                                                           (13, 4), (14, 5), (15, 4))]
+    prs += [(C[i::16, 0:4095], T["dg%d" % k][:, 1:4096]) for i, k in ((6, 0), (7, 1), (8, 7))]
+    dmag("Y", prs, "dcw", ["dg"], ["cwin"])
+    dmag("Y", [(T.mwin[:, :], T.m[:, :])], "dmm", (), ["mwin"])
+
+    def dist(aw, lkb, mout):
+        for k in range(4):
+            op("V", lambda: g.vector.tensor_tensor(out=T.df[:, k * 256:k * 256 + 256], in0=T[aw][:, 0:256].indirect(T[lkb][:, 16 * k:16 * k + 16]),
+                                                   in1=T[RA][:, :], op=OP.subtract), [aw, lkb, RA], ["df%d" % k])
+        for k in range(2):
+            act(T.dabs[:, k * 512:k * 512 + 512], T.df[:, k * 512:k * 512 + 512], AF.Abs, ["df%d" % (2 * k), "df%d" % (2 * k + 1)], ["dabs%d" % k])
+            op("P", mm(T["pL%d" % k][:, :], T.bqb[:, :], T.dabs[:, k * 512:k * 512 + 512], True, True), ["bqb", "dabs%d" % k], ["dp%d" % k], ["pL%d" % k])
+        for k in range(4):
+            act(T.kd[:, k * 256:k * 256 + 256], T["pL%d" % (k // 2)][:, (k % 2) * 256:(k % 2) * 256 + 256], AF.Identity, ["dp%d" % (k // 2)],
+                ["kd%d" % k], ["pL%d" % (k // 2)], float(k), 4.0)
+
+    def dist2(mout):
+        op("V", lambda: g.vector.tensor_tensor(out=T.kmn[:, 0:512], in0=T.kd[:, 0:512], in1=T.kd[:, 512:1024], op=OP.min),
+           ["kd0", "kd1", "kd2", "kd3"], ["kmn"])
+        op("V", lambda: g.vector.tensor_tensor(out=T.kmn[:, 512:768], in0=T.kmn[:, 0:256], in1=T.kmn[:, 256:512], op=OP.min), ["kmn"], ["kmm"])
+        for k in range(4):
+            op("V", lambda: g.vector.tensor_tensor(out=T[mout][:, k * 256:k * 256 + 256], in0=T.kd[:, k * 256:k * 256 + 256], in1=T.kmn[:, 512:768],
+                                                   op=OP.is_equal), ["kd%d" % k, "kmm"], [mout])
+
+    for k in range(4): cp(T.bqb[:, k::4], T.b4[:, :], ["b4"], ["bqb"])
+    dist("a0b", RL, "mk0")
+
+    for yt, x_, z_, ls_ in (("ytk", "xk", "zk", "lstk"), ("ytu", "xu", "zu", "lstu")):
+        for b in range(8):
+            for k in (0, 1):
+                cp(T[x_][:, 32 * b + 16 * k:32 * b + 16 * k + 16], T[yt][:, 128 * k + 16 * b:128 * k + 16 * b + 16], [yt], [x_])
+        op("V", lambda: g.vector.transpose(out=T[z_][:, :], in_=T[x_][:, :]), [x_], [z_])
+        for b in range(8):
+            cp(T[ls_][:, b::8], T[z_][:, 32 * b:32 * b + 32], [z_], [ls_])
+    dist2("mk0")
+    op("S", lambda: g.scalar.activation(out=T.meta[:, :], in_=T.cwin[:, :].indirect(T.lstk[:, :]), func=AF.Copy), ["cwin", "lstk"], ["meta"])
+    op("S", lambda: g.scalar.activation(out=T.bt[:, :], in_=T.cwin[:, :].indirect(T.lstu[:, :]), func=AF.Copy), ["cwin", "lstu"], ["bt"])
+    dmag("Y", [(T.meta[i::16, :], T["dg%d" % k][:, :]) for i, k in ((0, 0), (1, 1), (2, 6), (9, 2), (10, 3), (13, 4), (14, 5))], "dm1", ["dg"], ["meta"])
+
+    ts(T.xh[:, :], T.xc[:, :], 1, None, OP.arith_shift_right, None, ["xc"], ["xh"])
+    for t in range(4):
+        ts(T.xy[:, t * 64:t * 64 + 64], T.xc[:, t * 64:t * 64 + 64], 1.0, (3 - t) / 16.0, OP.mult, OP.add, ["xc"], ["xy%d" % t])
+
+    def xw(k): return T.xw[:, k * 64:k * 64 + 64]
+
+    def xs(b, t): return b[:, t * 64:t * 64 + 64]
+
+    def x2(o, a, b, f, r, w): op("V", lambda: g.vector.tensor_tensor(out=o, in0=a, in1=b, op=f), r, w)
+    for k, (i, j) in enumerate(((0, 2), (1, 3), (0, 3), (1, 2))):
+        x2(xw(k), xs(T.xh, i), xs(T.xh, j), OP.is_equal, ["xh"], ["xw%d" % k])
+    x2(xw(6), xs(T.xy, 2), xs(T.xy, 1), OP.subtract, ["xy1", "xy2"], ["xw6"])
+    x2(xw(7), xs(T.xy, 3), xs(T.xy, 1), OP.subtract, ["xy1", "xy3"], ["xw7"])
+    x2(xw(4), xw(0), xw(1), OP.max, ["xw0", "xw1"], ["xw4"])
+    x2(xw(5), xw(2), xw(3), OP.max, ["xw2", "xw3"], ["xw5"])
+    cp(xs(T.xo, 0), xs(T.xy, 0), ["xy0"], ["xo"])
+    x2(xw(8), xw(4), xw(6), OP.mult, ["xw4", "xw6"], ["xw8"])
+    x2(xw(9), xw(5), xw(7), OP.mult, ["xw5", "xw7"], ["xw9"])
+    x2(xw(10), xs(T.xy, 1), xw(8), OP.add, ["xy1", "xw8"], ["xw10"])
+    x2(xs(T.xo, 2), xs(T.xy, 2), xw(8), OP.subtract, ["xy2", "xw8"], ["xo"])
+    x2(xs(T.xo, 3), xs(T.xy, 3), xw(9), OP.subtract, ["xy3", "xw9"], ["xo"])
+    x2(xs(T.xo, 1), xw(10), xw(9), OP.add, ["xw10", "xw9"], ["xo"])
+    dmag("Y", [(T.y[t::4, :], T.xo[:, t * 64:t * 64 + 64]) for t in range(4)], "dy0", ["xo"], ["y0", "y1"])
+    dmag("Y", [(T.meta[i::16, :], T.bt[i::16, :]) for i in (11, 12)], "dm2", ["bt"], ["meta"])
+    cp(T.idb[:, :], T.idf[:, :], ["idf"], ["idb"])
+    cp(T.wmb[:, :], T.wm[:, :], ["wm"], ["wmb"])
+    ts(T.pc3[:, 0:1], T.pn[:, 0:1], 3, None, OP.bitwise_and, None, ["pn"], ["pc3"])
+    ts(T.adc[:, :], T.pc3[:, 0:1], -2, -1, OP.add, OP.max, ["pc3"], ["adc"])
+
+    AXR = lambda h: ["ax%dr%d" % (h % 2, r) for r in range(16)]
+
+    def pmx(o_, h, st=0, step=1): return T["pM%d" % h][:, o_ * 128 + st:o_ * 128 + 128:step]
+
+    def pnx(o_, h, st=0, step=1): return T["pN%d" % h][:, o_ * 128 + st:o_ * 128 + 128:step]
+
+    def gather_mul(h, lst, tok, vis, w):
+        op("V", lambda: g.vector.tensor_tensor(out=T["p%d" % h][:, :], in0=T.swin[:, :].indirect(T[lst][:, h * 128:h * 128 + 128]),
+                                               in1=T["ax%d" % (vis % 2)][:, h * 2048:h * 2048 + 2048], op=OP.mult),
+           ["swin", tok + str(h)] + AXR(vis), ["p%d" % h])
+
+    def dots(h, col, w):
+        op("P", [mm(T["pA%d" % h][:, col + r:col + 128:16], T["p%d" % h][:, r::16], T.w4[:, :], True, True) for r in range(16)],
+           ["p%d" % h, "w4"], [w + str(h)], ["pA%d" % h])
+
+    def meta_mm(h):
+        op("P", mm(pnx(3, h), T.yn[:, h * 128:h * 128 + 128], T.idf[:, :], True, True), ["yn%d" % h, "idf"], ["yd%d" % h], ["pN%d" % h])
+        cl = []
+        for r in range(16):
+            cl.append(mm(T["pM%d" % h][:, r::16], T["gm%d" % h][:, r::16], T.wmb[:, 0:32], True, True))
+            cl.append(mm(T["pN%d" % h][:, r:384:16], T["gm%d" % h][:, r::16], T.wmb[:, 32:56], True, True))
+        op("P", cl, ["gm%d" % h, "wmb"], ["m%d" % h, "n%d" % h], ["pM%d" % h, "pN%d" % h])
+
+    def s_copies(h):
+        act(v("ups", h), pmx(1, h), AF.Copy, tk("m", h), tk("ups", h), ["pM%d" % h])
+        act(v("yd16", h), pnx(3, h), AF.Identity, tk("yd", h), tk("yd16", h), ["pN%d" % h], 0.0, 16.0)
+
+    def off_a(h):
+        tt(v("lab", h), v("yd16", h), pmx(3, h), OP.subtract, h, "lab", "yd16 m", "pM")
+        tt(v("eq", h), v("ups", h, 0, 2), pmx(1, h, 1, 2), OP.is_equal, h, "eq", "ups m", "pM")
+        tt(v("lbk", h), v("yd16", h), pnx(2, h), OP.subtract, h, "lbk", "yd16 n", "pN")
+        tt(v("peq", h), v("eq", h), pmx(1, h, 0, 2), OP.mult, h, "peq", "eq m", "pM")
+        tt(v("xa", h), v("lab", h, 0, 2), v("lab", h, 1, 2), OP.max, h, "xa", "lab")
+        tt(v("na", h), v("lab", h, 0, 2), v("lab", h, 1, 2), OP.min, h, "na", "lab")
+
+    def dec1(h):
+        tt(v("kes", h), v("lbk", h), T["pA%d" % h][:, 0:128], OP.add, h, "kes", "lbk ke", "pA")
+        e, o = v("kes", h, 0, 2), v("kes", h, 1, 2)
+        tt(v("mab", h), e, o, OP.max, h, "mab", "kes")
+        tt(v("w1", h), o, e, OP.is_gt, h, "w1", "kes")
+        tt(v("w0", h), e, o, OP.is_gt, h, "w0", "kes")
+        A, B = v("mab", h, 0, 2), v("mab", h, 1, 2)
+        tt(v("sab", h, 0, 2), A, B, OP.is_gt, h, "sA", "mab")
+        tt(v("sab", h, 1, 2), B, A, OP.is_gt, h, "sB", "mab")
+        tt(v("o", h, 0, 2), v("sab", h), v("w0", h), OP.mult, h, "oe", "sA sB w0")
+        tt(v("o", h, 1, 2), v("sab", h), v("w1", h), OP.mult, h, "oo", "sA sB w1")
+        sA, sB = v("sab", h, 0, 2), v("sab", h, 1, 2)
+        tt(v("pa", h), sB, v("peq", h, 0, 2), OP.mult, h, "pa", "sB peq")
+        tt(v("pb", h), sA, v("peq", h, 1, 2), OP.mult, h, "pb", "sA peq")
+        tt(v("prk", h), v("o", h), pmx(0, h), OP.mult, h, "prk", "oe oo m", "pM")
+        tt(v("ga", h), sB, pmx(2, h, 0, 4), OP.mult, h, "ga", "sB m", "pM")
+        tt(v("gb", h), sA, pmx(2, h, 2, 4), OP.mult, h, "gb", "sA m", "pM")
+        tt(v("t1", h), v("prk", h, 0, 2), v("prk", h, 1, 2), OP.add, h, "t1", "prk")
+        tt(v("lt", h, 0, 4), v("pa", h), v("pb", h), OP.add, h, "lta", "pa pb")
+        tt(v("lt", h, 1, 4), v("ga", h), v("gb", h), OP.add, h, "ltb", "ga gb")
+        tt(v("lt", h, 2, 4), v("t1", h, 0, 2), v("t1", h, 1, 2), OP.add, h, "ltc", "t1")
+        tt(v("lt", h, 3, 4), v("t1", h, 0, 2), v("t1", h, 1, 2), OP.add, h, "ltd", "t1")
+        op("P", mm(T["pL%d" % h][:, 0:128], v("lt", h), T.idf[:, :], True, True), tk("lta ltb ltc ltd", h) + ["idf"], tk("plt", h), ["pL%d" % h])
+
+    def conv(h):
+        ts(T.l2[:, h * 128:h * 128 + 128], T["pL%d" % h][:, 0:128], T.adc[:, 0:1], None, OP.add, None, tk("plt", h) + ["adc"], tk("l2", h), ["pL%d" % h])
+
+    def off_b1(h):
+        sA, sB = v("sab", h, 0, 2), v("sab", h, 1, 2)
+        tt(v("nab", h), v("kes", h, 0, 2), v("kes", h, 1, 2), OP.min, h, "nab", "kes")
+        tt(vb("mk", h, 0, 32), v("mab", h, 0, 2), v("mab", h, 1, 2), OP.max, h, "mka", "mab")
+        tt(v("ja", h), sB, v("xa", h, 0, 2), OP.mult, h, "ja", "sB xa")
+        tt(v("jb", h), sA, v("xa", h, 1, 2), OP.mult, h, "jb", "sA xa")
+        tt(v("pa2", h), sB, v("na", h, 0, 2), OP.mult, h, "pa2", "sB na")
+        tt(v("pb2", h), sA, v("na", h, 1, 2), OP.mult, h, "pb2", "sA na")
+        tt(v("ka", h), sA, v("nab", h, 0, 2), OP.mult, h, "ka", "sA nab")
+        tt(v("kb", h), sB, v("nab", h, 1, 2), OP.mult, h, "kb", "sB nab")
+        tt(v("lj", h), v("ja", h), v("jb", h), OP.add, h, "lj", "ja jb")
+        tt(v("ljp", h), v("pa2", h), v("pb2", h), OP.add, h, "ljp", "pa2 pb2")
+        tt(vb("mk", h, 32, 64), v("ka", h), v("kb", h), OP.add, h, "mkb", "ka kb")
+        tt(v("prl", h), v("o", h), pnx(0, h), OP.mult, h, "prl", "oe oo n", "pN")
+        tt(v("prr", h), v("o", h), pnx(1, h), OP.mult, h, "prr", "oe oo n", "pN")
+        wi = T["wi%d" % h]
+        cp(wi[:, 0:64], v("mk", h), tk("mka mkb", h), tk("mki", h))
+        tt(v("u1", h), v("o", h, 1, 2), pmx(1, h, 0, 2), OP.mult, h, "u1", "oo m", "pM")
+        tt(v("u2", h), v("o", h, 0, 2), pmx(1, h, 1, 2), OP.mult, h, "u2", "oe m", "pM")
+        ts(wi[:, 64:128], wi[:, 0:64], 3, None, OP.bitwise_and, None, tk("mki", h), tk("mkj", h))
+        tt(v("y1", h), v("o", h, 1, 2), pnx(3, h, 0, 2), OP.mult, h, "y1t", "oo yd", "pN")
+        tt(v("y2", h), v("o", h, 0, 2), pnx(3, h, 1, 2), OP.mult, h, "y2t", "oe yd", "pN")
+        cp(v("lbf", h), wi[:, 64:128], tk("mkj", h), tk("lbf", h))
+        tt(v("tl", h), v("prl", h, 0, 2), v("prl", h, 1, 2), OP.add, h, "tl", "prl")
+        tt(v("tr", h), v("prr", h, 0, 2), v("prr", h, 1, 2), OP.add, h, "tr", "prr")
+        tt(v("u3", h), v("u1", h), v("u2", h), OP.add, h, "u3", "u1 u2")
+        tt(v("y3", h), v("y1", h), v("y2", h), OP.add, h, "y3", "y1t y2t")
+        tt(vb("z", h, 0, 32), v("tl", h, 0, 2), v("tl", h, 1, 2), OP.add, h, "za", "tl")
+        tt(vb("z", h, 32, 64), v("tr", h, 0, 2), v("tr", h, 1, 2), OP.add, h, "zb", "tr")
+        tt(v("mx", h), v("lj", h), vb("lbf", h, 32, 64), OP.max, h, "mx", "lj lbf")
+        tt(v("mn", h), v("lj", h), vb("lbf", h, 32, 64), OP.min, h, "mn", "lj lbf")
+        tt(v("upu", h), v("u3", h, 0, 2), v("u3", h, 1, 2), OP.add, h, "upu", "u3")
+        tt(v("s1", h, 1, 4), v("y3", h, 0, 2), v("y3", h, 1, 2), OP.add, h, "s1b", "y3")
+        ts(v("hasp", h), v("lt", h, 0, 4), 0.0, None, OP.is_gt, None, tk("lta", h), tk("hasp", h))
+        tt(v("sib", h), v("upu", h), v("lt", h, 1, 4), OP.is_equal, h, "sib", "upu ltb")
+        c = 1.0 / 16.0
+        act(v("ljm", h), v("lj", h), AF.Identity, tk("lj", h), tk("ljm", h), (), -1.0, c)
+        act(v("ljq", h), v("ljp", h), AF.Identity, tk("ljp", h), tk("ljq", h), (), 1.0, c)
+        act(v("lp", h), v("ljp", h), AF.Identity, tk("ljp", h), tk("lp", h), (), 0.0, c)
+        act(v("ls", h), vb("lbf", h, 0, 32), AF.Identity, tk("lbf", h), tk("ls", h), (), 0.0, c)
+        act(v("zc", h), v("z", h), AF.Relu, tk("za zb", h), tk("zc", h), (), -BIG, 1.0)
+        act(v("mxm", h), v("mx", h), AF.Identity, tk("mx", h), tk("mxm", h), (), -1.0, c)
+        act(v("mn1", h), v("mn", h), AF.Identity, tk("mn", h), tk("mn1", h), (), 1.0, c)
+
+    def off_b2(h):
+        za, zb = vb("zc", h, 0, 32), vb("zc", h, 32, 64)
+        tt(v("s1", h, 0, 4), v("lt", h, 0, 4), v("ljm", h), OP.add, h, "s1a", "lta ljm")
+        tt(v("s1", h, 2, 4), v("lt", h, 2, 4), v("ls", h), OP.add, h, "s1c", "ltc ls")
+        tt(v("s1", h, 3, 4), v("lt", h, 3, 4), v("ljq", h), OP.add, h, "s1d", "ltd ljq")
+        tt(v("aa", h), za, v("ls", h), OP.add, h, "aa", "zc ls")
+        tt(v("bb", h), zb, v("lp", h), OP.add, h, "bb", "zc lp")
+        tt(v("dz", h), za, zb, OP.subtract, h, "dz", "zc")
+        tt(v("s2", h, 0, 4), v("lt", h, 1, 4), v("mxm", h), OP.add, h, "s2a", "ltb mxm")
+        tt(v("zr1", h), zb, v("mn1", h), OP.add, h, "zr1", "zc mn1")
+        tt(v("dab", h), v("aa", h), v("bb", h), OP.subtract, h, "dab", "aa bb")
+        tt(v("dr", h), v("s1", h, 3, 4), v("s1", h, 2, 4), OP.subtract, h, "dr", "s1c s1d")
+
+    def dec2(h):
+        def F(k): return T["pA%d" % h][:, 128 + k:256:4]
+        ls, M, KU = vb("lbf", h, 0, 32), vb("mk", h, 0, 32), vb("mk", h, 32, 64)
+        pa = ["pA%d" % h]
+        tt(v("fk2", h), ls, F(2), OP.add, h, "fk2", "lbf f", "pA")
+        tt(v("fk3", h), v("ljp", h), F(3), OP.add, h, "fk3", "ljp f", "pA")
+        tt(v("fk0", h), v("lj", h), F(0), OP.add, h, "fk0", "lj f", "pA")
+        ts(v("d0", h), F(0), 3.0, None, OP.add, None, tk("f", h), tk("d0", h), pa)
+        ts(v("d1", h), F(1), 3.0, None, OP.add, None, tk("f", h), tk("d1", h), pa)
+        tt(v("kl", h), v("fk2", h), vb("z", h, 0, 32), OP.min, h, "klt", "fk2 za")
+        tt(v("kr", h), v("fk3", h), vb("z", h, 32, 64), OP.min, h, "krt", "fk3 zb")
+        tt(v("mxu", h), v("fk0", h), KU, OP.max, h, "mxu", "fk0 mkb")
+        tt(v("g1a", h), M, v("d0", h), OP.is_gt, h, "g1a", "mka d0")
+        tt(v("k2", h), v("kl", h), v("kr", h), OP.max, h, "k2", "klt krt")
+        tt(v("sl", h), v("kl", h), v("kr", h), OP.is_gt, h, "sl", "klt krt")
+        tt(v("g1", h), v("g1a", h), v("hasp", h), OP.mult, h, "g1", "g1a hasp")
+        tt(v("b1", h), v("k2", h), v("mxu", h), OP.is_gt, h, "b1", "k2 mxu")
+        tt(v("b2", h), v("k2", h), v("d1", h), OP.is_gt, h, "b2", "k2 d1")
+        tt(v("e1", h), v("sl", h), v("dr", h), OP.mult, h, "e1", "sl dr")
+        tt(v("e2", h), v("sl", h), v("dab", h), OP.mult, h, "e2", "sl dab")
+        tt(v("gs", h), v("g1", h), v("sib", h), OP.mult, h, "gs", "g1 sib")
+        tt(v("bbb", h), v("b1", h), v("b2", h), OP.mult, h, "bbb", "b1 b2")
+        ts(v("m0", h), v("g1", h), -1.0, 1.0, OP.mult, OP.add, tk("g1", h), tk("m0", h))
+        tt(v("e3", h), v("sl", h), v("dz", h), OP.mult, h, "e3", "sl dz")
+        tt(v("go2", h), v("bbb", h), v("gs", h), OP.mult, h, "go2", "bbb gs")
+        tt(v("s2", h, 1, 4), v("s1", h, 2, 4), v("e1", h), OP.add, h, "s2b", "s1c e1")
+        tt(v("s2", h, 2, 4), v("bb", h), v("e2", h), OP.add, h, "s2c", "bb e2")
+        tt(v("s2", h, 3, 4), v("zr1", h), v("e3", h), OP.add, h, "s2d", "zr1 e3")
+        for k in range(4): tt(v("n0", h, k, 4), v("m0", h), pnx(3, h, k, 4), OP.mult, h, "n0" + "abcd"[k], "m0 yd", "pN")
+        tt(v("m1", h), v("g1", h), v("go2", h), OP.subtract, h, "m1", "g1 go2")
+        for k in range(4): tt(v("n2", h, k, 4), v("go2", h), v("s2", h, k, 4), OP.mult, h, "n2" + "abcd"[k], "go2 s2" + "abcd"[k])
+        for k in range(4): tt(v("n1", h, k, 4), v("m1", h), v("s1", h, k, 4), OP.mult, h, "n1" + "abcd"[k], "m1 s1" + "abcd"[k])
+        for j, n in enumerate(("n0", "n2", "n1")):
+            op("P", mm(T["pL%d" % h][:, 128:256], v(n, h), T.idf[:, :], j == 0, j == 2), tk(" ".join(n + x for x in "abcd"), h) + ["idf"],
+               tk("pnn", h), ["pL%d" % h])
+
+    def keep(h):
+        cp(T.ml[:, h * 128:h * 128 + 128], T["pL%d" % h][:, 128:256], tk("pnn", h), tk("ml", h), ["pL%d" % h])
+        cp(T.y[:, h * 128:h * 128 + 128], T["pL%d" % h][:, 128:256], tk("pnn", h), tk("y", h), ["pL%d" % h])
+
+    def m_gather(h, e):
+        if e == "S":
+            op("S", lambda: g.scalar.activation(out=T["mg%d" % h][:, :], in_=T.mwin[:, :].indirect(T.ml[:, h * 128:h * 128 + 128]), func=AF.Copy),
+               ["mwin"] + tk("ml", h), tk("mg", h))
+        else:
+            op("V", lambda: g.vector.tensor_copy(out=T["mg%d" % h][:, :], in_=T.mwin[:, :].indirect(T.ml[:, h * 128:h * 128 + 128])),
+               ["mwin"] + tk("ml", h), tk("mg", h))
+
+    def m_sum(h):
+        op("P", [mm(T["pL%d" % h][:, 256:384], T.idb[:, :], T["mg%d" % h][:, r::16], r == 0, r == 15) for r in range(16)],
+           tk("mg", h) + ["idb"], tk("pms", h), ["pL%d" % h])
+
+    def m_out(h, vis):
+        act(T["ms%d" % vis][:, h * 128:h * 128 + 128], T["pL%d" % h][:, 256:384], AF.Copy, tk("pms", h), ["ms%dh%d" % (vis, h)], ["pL%d" % h])
+
+    def m_send(vis):
+        c = cores[(me - vis) % N]
+        if vis in (1, 2):
+            send(T["ms%d" % vis][:, :], "", [(c, T["rE%d" % vis][:, :])], "aE%d" % vis, ["ms%dh0" % vis, "ms%dh1" % vis])
+        if vis == 3:
+            for h in (0, 1):
+                send(T.ms3[:, h * 128:h * 128 + 128], "", [(c, T.rE3[:, h * 128:h * 128 + 128])], "aE3" + "ab"[h], ["ms3h%d" % h])
+
+    for vis in range(4):
+        b = (me - vis) % N
+        mk = "mk0" if vis == 0 else "rm%d" % b
+        lk = "rl%d" % b
+        op("V", lambda: g.vector.tensor_tensor(out=T.pr[:, :], in0=T.y[:, 0:256].indirect(T[lk][:, 0:64]), in1=T[mk][:, :], op=OP.mult),
+           ["y0", "y1", lk, mk], ["pr"])
+        op("V", lambda: g.vector.tensor_tensor(out=T.a2[:, :], in0=T.pr[:, 0:512], in1=T.pr[:, 512:1024], op=OP.add), ["pr"], ["a2"])
+        for h in (0, 1):
+            op("V", lambda: g.vector.tensor_tensor(out=T.yn[:, h * 128:h * 128 + 128], in0=T.a2[:, h * 128:h * 128 + 128],
+                                                   in1=T.a2[:, 256 + h * 128:384 + h * 128], op=OP.add), ["a2"], ["yn%d" % h])
+        for h in (0, 1):
+            cp(T.cl[:, h * 128:h * 128 + 128], T.yn[:, h * 128:h * 128 + 128], ["yn%d" % h], ["cl%d" % h])
+        for h in (0, 1):
+            op("S", lambda: g.scalar.activation(out=T["gm%d" % h][:, :], in_=T.meta[:, :].indirect(T.cl[:, h * 128:h * 128 + 128]), func=AF.Copy),
+               ["meta", "cl%d" % h], ["gm%d" % h])
+            gather_mul(h, "cl", "cl", vis, "")
+        if vis == 0: dist("ra%d" % ((me + 1) % N), RL, RM)
+        for h in (0, 1):
+            meta_mm(h)
+            dots(h, 0, "ke")
+        for h in (0, 1): s_copies(h)
+        if vis == 0:
+            dist2(RM)
+            spread_g((me - 1) % N, "ax1", range(16))
+            send(T[RM][:, :], RM, [(c, T[RM][:, :]) for c in peers], "aM%d" % me, [RM])
+        if vis > 0:
+            m_gather(0, "S"); m_gather(1, "S")
+        for h in (0, 1):
+            off_a(h); dec1(h)
+        for h in (0, 1):
+            conv(h); gather_mul(h, "l2", "l2", vis, "")
+        for h in (0, 1):
+            dots(h, 128, "f")
+        if vis in (0, 1): spread_g((me - vis - 2) % N, "ax%d" % (vis % 2), range(16))
+        if vis > 0:
+            m_sum(0); m_sum(1)
+        for h in (0, 1): off_b1(h)
+        if vis > 0:
+            m_out(0, vis - 1); m_out(1, vis - 1)
+            m_send(vis - 1)
+        for h in (0, 1):
+            off_b2(h); dec2(h)
+        for h in (0, 1): keep(h)
+
+    m_gather(0, "S"); m_gather(1, "V")
+    m_sum(0); m_out(0, 3)
+    for t in range(4): cp(T.wt[:, t * 128 + t:(t + 1) * 128:4], T.b4[:, :], ["b4", "wt"], ["wt%d" % t])
+    cp(T.cf[:, :], T.ml[:, :], ["ml0", "ml1"], ["cf"])
+    m_sum(1); m_out(1, 3); m_send(3)
+    op("V", lambda: g.vector.tensor_tensor(out=T.lby[:, :], in0=T.y[:, :], in1=T.cf[:, :], op=OP.subtract), ["y0", "y1", "cf"], ["lby"])
+    for t in range(4):
+        ts(T.eqt[:, t * 256:t * 256 + 256], T.lby[:, :], (3 - t) / 16.0, None, OP.is_equal, None, ["lby"], ["eqt%d" % t])
+    for t in range(4):
+        op("V", lambda: g.vector.tensor_tensor(out=T.ypt[:, t * 256:t * 256 + 256], in0=T.eqt[:, t * 256:t * 256 + 256], in1=T.cf[:, :], op=OP.mult),
+           ["eqt%d" % t, "cf"], ["ypt%d" % t])
+        op("P", mm(T.pN0[:, 0:256], T.wt[:, t * 128:t * 128 + 128], T.ypt[:, t * 256:t * 256 + 256], t == 0, t == 3), ["wt%d" % t, "ypt%d" % t],
+           ["pyc"], ["pN0"])
+    op("V", lambda: g.vector.tensor_tensor(out=T.acc[:, 0:256], in0=T.ms0[:, :], in1=T.rE1[:, :], op=OP.add), ["ms0h0", "ms0h1", "rE1"], ["acc0"])
+    cp(T.ycs[:, :], T.pN0[:, 0:256], ["pyc"], ["ycs"], ["pN0"])
+    dmag("Y", [(T.yc[:, :], T.ycs[:, :])], "dyc", ["ycs"], ["yc"])
+    op("V", lambda: g.vector.tensor_tensor(out=T.acc[:, 256:512], in0=T.acc[:, 0:256], in1=T.rE2[:, :], op=OP.add), ["acc0", "rE2"], ["acc1"])
+    for h in (0, 1):
+        c = slice(h * 128, h * 128 + 128)
+        op("V", lambda: g.vector.tensor_tensor(out=T.fin[:, c], in0=T.acc[:, 256 + h * 128:384 + h * 128], in1=T.rE3[:, c], op=OP.add),
+           ["acc1", "rE3h%d" % h], ["fin%d" % h])
+        op("V", lambda: g.vector.tensor_tensor(out=T.yes[:, c], in0=T.fin[:, c], in1=T[RA][:, c], op=OP.mult), ["fin%d" % h, RA], ["yes%d" % h])
+        dmag("Y", [(T.ye[:, c], T.yes[:, c])], "dye%d" % h, ["yes%d" % h], ["ye%d" % h])
+
+    need("G", [(s, cnt[s]) for s in cnt])

@@ -1,68 +1,86 @@
+import numpy as np
 from concourse.bass import DstId, RemoteDMATransfer
 from concourse.mybir import AluOpType, ActivationFunctionType
 
 OP = AluOpType
 AF = ActivationFunctionType
-BIG = 8388608.0
+RND1 = 12582912.0
+RNDH = 6291456.0
+PEN = 2097152.0
+TAG = [""]
 
-_W = {}
-_n = [0]
-for _k in "ups yd16 lab lbk kes o prk prl prr lt s1 s2 n0 n1 n2".split():
-    _W[_k] = (_n[0], 128); _n[0] += 128
-for _k in "eq peq xa na mab nab w1 w0 sab t1 tl tr u1 u2 u3 y1 y2 y3 mk lbf z zc".split():
-    _W[_k] = (_n[0], 64); _n[0] += 64
-for _k in ("pa pb ga gb ka kb ja jb pa2 pb2 lj ljp upu sib hasp mx mn ljm ljq ls lp mxm mn1 aa bb dz zr1 dab dr "
-           "fk0 fk2 fk3 d0 d1 kl kr mxu g1a k2 sl g1 gs b1 b2 bbb m0 e1 e2 e3 go2 m1").split():
-    _W[_k] = (_n[0], 32); _n[0] += 32
-
+F32, B16, I32, U16 = "float32", "bfloat16", "int32", "uint16"
+NXV = 32
 SCRATCH = {
-    "kl": ("sbuf", [128, 256], "int32"), "ul": ("sbuf", [128, 256], "int32"),
-    "ytk": ("sbuf", [128, 256], "int32"), "ytu": ("sbuf", [128, 256], "int32"),
-    "xk": ("sbuf", [128, 256], "float32"), "xu": ("sbuf", [128, 256], "float32"),
-    "zk": ("sbuf", [128, 256], "float32"), "zu": ("sbuf", [128, 256], "float32"),
-    "lstk": ("sbuf", [128, 256], "uint16"), "lstu": ("sbuf", [128, 256], "uint16"),
-    "u1i": ("sbuf", [128, 256], "int32"),
-    "di": ("sbuf", [128, 1536], "int32"), "db": ("sbuf", [128, 2048], "bfloat16"),
-    "pn": ("sbuf", [128, 256], "int32"), "pc3": ("sbuf", [128, 2], "int32"), "adc": ("sbuf", [128, 1], "float32"),
-    "pcf": ("sbuf", [128, 1], "float32"),
-    "lki": ("sbuf", [128, 64], "int32"), "a0b": ("sbuf", [128, 256], "bfloat16"),
-    "swin": ("sbuf", [128, 4096], "bfloat16"), "mwin": ("sbuf", [128, 4096], "bfloat16"),
-    "cwin": ("sbuf", [128, 4096], "bfloat16"), "meta": ("sbuf", [128, 4096], "bfloat16"), "bt": ("sbuf", [128, 4096], "bfloat16"),
-    "ax0": ("sbuf", [128, 4096], "bfloat16"), "ax1": ("sbuf", [128, 4096], "bfloat16"),
-    "p0": ("sbuf", [128, 2048], "float32"), "p1": ("sbuf", [128, 2048], "float32"),
-    "gm0": ("sbuf", [128, 2048], "bfloat16"), "gm1": ("sbuf", [128, 2048], "bfloat16"),
-    "mg0": ("sbuf", [128, 2048], "bfloat16"), "mg1": ("sbuf", [128, 2048], "bfloat16"),
-    "df": ("sbuf", [128, 1024], "bfloat16"), "dabs": ("sbuf", [128, 1024], "bfloat16"),
-    "kd": ("sbuf", [128, 1024], "float32"), "kmn": ("sbuf", [128, 768], "float32"),
-    "mk0": ("sbuf", [128, 1024], "bfloat16"),
-    "xc": ("sbuf", [128, 256], "int32"), "xh": ("sbuf", [128, 256], "int32"), "xy": ("sbuf", [128, 256], "float32"),
-    "xw": ("sbuf", [128, 704], "float32"), "xo": ("sbuf", [128, 256], "float32"),
-    "y": ("sbuf", [128, 256], "float32"), "yn": ("sbuf", [128, 256], "float32"),
-    "pr": ("sbuf", [128, 1024], "float32"), "a2": ("sbuf", [128, 512], "float32"),
-    "cl": ("sbuf", [128, 256], "uint16"), "l2": ("sbuf", [128, 256], "uint16"), "ml": ("sbuf", [128, 256], "uint16"),
-    "w0": ("sbuf", [128, _n[0]], "float32"), "w1": ("sbuf", [128, _n[0]], "float32"),
-    "wi0": ("sbuf", [128, 128], "int32"), "wi1": ("sbuf", [128, 128], "int32"),
-    "idf": ("sbuf", [128, 128], "float32"), "idb": ("sbuf", [128, 128], "bfloat16"), "zz": ("sbuf", [128, 128], "float32"),
-    "b4": ("sbuf", [128, 32], "float32"), "bqb": ("sbuf", [128, 128], "bfloat16"),
-    "wt": ("sbuf", [128, 512], "float32"), "w4": ("sbuf", [128, 8], "float32"),
-    "wm": ("sbuf", [128, 56], "float32"), "wmb": ("sbuf", [128, 56], "bfloat16"),
-    "cf": ("sbuf", [128, 256], "float32"), "lby": ("sbuf", [128, 256], "float32"), "eqt": ("sbuf", [128, 1024], "float32"),
-    "ypt": ("sbuf", [128, 1024], "float32"), "ycs": ("sbuf", [128, 256], "float32"),
-    "acc": ("sbuf", [128, 512], "float32"), "fin": ("sbuf", [128, 256], "float32"), "yes": ("sbuf", [128, 256], "float32"),
+    "kl": ("sbuf", [128, 256], I32), "ul": ("sbuf", [128, 256], I32), "pn": ("sbuf", [128, 2], I32), "pf": ("sbuf", [128, 1], F32),
+    "ytk": ("sbuf", [128, 2, 8, 16], I32), "xk": ("sbuf", [128, 256], F32), "zk": ("sbuf", [128, 256], F32),
+    "lstk": ("sbuf", [128, 256], U16),
+    "di": ("sbuf", [128, 2, 256], I32), "db": ("sbuf", [128, 9, 256], B16), "dp": ("sbuf", [128, 4, 128], B16),
+    "lki": ("sbuf", [128, 64], I32), "lku": ("sbuf", [128, 64], U16), "lkk": ("sbuf", [128, 64], F32), "kof": ("sbuf", [128, 64], F32),
+    "a0b": ("sbuf", [128, 256], B16), "il": ("sbuf", [128, 64], U16),
+    "swin": ("sbuf", [128, 4096], B16), "mwin": ("sbuf", [128, 4096], B16), "cwin": ("sbuf", [128, 2048], B16),
+    "meta": ("sbuf", [128, 4096], B16), "kk": ("sbuf", [128, 4096], B16),
+    "ax0": ("sbuf", [128, 2048], B16), "ax1": ("sbuf", [128, 2048], B16),
+    "df": ("sbuf", [128, 1024], B16), "dabs": ("sbuf", [128, 1024], B16),
+    "kd": ("sbuf", [128, 4, 4, 16], F32), "km": ("sbuf", [128, 4, 2, 16], F32), "ki": ("sbuf", [128, 128], I32),
+    "xc": ("sbuf", [128, 4, 64], I32), "xh": ("sbuf", [128, 4, 64], I32), "xy": ("sbuf", [128, 4, 64], F32),
+    "xw": ("sbuf", [128, 11, 64], F32), "xo": ("sbuf", [128, 4, 64], F32), "y": ("sbuf", [128, 256], F32),
+    "one": ("sbuf", [128, 256], F32), "idf": ("sbuf", [128, 144], F32), "idb": ("sbuf", [128, 128], B16),
+    "gi": ("sbuf", [128, 8], F32), "gh": ("sbuf", [128, 8], F32), "m32": ("sbuf", [128, 32], F32), "g16": ("sbuf", [128, 128], F32),
+    "cf": ("sbuf", [128, 16 * NXV], F32), "xv": ("sbuf", [128, NXV], F32), "pt": ("sbuf", [128, 4, 5, 4], F32),
+    "w16": ("sbuf", [128, 4, 8, 4], F32), "wz": ("sbuf", [128, 3, 16], F32),
+    "wg": ("sbuf", [128, 32, 8, 4], B16), "wl": ("sbuf", [128, 4, 32, 4], B16), "wp": ("sbuf", [128, 8, 8, 4], F32),
+    "sel": ("sbuf", [128, 4, 144], F32), "zq": ("sbuf", [128, 4, 144], B16), "wi": ("sbuf", [128, 128], B16),
+    "r4": ("sbuf", [128, 128], F32), "r5": ("sbuf", [128, 160], F32), "kc": ("sbuf", [128, 160], B16),
+    "ycs": ("sbuf", [128, 256], F32), "acc": ("sbuf", [128, 256], F32), "yes": ("sbuf", [128, 256], F32),
 }
-for _k in range(8): SCRATCH["dg%d" % _k] = ("dram", [8, 4096], "bfloat16")
+for _h in "01":
+    for _n, _s, _d in (("yw", [256], F32), ("yg", [512], F32), ("cl", [128], U16), ("l2", [128], U16), ("ml", [128], U16), ("nr", [128], F32),
+                       ("lam", [128], B16), ("p", [2048], F32), ("gm", [2048], B16), ("mg", [2048], B16), ("x", [128, 28], F32),
+                       ("dn", [128], F32), ("mk", [128], F32), ("sl", [128, 4], F32), ("st", [128, 4], F32), ("zl", [32, 4], F32),
+                       ("zs", [36, 4], F32), ("zp", [32, 4], F32), ("dt", [128, 4], F32), ("t5", [160], F32), ("so", [4, 128], F32)):
+        SCRATCH[_n + _h] = ("sbuf", [128] + _s, _d)
+    for _n in ("pK", "pC", "pD"): SCRATCH[_n + _h] = ("psum", [128, 4, 128], F32)
+    SCRATCH["pL" + _h] = ("psum", [128, 512], F32)
 for _k in range(4):
-    SCRATCH["ra%d" % _k] = ("sbuf", [128, 256], "bfloat16")
-    SCRATCH["rl%d" % _k] = ("sbuf", [128, 64], "uint16")
-    SCRATCH["rm%d" % _k] = ("sbuf", [128, 1024], "bfloat16")
-    SCRATCH["rE%d" % _k] = ("sbuf", [128, 256], "float32")
-    SCRATCH["ms%d" % _k] = ("sbuf", [128, 256], "float32")
-for _k in ("pA", "pM", "pN", "pL"):
-    for _h in "01": SCRATCH[_k + _h] = ("psum", [128, 512], "float32")
+    SCRATCH["ra%d" % _k] = ("sbuf", [128, 256], B16)
+    SCRATCH["ri%d" % _k] = ("sbuf", [128, 64], U16)
+for _k in range(5):
+    SCRATCH["ms%d" % _k] = ("sbuf", [128, 256], F32)
+    if _k: SCRATCH["rE%d" % _k] = ("sbuf", [128, 256], F32)
 
-_DS = ["dk", "du", "da", "dl", "da0", "dyk", "dyu", "dxc", "dss", "dmm", "ddg", "dcw", "dm1", "dm2", "dy0", "dyc", "dye0", "dye1"]
-SEMAPHORES = ["sv", "ss", "sp", "sg", "rl"] + _DS + ["aA%d" % k for k in range(4)] + ["aL%d" % k for k in range(4)] \
-    + ["aM%d" % k for k in range(4)] + ["aE1", "aE2", "aE3a", "aE3b"]
+_DS = ["dk", "du", "da", "dl", "da0", "dyk", "dxc", "dss", "dmm", "dxv", "dcw", "dm0", "dm1", "dm2", "dm3", "dy0", "dyc", "dye0", "dye1"]
+SEMAPHORES = ["sv", "ss", "sp", "sg", "rl"] + _DS + ["aA%d" % k for k in range(4)] + ["aI%d" % k for k in range(4)] + ["aE%d" % k for k in range(1, 5)]
+
+ALL = slice(None)
+
+
+def S(a, b=None, c=None): return slice(a, b, c)
+
+
+def telescoped(slot_of):
+    w = {}
+    for t in range(4):
+        w[(slot_of(t), t)] = w.get((slot_of(t), t), 0) + 1
+        if t < 3: w[(slot_of(t + 1), t)] = w.get((slot_of(t + 1), t), 0) - 1
+    return [(s, t, c) for (s, t), c in sorted(w.items()) if c]
+
+
+PATTERNS = [[(t, t, 1) for t in range(4)], telescoped(lambda t: t ^ 1), telescoped(lambda t: 2 - (t & 2)), telescoped(lambda t: 3 - (t & 2)),
+            telescoped(lambda t: t)]
+P_ID, P_U, P_A, P_B, P_T = range(5)
+KID = {0: 1.0, 1: 1.0}; UP = {2: 1.0, 3: 2.0, 4: 2.0}; UPP = {3: 1.0, 4: 1.0}; NODE = {5: 1.0, 6: 2.0, 7: 256.0}; NP = {6: 1.0, 7: 128.0}
+KKL = {8: 1.0, 9: 1.0}; KKR = {10: 1.0, 11: 1.0}; NP2 = {13: 1.0, 14: 128.0}
+
+
+def lin(*terms):
+    d = {}
+    for c, rows in terms:
+        for k, w in rows.items(): d[k] = d.get(k, 0.0) + c * w
+    return d
+
+
+VALUES = [UP, KID, NODE, lin((1, KKR), (-1, KID)), lin((1, KKL), (-1, KKR)), lin((4096, NP2), (1, UPP)), lin((-4096, NP2)), lin((-1, NP)), {12: 1.0}]
 
 
 def rank_program(g, core, T, topo):
@@ -73,7 +91,18 @@ def rank_program(g, core, T, topo):
     peers = [c for c in cores if c != core]
     Q = {"V": g.vector, "S": g.scalar, "P": g.tensor, "G": g, "Y": g.sync}
     SEM = {"V": "sv", "S": "ss", "P": "sp", "G": "sg"}
-    cnt = {}; known = {e: {} for e in Q}; snap = {}; lastw = {}; reads = {}; bank = {}
+    cnt = {}; known = {e: {} for e in Q}; snap = {}; wr = {}; rd = {}; bank = {}; masks = {}
+
+    def A(name, *ix, rows=ALL):
+        shape = SCRATCH[name][1][1:]
+        ix = tuple(ix) if ix else (ALL,)
+        key = (name, repr(ix))
+        if key not in masks:
+            m = np.zeros(shape, bool); m[ix] = True
+            masks[key] = int("".join("1" if x else "0" for x in m.reshape(-1)), 2)
+        return (T[name][(rows,) + ix], [(name, masks[key])])
+
+    def IN(win, off): return (win[0].indirect(off[0]), win[1] + off[1])
 
     def need(e, evs):
         best = {}
@@ -86,454 +115,440 @@ def rank_program(g, core, T, topo):
                 if kn.get(s2, 0) < v2: kn[s2] = v2
             kn[s] = v
 
-    def deps(e, r, w, b, asyn=False):
+    def deps(e, key, r, w, acc=False):
         evs = []
-        for t in r:
-            if t in lastw: evs.append(lastw[t])
-        for t in w:
-            if t in lastw: evs.append(lastw[t])
-            for e2, ev in reads.get(t, {}).items():
-                if e2 != e or asyn: evs.append(ev)
-        for t in b:
-            for e2, ev in bank.get(t, {}).items():
-                if e2 != e: evs.append(ev)
+        for n, m in r:
+            evs += [ev for m2, k2, ev in wr.get(n, []) if m & m2]
+        for n, m in w:
+            evs += [ev for m2, k2, ev in wr.get(n, []) if m & m2 and not (acc and k2[:len(key)] == key)]
+            evs += [ev for (k2, m2), ev in rd.get(n, {}).items() if m & m2 and k2 != key]
+        for n, m in r + w:
+            evs += [ev for k2, ev in bank.get(n, {}).items() if k2 != key]
         need(e, evs)
 
-    def done(e, key, ev, r, w, b):
+    def done(e, key, ev, r, w, part=False):
         snap[ev] = dict(known[e])
-        for t in r: reads.setdefault(t, {})[key] = ev
-        for t in w:
-            lastw[t] = ev; reads[t] = {}
-        for t in b: bank.setdefault(t, {})[key] = ev
+        for n, m in w:
+            if part: wr[n] = wr.get(n, []) + [(m, key, ev)]
+            else:
+                wr[n] = [(m2 & ~m, k2, v2) for m2, k2, v2 in wr.get(n, []) if m2 & ~m] + [(m, key, ev)]
+                rd[n] = {k: v2 for k, v2 in rd.get(n, {}).items() if k[1] & ~m}
+        for n, m in r: rd.setdefault(n, {})[(key, m)] = ev
+        for n, m in r + w:
+            if SCRATCH[n][0] == "psum": bank.setdefault(n, {})[key] = ev
 
-    def op(e, calls, r=(), w=(), b=()):
-        deps(e, r, w, b)
+    def op(e, calls, r, w, acc=False):
+        r = [x for a in r if isinstance(a, tuple) for x in a[1]]; w = [x for a in w for x in a[1]]
+        deps(e, e, r, w, acc)
         s = SEM[e]
-        for c in (calls if isinstance(calls, list) else [calls]):
+        for c in calls:
             c().then_inc(T.sem[s], 1); cnt[s] = cnt.get(s, 0) + 1
-        done(e, e, (s, cnt[s]), r, w, b)
+        done(e, e, (s, cnt[s]), r, w)
 
-    def dmag(e, pairs, sem, r=(), w=()):
-        deps(e, r, w, (), True)
+    def dma(e, pairs, sem, part=False):
+        r = [x for o, i in pairs for x in i[1]]; w = [x for o, i in pairs for x in o[1]]
+        deps(e, "dma" if part else "dma" + sem, r, w, part)
         for o, i in pairs:
-            Q[e].dma_start(out=o, in_=i).then_inc(T.sem[sem], 16)
+            Q[e].dma_start(out=o[0], in_=i[0]).then_inc(T.sem[sem], 16)
         cnt[sem] = 16 * len(pairs)
-        done(e, "dma" + sem, (sem, cnt[sem]), r, w, ())
+        done(e, "dma" + sem, (sem, cnt[sem]), r, w, part)
 
-    def send(src, name, dsts, rsem, r):
-        deps("G", r, (), ())
-        eng = topo.engines(core, dsts[0][0])
+    def H(ap): return (ap, [])
+
+    def send(src, dst, to, rsem):
+        deps("G", "send", src[1], [])
         ids = []
-        for c, _x in dsts:
+        for c in to:
             a = topo.addr(c); ids.append(DstId(rid=a[0], pnc=a[1]))
-        g.remote_dma_fused([RemoteDMATransfer(dst_ids=ids, dma_engine_mask=topo.mask(core, dsts[0][0]), remote_sem=T.sem[rsem],
-                                              srcs=[src], dsts=[d for _c, d in dsts])], local_sem=T.sem.rl)
-        cnt["rl"] = cnt.get("rl", 0) + len(eng)
+        g.remote_dma_fused([RemoteDMATransfer(dst_ids=ids, dma_engine_mask=topo.mask(core, to[0]), remote_sem=T.sem[rsem],
+                                              srcs=[src[0]], dsts=[dst[0] for c in to])], local_sem=T.sem.rl)
+        cnt["rl"] = cnt.get("rl", 0) + len(topo.engines(core, to[0]))
 
-    def v(n, h, st=0, step=1):
-        o, w = _W[n]; return T["w%d" % h][:, o + st:o + w:step]
+    def val(x): return x[0] if isinstance(x, tuple) else x
 
-    def vb(n, h, a, b):
-        o, w = _W[n]; return T["w%d" % h][:, o + a:o + b]
+    def tt(o, a, b, f): op("V", [lambda: g.vector.tensor_tensor(out=o[0], in0=a[0], in1=b[0], op=f)], [a, b], [o])
 
-    def tk(s, h): return [x + str(h) for x in s.split()]
+    def ts(o, a, s1, f0, s2=None, f1=None):
+        if f1 is None: op("V", [lambda: g.vector.tensor_scalar(out=o[0], in0=a[0], scalar1=val(s1), scalar2=None, op0=f0)], [a, s1], [o])
+        else: op("V", [lambda: g.vector.tensor_scalar(out=o[0], in0=a[0], scalar1=val(s1), scalar2=val(s2), op0=f0, op1=f1)], [a, s1, s2], [o])
 
-    def tt(o, a, b, f, h, w, r, bk=""):
-        op("V", lambda: g.vector.tensor_tensor(out=o, in0=a, in1=b, op=f), tk(r, h), tk(w, h), tk(bk, h))
+    def cp(o, a): op("V", [lambda: g.vector.tensor_copy(out=o[0], in_=a[0])], [a], [o])
 
-    def ts(o, a, s1, s2, f0, f1, r, w, b=()):
-        if f1 is None: op("V", lambda: g.vector.tensor_scalar(out=o, in0=a, scalar1=s1, scalar2=None, op0=f0), r, w, b)
-        else: op("V", lambda: g.vector.tensor_scalar(out=o, in0=a, scalar1=s1, scalar2=s2, op0=f0, op1=f1), r, w, b)
+    def scan(o, d0, d1, f):
+        op("V", [lambda: g.vector.tensor_tensor_scan(out=o[0], data0=d0[0], data1=d1[0], initial=0.0, op0=OP.mult, op1=f)], [d0, d1], [o])
 
-    def cp(o, a, r, w, b=()):
-        op("V", lambda: g.vector.tensor_copy(out=o, in_=a), r, w, b)
+    def ms(o, c): op("V", [lambda: g.vector.memset(o[0], c)], [], [o])
 
-    def act(o, a, f, r, w, b=(), bias=0.0, scale=1.0):
-        op("S", lambda: g.scalar.activation(out=o, in_=a, func=f, bias=bias, scale=scale), r, w, b)
+    def act(o, a, f=AF.Copy, bias=0.0, scale=1.0):
+        op("S", [lambda: g.scalar.activation(out=o[0], in_=a[0], func=f, bias=val(bias), scale=val(scale))], [a, bias, scale], [o])
 
-    def ms(o, c, w):
-        op("V", lambda: g.vector.memset(o, c), (), w)
+    def fill(o, c):
+        act(o, A("one", S(0, int(np.prod(o[0].shape[1:])))), scale=float(c))
 
-    def mm(o, l, r_, st, sp):
-        return lambda: g.tensor.matmul(out=o, lhsT=l, rhs=r_, start=st, stop=sp)
+    def mm(group, acc=False):
+        op("P", [(lambda q=q: g.tensor.matmul(out=q[0][0], lhsT=q[1][0], rhs=q[2][0], start=q[3], stop=q[4])) for q in group],
+           [q[1] for q in group] + [q[2] for q in group], [q[0] for q in group], acc)
 
-    RA = "ra%d" % me; RL = "rl%d" % me; RM = "rm%d" % me
+    def gsel(o, a, pat, base, cm, cmp_, fill_):
+        op("G", [lambda: g.affine_select(out=o[0], in_=a[0], pattern=pat, compare_op=cmp_, fill=fill_, base=base, channel_multiplier=cm)], [a], [o])
+
+    def iota(o, pat, base, cm, small=True):
+        op("G", [lambda: g.iota(o[0], pat, base, cm, allow_small_or_imprecise_dtypes=small)], [], [o])
+
+    def tag(s): TAG[0] = s
+
+    RA = "ra%d" % me
     ne = len(topo.engines(core, peers[0]))
     for k in range(N):
         if k != me:
-            lastw["ra%d" % k] = ("aA%d" % k, ne); lastw["rl%d" % k] = ("aL%d" % k, ne); lastw["rm%d" % k] = ("aM%d" % k, ne)
-    lastw["rE1"] = ("aE1", ne); lastw["rE2"] = ("aE2", ne); lastw["rE3h0"] = ("aE3a", ne); lastw["rE3h1"] = ("aE3b", ne)
+            wr["ra%d" % k] = [(A("ra%d" % k)[1][0][1], "far", ("aA%d" % k, ne))]
+            wr["ri%d" % k] = [(A("ri%d" % k)[1][0][1], "far", ("aI%d" % k, ne))]
+    for k in range(1, 5): wr["rE%d" % k] = [(A("rE%d" % k)[1][0][1], "far", ("aE%d" % k, ne))]
 
-    dmag("Y", [(T.kl[:, :], T.kid[:, :])], "dk", (), ["kl"])
-    dmag("S", [(T[RA][:, :], T.a[:, :])], "da", (), [RA])
-    dmag("S", [(T.lki[:, :], T.lk[:, :])], "dl", (), ["lki"])
-    dmag("S", [(T.a0b[:, :], T.a0[:, :])], "da0", (), ["a0b"])
-    dmag("Y", [(T.ul[:, :], T.up[:, :])], "du", (), ["ul"])
-    dmag("Y", [(T.ytk[:, 128 * k:128 * k + 128], T.kid[k::2, :]) for k in (0, 1)], "dyk", (), ["ytk"])
-    dmag("Y", [(T.ytu[:, 128 * k:128 * k + 128], T.up[k::2, :]) for k in (0, 1)], "dyu", (), ["ytu"])
-    dmag("S", [(T.xc[:, t * 64:t * 64 + 64], T.cut0[t::4, :]) for t in range(4)], "dxc", (), ["xc"])
-    dmag("S", [(T.swin[:, :], T.s[:, :])], "dss", (), ["swin"])
+    tag("load")
+    dma("Y", [(A("kl"), H(T.kid[:, :]))], "dk")
+    dma("S", [(A(RA), H(T.a[:, :]))], "da")
+    dma("Y", [(A("ytk", k), H(T.kid[k::2, :])) for k in (0, 1)], "dyk")
+    dma("S", [(A("lki"), H(T.lk[:, :]))], "dl")
+    dma("S", [(A("a0b"), H(T.a0[:, :]))], "da0")
+    dma("Y", [(A("ul"), H(T.up[:, :]))], "du")
+    dma("S", [(A("xc", t), H(T.cut0[t::4, :])) for t in range(4)], "dxc")
 
-    ms(T.b4[:, :], 1.0, ["b4"]); ms(T.zz[:, :], 0.0, ["zz"]); ms(T.wm[:, :], 0.0, ["wm"]); ms(T.w4[:, :], 4.0, ["w4"])
-    ms(T.cwin[:, 4080:4096], 0.0, ["cwin"]); ms(T.wt[:, :], 0.0, ["wt"])
+    tag("const")
+    ms(A("one"), 1.0); ms(A("cf"), 0.0); ms(A("pt"), 0.0)
+    for j, rows in enumerate(VALUES):
+        for k, w in rows.items(): ms(A("cf", S(k * NXV + j, k * NXV + j + 1)), w)
+    for q in range(4):
+        fill(A("cf", S(4 * q * NXV + 9 + q, (4 * q + 4) * NXV, NXV)), 1.0)
+        fill(A("cf", S(q * NXV + 13, None, 4 * NXV)), -32768.0 * (1.5 - q) / 8)
+    for f in range(4):
+        for s, t, c in PATTERNS[f]: fill(A("cf", S(s * NXV + 16 + 4 * f + t, None, 4 * NXV)), c)
+    dma("Y", [(A("xv"), A("cf", rows=S(0, 8)))], "dxv")
+    dma("Y", [(A("swin"), H(T.s[:, :]))], "dss")
+    ms(A("cwin"), 0.0)
+    iota(A("pn", S(0, 1)), [[0, 1]], 0, 1, False)
+    gsel(A("gi"), A("one", S(0, 8)), [[-16, 8]], 0, 1, OP.is_ge, 0.0)
+    gsel(A("gi"), A("gi"), [[16, 8]], 15, -1, OP.is_ge, 0.0)
+    iota(A("db", 5), [[0, 128], [1, 2]], 0, 0); iota(A("db", 6), [[1, 128], [0, 2]], 0, 0)
+    iota(A("kof"), [[256, 4], [0, 16]], 0, 0)
+    send(A(RA), A(RA), peers, "aA%d" % me)
+    gsel(A("idf"), A("one", S(0, 144)), [[-1, 144]], 8, 1, OP.is_equal, 0.0)
+    gsel(A("g16"), A("one", S(0, 128)), [[-16, 8], [0, 16]], 0, 1, OP.is_ge, 0.0)
+    gsel(A("g16"), A("g16"), [[16, 8], [0, 16]], 15, -1, OP.is_ge, 0.0)
+    gsel(A("m32"), A("one", S(0, 32)), [[-4, 4], [-16, 8]], 0, 1, OP.is_ge, 0.0)
+    gsel(A("m32"), A("m32"), [[4, 4], [16, 8]], 3, -1, OP.is_ge, 0.0)
+    for f in range(5):
+        for s, t, c in PATTERNS[f]: fill(A("pt", s, f, S(t, t + 1)), c)
 
-    def sel(buf, tok, pat, base, cm, cmp_, fill, src=None, stok=None):
-        op("G", lambda: g.affine_select(out=buf, in_=buf if src is None else src, pattern=pat, compare_op=cmp_, fill=fill, base=base,
-                                        channel_multiplier=cm), [tok] if stok is None else [stok], [tok])
-    op("G", lambda: g.iota(T.pn[:, :], [[0, 256]], 0, 1), (), ["pn"])
-    op("G", lambda: g.iota(T.di[:, 1024:1280], [[1, 256]], 0, 0), (), ["di4"])
-    sel(T.b4[:, :], "b4", [[-4, 32]], 0, 1, OP.is_ge, 0.0)
-    sel(T.b4[:, :], "b4", [[4, 32]], 3, -1, OP.is_ge, 0.0)
-
-    cp(T[RL][:, :], T.lki[:, :], ["lki"], [RL])
-    send(T[RA][:, :], RA, [(c, T[RA][:, :]) for c in peers], "aA%d" % me, [RA])
-    send(T[RL][:, :], RL, [(c, T[RL][:, :]) for c in peers], "aL%d" % me, [RL])
-
-    sel(T.idf[:, :], "idf", [[-1, 128]], 0, 1, OP.not_equal, 1.0, T.zz[:, :], "zz")
-    sel(T.w4[:, :], "w4", [[-16, 8]], 0, 1, OP.is_ge, 0.0)
-    sel(T.w4[:, :], "w4", [[16, 8]], 15, -1, OP.is_ge, 0.0)
-    TERMS = [(0, 0, 2.0), (0, 1, 512.0), (1, 9, 1.0), (1, 10, 256.0), (2, 11, 1.0), (2, 12, 256.0), (3, 13, 16.0), (3, 14, 4096.0),
-             (4, 3, 2.0), (4, 4, 512.0), (4, 5, BIG), (5, 6, 2.0), (5, 7, 512.0), (5, 8, BIG), (6, 13, 16.0), (6, 14, 4096.0), (6, 2, BIG)]
-    for o_ in range(7):
-        for oo, i_, w_ in TERMS:
-            if oo == o_: sel(T.wm[:, oo * 8:oo * 8 + 8], "wm", [[-16, 8]], -i_, 1, OP.not_equal, w_)
-
-    def spread_g(b, ax, rows):
-        for r in rows:
-            op("G", lambda: g.affine_select(out=T[ax][:, r::16], in_=T["ra%d" % b][:, :], pattern=[[0, 256]], compare_op=OP.is_gt, fill=0.0,
-                                            base=1, channel_multiplier=0), ["ra%d" % b], [ax + "r%d" % r])
-    spread_g(me, "ax0", range(8, 16))
-    for r in range(8):
-        act(T.ax0[:, r::16], T[RA][:, :], AF.Copy, [RA], ["ax0r%d" % r])
-
-    ts(T.di[:, 0:256], T.kl[:, :], 1, 255, OP.arith_shift_right, OP.bitwise_and, ["kl"], ["di0"])
-    ts(T.di[:, 256:512], T.kl[:, :], 9, None, OP.arith_shift_right, None, ["kl"], ["di1"])
-    ts(T.db[:, 1536:1792], T.kl[:, :], 0, None, OP.is_lt, None, ["kl"], ["db6"])
-    ts(T.db[:, 1792:2048], T.kl[:, :], 0, None, OP.is_ge, None, ["kl"], ["db7"])
-    ts(T.u1i[:, :], T.ul[:, :], 1, None, OP.add, None, ["ul"], ["u1i"])
-    ts(T.di[:, 1280:1536], T.pn[:, :], 15, None, OP.bitwise_and, None, ["pn"], ["di5"])
-    ts(T.di[:, 512:768], T.u1i[:, :], 255, None, OP.bitwise_and, None, ["u1i"], ["di2"])
-    ts(T.di[:, 768:1024], T.u1i[:, :], 8, None, OP.arith_shift_right, None, ["u1i"], ["di3"])
-    cp(T.db[:, 0:1536], T.di[:, :], ["di%d" % k for k in range(6)], ["db0"])
-    dmag("Y", [(T["dg%d" % k][:, :], T.db[:, 256 * k:256 * k + 256]) for k in range(8)], "ddg", ["db0", "db6", "db7"], ["dg"])
-    C = T.cwin
-    prs = [(C[i::16, :], T["dg%d" % k][:, :]) for i, k in ((0, 0), (1, 1), (2, 6), (3, 0), (4, 1), (5, 7), (9, 2), (10, 3), (11, 2), (12, 3),
-                                                           (13, 4), (14, 5), (15, 4))]
-    prs += [(C[i::16, 0:4095], T["dg%d" % k][:, 1:4096]) for i, k in ((6, 0), (7, 1), (8, 7))]
-    dmag("Y", prs, "dcw", ["dg"], ["cwin"])
-    dmag("Y", [(T.mwin[:, :], T.m[:, :])], "dmm", (), ["mwin"])
-
-    def dist(aw, lkb, mout):
-        for k in range(4):
-            op("V", lambda: g.vector.tensor_tensor(out=T.df[:, k * 256:k * 256 + 256], in0=T[aw][:, 0:256].indirect(T[lkb][:, 16 * k:16 * k + 16]),
-                                                   in1=T[RA][:, :], op=OP.subtract), [aw, lkb, RA], ["df%d" % k])
-        for k in range(2):
-            act(T.dabs[:, k * 512:k * 512 + 512], T.df[:, k * 512:k * 512 + 512], AF.Abs, ["df%d" % (2 * k), "df%d" % (2 * k + 1)], ["dabs%d" % k])
-            op("P", mm(T["pL%d" % k][:, :], T.bqb[:, :], T.dabs[:, k * 512:k * 512 + 512], True, True), ["bqb", "dabs%d" % k], ["dp%d" % k], ["pL%d" % k])
-        for k in range(4):
-            act(T.kd[:, k * 256:k * 256 + 256], T["pL%d" % (k // 2)][:, (k % 2) * 256:(k % 2) * 256 + 256], AF.Identity, ["dp%d" % (k // 2)],
-                ["kd%d" % k], ["pL%d" % (k // 2)], float(k), 4.0)
-
-    def dist2(mout):
-        op("V", lambda: g.vector.tensor_tensor(out=T.kmn[:, 0:512], in0=T.kd[:, 0:512], in1=T.kd[:, 512:1024], op=OP.min),
-           ["kd0", "kd1", "kd2", "kd3"], ["kmn"])
-        op("V", lambda: g.vector.tensor_tensor(out=T.kmn[:, 512:768], in0=T.kmn[:, 0:256], in1=T.kmn[:, 256:512], op=OP.min), ["kmn"], ["kmm"])
-        for k in range(4):
-            op("V", lambda: g.vector.tensor_tensor(out=T[mout][:, k * 256:k * 256 + 256], in0=T.kd[:, k * 256:k * 256 + 256], in1=T.kmn[:, 512:768],
-                                                   op=OP.is_equal), ["kd%d" % k, "kmm"], [mout])
-
-    for k in range(4): cp(T.bqb[:, k::4], T.b4[:, :], ["b4"], ["bqb"])
-    dist("a0b", RL, "mk0")
-
-    for yt, x_, z_, ls_ in (("ytk", "xk", "zk", "lstk"), ("ytu", "xu", "zu", "lstu")):
-        for b in range(8):
-            for k in (0, 1):
-                cp(T[x_][:, 32 * b + 16 * k:32 * b + 16 * k + 16], T[yt][:, 128 * k + 16 * b:128 * k + 16 * b + 16], [yt], [x_])
-        op("V", lambda: g.vector.transpose(out=T[z_][:, :], in_=T[x_][:, :]), [x_], [z_])
-        for b in range(8):
-            cp(T[ls_][:, b::8], T[z_][:, 32 * b:32 * b + 32], [z_], [ls_])
-    dist2("mk0")
-    op("S", lambda: g.scalar.activation(out=T.meta[:, :], in_=T.cwin[:, :].indirect(T.lstk[:, :]), func=AF.Copy), ["cwin", "lstk"], ["meta"])
-    op("S", lambda: g.scalar.activation(out=T.bt[:, :], in_=T.cwin[:, :].indirect(T.lstu[:, :]), func=AF.Copy), ["cwin", "lstu"], ["bt"])
-    dmag("Y", [(T.meta[i::16, :], T["dg%d" % k][:, :]) for i, k in ((0, 0), (1, 1), (2, 6), (9, 2), (10, 3), (13, 4), (14, 5))], "dm1", ["dg"], ["meta"])
-
-    ts(T.xh[:, :], T.xc[:, :], 1, None, OP.arith_shift_right, None, ["xc"], ["xh"])
-    for t in range(4):
-        ts(T.xy[:, t * 64:t * 64 + 64], T.xc[:, t * 64:t * 64 + 64], 1.0, (3 - t) / 16.0, OP.mult, OP.add, ["xc"], ["xy%d" % t])
-
-    def xw(k): return T.xw[:, k * 64:k * 64 + 64]
-
-    def xs(b, t): return b[:, t * 64:t * 64 + 64]
-
-    def x2(o, a, b, f, r, w): op("V", lambda: g.vector.tensor_tensor(out=o, in0=a, in1=b, op=f), r, w)
-    for k, (i, j) in enumerate(((0, 2), (1, 3), (0, 3), (1, 2))):
-        x2(xw(k), xs(T.xh, i), xs(T.xh, j), OP.is_equal, ["xh"], ["xw%d" % k])
-    x2(xw(6), xs(T.xy, 2), xs(T.xy, 1), OP.subtract, ["xy1", "xy2"], ["xw6"])
-    x2(xw(7), xs(T.xy, 3), xs(T.xy, 1), OP.subtract, ["xy1", "xy3"], ["xw7"])
-    x2(xw(4), xw(0), xw(1), OP.max, ["xw0", "xw1"], ["xw4"])
-    x2(xw(5), xw(2), xw(3), OP.max, ["xw2", "xw3"], ["xw5"])
-    cp(xs(T.xo, 0), xs(T.xy, 0), ["xy0"], ["xo"])
-    x2(xw(8), xw(4), xw(6), OP.mult, ["xw4", "xw6"], ["xw8"])
-    x2(xw(9), xw(5), xw(7), OP.mult, ["xw5", "xw7"], ["xw9"])
-    x2(xw(10), xs(T.xy, 1), xw(8), OP.add, ["xy1", "xw8"], ["xw10"])
-    x2(xs(T.xo, 2), xs(T.xy, 2), xw(8), OP.subtract, ["xy2", "xw8"], ["xo"])
-    x2(xs(T.xo, 3), xs(T.xy, 3), xw(9), OP.subtract, ["xy3", "xw9"], ["xo"])
-    x2(xs(T.xo, 1), xw(10), xw(9), OP.add, ["xw10", "xw9"], ["xo"])
-    dmag("Y", [(T.y[t::4, :], T.xo[:, t * 64:t * 64 + 64]) for t in range(4)], "dy0", ["xo"], ["y0", "y1"])
-    dmag("Y", [(T.meta[i::16, :], T.bt[i::16, :]) for i in (11, 12)], "dm2", ["bt"], ["meta"])
-    cp(T.idb[:, :], T.idf[:, :], ["idf"], ["idb"])
-    cp(T.wmb[:, :], T.wm[:, :], ["wm"], ["wmb"])
-    ts(T.pc3[:, 0:1], T.pn[:, 0:1], 3, None, OP.bitwise_and, None, ["pn"], ["pc3"])
-    ts(T.adc[:, :], T.pc3[:, 0:1], -2, -1, OP.add, OP.max, ["pc3"], ["adc"])
-
-    AXR = lambda h: ["ax%dr%d" % (h % 2, r) for r in range(16)]
-
-    def pmx(o_, h, st=0, step=1): return T["pM%d" % h][:, o_ * 128 + st:o_ * 128 + 128:step]
-
-    def pnx(o_, h, st=0, step=1): return T["pN%d" % h][:, o_ * 128 + st:o_ * 128 + 128:step]
-
-    def gather_mul(h, lst, tok, vis, w):
-        op("V", lambda: g.vector.tensor_tensor(out=T["p%d" % h][:, :], in0=T.swin[:, :].indirect(T[lst][:, h * 128:h * 128 + 128]),
-                                               in1=T["ax%d" % (vis % 2)][:, h * 2048:h * 2048 + 2048], op=OP.mult),
-           ["swin", tok + str(h)] + AXR(vis), ["p%d" % h])
-
-    def dots(h, col, w):
-        op("P", [mm(T["pA%d" % h][:, col + r:col + 128:16], T["p%d" % h][:, r::16], T.w4[:, :], True, True) for r in range(16)],
-           ["p%d" % h, "w4"], [w + str(h)], ["pA%d" % h])
-
-    def meta_mm(h):
-        op("P", mm(pnx(3, h), T.yn[:, h * 128:h * 128 + 128], T.idf[:, :], True, True), ["yn%d" % h, "idf"], ["yd%d" % h], ["pN%d" % h])
-        cl = []
-        for r in range(16):
-            cl.append(mm(T["pM%d" % h][:, r::16], T["gm%d" % h][:, r::16], T.wmb[:, 0:32], True, True))
-            cl.append(mm(T["pN%d" % h][:, r:384:16], T["gm%d" % h][:, r::16], T.wmb[:, 32:56], True, True))
-        op("P", cl, ["gm%d" % h, "wmb"], ["m%d" % h, "n%d" % h], ["pM%d" % h, "pN%d" % h])
-
-    def s_copies(h):
-        act(v("ups", h), pmx(1, h), AF.Copy, tk("m", h), tk("ups", h), ["pM%d" % h])
-        act(v("yd16", h), pnx(3, h), AF.Identity, tk("yd", h), tk("yd16", h), ["pN%d" % h], 0.0, 16.0)
-
-    def off_a(h):
-        tt(v("lab", h), v("yd16", h), pmx(3, h), OP.subtract, h, "lab", "yd16 m", "pM")
-        tt(v("eq", h), v("ups", h, 0, 2), pmx(1, h, 1, 2), OP.is_equal, h, "eq", "ups m", "pM")
-        tt(v("lbk", h), v("yd16", h), pnx(2, h), OP.subtract, h, "lbk", "yd16 n", "pN")
-        tt(v("peq", h), v("eq", h), pmx(1, h, 0, 2), OP.mult, h, "peq", "eq m", "pM")
-        tt(v("xa", h), v("lab", h, 0, 2), v("lab", h, 1, 2), OP.max, h, "xa", "lab")
-        tt(v("na", h), v("lab", h, 0, 2), v("lab", h, 1, 2), OP.min, h, "na", "lab")
-
-    def dec1(h):
-        tt(v("kes", h), v("lbk", h), T["pA%d" % h][:, 0:128], OP.add, h, "kes", "lbk ke", "pA")
-        e, o = v("kes", h, 0, 2), v("kes", h, 1, 2)
-        tt(v("mab", h), e, o, OP.max, h, "mab", "kes")
-        tt(v("w1", h), o, e, OP.is_gt, h, "w1", "kes")
-        tt(v("w0", h), e, o, OP.is_gt, h, "w0", "kes")
-        A, B = v("mab", h, 0, 2), v("mab", h, 1, 2)
-        tt(v("sab", h, 0, 2), A, B, OP.is_gt, h, "sA", "mab")
-        tt(v("sab", h, 1, 2), B, A, OP.is_gt, h, "sB", "mab")
-        tt(v("o", h, 0, 2), v("sab", h), v("w0", h), OP.mult, h, "oe", "sA sB w0")
-        tt(v("o", h, 1, 2), v("sab", h), v("w1", h), OP.mult, h, "oo", "sA sB w1")
-        sA, sB = v("sab", h, 0, 2), v("sab", h, 1, 2)
-        tt(v("pa", h), sB, v("peq", h, 0, 2), OP.mult, h, "pa", "sB peq")
-        tt(v("pb", h), sA, v("peq", h, 1, 2), OP.mult, h, "pb", "sA peq")
-        tt(v("prk", h), v("o", h), pmx(0, h), OP.mult, h, "prk", "oe oo m", "pM")
-        tt(v("ga", h), sB, pmx(2, h, 0, 4), OP.mult, h, "ga", "sB m", "pM")
-        tt(v("gb", h), sA, pmx(2, h, 2, 4), OP.mult, h, "gb", "sA m", "pM")
-        tt(v("t1", h), v("prk", h, 0, 2), v("prk", h, 1, 2), OP.add, h, "t1", "prk")
-        tt(v("lt", h, 0, 4), v("pa", h), v("pb", h), OP.add, h, "lta", "pa pb")
-        tt(v("lt", h, 1, 4), v("ga", h), v("gb", h), OP.add, h, "ltb", "ga gb")
-        tt(v("lt", h, 2, 4), v("t1", h, 0, 2), v("t1", h, 1, 2), OP.add, h, "ltc", "t1")
-        tt(v("lt", h, 3, 4), v("t1", h, 0, 2), v("t1", h, 1, 2), OP.add, h, "ltd", "t1")
-        op("P", mm(T["pL%d" % h][:, 0:128], v("lt", h), T.idf[:, :], True, True), tk("lta ltb ltc ltd", h) + ["idf"], tk("plt", h), ["pL%d" % h])
-
-    def conv(h):
-        ts(T.l2[:, h * 128:h * 128 + 128], T["pL%d" % h][:, 0:128], T.adc[:, 0:1], None, OP.add, None, tk("plt", h) + ["adc"], tk("l2", h), ["pL%d" % h])
-
-    def off_b1(h):
-        sA, sB = v("sab", h, 0, 2), v("sab", h, 1, 2)
-        tt(v("nab", h), v("kes", h, 0, 2), v("kes", h, 1, 2), OP.min, h, "nab", "kes")
-        tt(vb("mk", h, 0, 32), v("mab", h, 0, 2), v("mab", h, 1, 2), OP.max, h, "mka", "mab")
-        tt(v("ja", h), sB, v("xa", h, 0, 2), OP.mult, h, "ja", "sB xa")
-        tt(v("jb", h), sA, v("xa", h, 1, 2), OP.mult, h, "jb", "sA xa")
-        tt(v("pa2", h), sB, v("na", h, 0, 2), OP.mult, h, "pa2", "sB na")
-        tt(v("pb2", h), sA, v("na", h, 1, 2), OP.mult, h, "pb2", "sA na")
-        tt(v("ka", h), sA, v("nab", h, 0, 2), OP.mult, h, "ka", "sA nab")
-        tt(v("kb", h), sB, v("nab", h, 1, 2), OP.mult, h, "kb", "sB nab")
-        tt(v("lj", h), v("ja", h), v("jb", h), OP.add, h, "lj", "ja jb")
-        tt(v("ljp", h), v("pa2", h), v("pb2", h), OP.add, h, "ljp", "pa2 pb2")
-        tt(vb("mk", h, 32, 64), v("ka", h), v("kb", h), OP.add, h, "mkb", "ka kb")
-        tt(v("prl", h), v("o", h), pnx(0, h), OP.mult, h, "prl", "oe oo n", "pN")
-        tt(v("prr", h), v("o", h), pnx(1, h), OP.mult, h, "prr", "oe oo n", "pN")
-        wi = T["wi%d" % h]
-        cp(wi[:, 0:64], v("mk", h), tk("mka mkb", h), tk("mki", h))
-        tt(v("u1", h), v("o", h, 1, 2), pmx(1, h, 0, 2), OP.mult, h, "u1", "oo m", "pM")
-        tt(v("u2", h), v("o", h, 0, 2), pmx(1, h, 1, 2), OP.mult, h, "u2", "oe m", "pM")
-        ts(wi[:, 64:128], wi[:, 0:64], 3, None, OP.bitwise_and, None, tk("mki", h), tk("mkj", h))
-        tt(v("y1", h), v("o", h, 1, 2), pnx(3, h, 0, 2), OP.mult, h, "y1t", "oo yd", "pN")
-        tt(v("y2", h), v("o", h, 0, 2), pnx(3, h, 1, 2), OP.mult, h, "y2t", "oe yd", "pN")
-        cp(v("lbf", h), wi[:, 64:128], tk("mkj", h), tk("lbf", h))
-        tt(v("tl", h), v("prl", h, 0, 2), v("prl", h, 1, 2), OP.add, h, "tl", "prl")
-        tt(v("tr", h), v("prr", h, 0, 2), v("prr", h, 1, 2), OP.add, h, "tr", "prr")
-        tt(v("u3", h), v("u1", h), v("u2", h), OP.add, h, "u3", "u1 u2")
-        tt(v("y3", h), v("y1", h), v("y2", h), OP.add, h, "y3", "y1t y2t")
-        tt(vb("z", h, 0, 32), v("tl", h, 0, 2), v("tl", h, 1, 2), OP.add, h, "za", "tl")
-        tt(vb("z", h, 32, 64), v("tr", h, 0, 2), v("tr", h, 1, 2), OP.add, h, "zb", "tr")
-        tt(v("mx", h), v("lj", h), vb("lbf", h, 32, 64), OP.max, h, "mx", "lj lbf")
-        tt(v("mn", h), v("lj", h), vb("lbf", h, 32, 64), OP.min, h, "mn", "lj lbf")
-        tt(v("upu", h), v("u3", h, 0, 2), v("u3", h, 1, 2), OP.add, h, "upu", "u3")
-        tt(v("s1", h, 1, 4), v("y3", h, 0, 2), v("y3", h, 1, 2), OP.add, h, "s1b", "y3")
-        ts(v("hasp", h), v("lt", h, 0, 4), 0.0, None, OP.is_gt, None, tk("lta", h), tk("hasp", h))
-        tt(v("sib", h), v("upu", h), v("lt", h, 1, 4), OP.is_equal, h, "sib", "upu ltb")
-        c = 1.0 / 16.0
-        act(v("ljm", h), v("lj", h), AF.Identity, tk("lj", h), tk("ljm", h), (), -1.0, c)
-        act(v("ljq", h), v("ljp", h), AF.Identity, tk("ljp", h), tk("ljq", h), (), 1.0, c)
-        act(v("lp", h), v("ljp", h), AF.Identity, tk("ljp", h), tk("lp", h), (), 0.0, c)
-        act(v("ls", h), vb("lbf", h, 0, 32), AF.Identity, tk("lbf", h), tk("ls", h), (), 0.0, c)
-        act(v("zc", h), v("z", h), AF.Relu, tk("za zb", h), tk("zc", h), (), -BIG, 1.0)
-        act(v("mxm", h), v("mx", h), AF.Identity, tk("mx", h), tk("mxm", h), (), -1.0, c)
-        act(v("mn1", h), v("mn", h), AF.Identity, tk("mn", h), tk("mn1", h), (), 1.0, c)
-
-    def off_b2(h):
-        za, zb = vb("zc", h, 0, 32), vb("zc", h, 32, 64)
-        tt(v("s1", h, 0, 4), v("lt", h, 0, 4), v("ljm", h), OP.add, h, "s1a", "lta ljm")
-        tt(v("s1", h, 2, 4), v("lt", h, 2, 4), v("ls", h), OP.add, h, "s1c", "ltc ls")
-        tt(v("s1", h, 3, 4), v("lt", h, 3, 4), v("ljq", h), OP.add, h, "s1d", "ltd ljq")
-        tt(v("aa", h), za, v("ls", h), OP.add, h, "aa", "zc ls")
-        tt(v("bb", h), zb, v("lp", h), OP.add, h, "bb", "zc lp")
-        tt(v("dz", h), za, zb, OP.subtract, h, "dz", "zc")
-        tt(v("s2", h, 0, 4), v("lt", h, 1, 4), v("mxm", h), OP.add, h, "s2a", "ltb mxm")
-        tt(v("zr1", h), zb, v("mn1", h), OP.add, h, "zr1", "zc mn1")
-        tt(v("dab", h), v("aa", h), v("bb", h), OP.subtract, h, "dab", "aa bb")
-        tt(v("dr", h), v("s1", h, 3, 4), v("s1", h, 2, 4), OP.subtract, h, "dr", "s1c s1d")
-
-    def dec2(h):
-        def F(k): return T["pA%d" % h][:, 128 + k:256:4]
-        ls, M, KU = vb("lbf", h, 0, 32), vb("mk", h, 0, 32), vb("mk", h, 32, 64)
-        pa = ["pA%d" % h]
-        tt(v("fk2", h), ls, F(2), OP.add, h, "fk2", "lbf f", "pA")
-        tt(v("fk3", h), v("ljp", h), F(3), OP.add, h, "fk3", "ljp f", "pA")
-        tt(v("fk0", h), v("lj", h), F(0), OP.add, h, "fk0", "lj f", "pA")
-        ts(v("d0", h), F(0), 3.0, None, OP.add, None, tk("f", h), tk("d0", h), pa)
-        ts(v("d1", h), F(1), 3.0, None, OP.add, None, tk("f", h), tk("d1", h), pa)
-        tt(v("kl", h), v("fk2", h), vb("z", h, 0, 32), OP.min, h, "klt", "fk2 za")
-        tt(v("kr", h), v("fk3", h), vb("z", h, 32, 64), OP.min, h, "krt", "fk3 zb")
-        tt(v("mxu", h), v("fk0", h), KU, OP.max, h, "mxu", "fk0 mkb")
-        tt(v("g1a", h), M, v("d0", h), OP.is_gt, h, "g1a", "mka d0")
-        tt(v("k2", h), v("kl", h), v("kr", h), OP.max, h, "k2", "klt krt")
-        tt(v("sl", h), v("kl", h), v("kr", h), OP.is_gt, h, "sl", "klt krt")
-        tt(v("g1", h), v("g1a", h), v("hasp", h), OP.mult, h, "g1", "g1a hasp")
-        tt(v("b1", h), v("k2", h), v("mxu", h), OP.is_gt, h, "b1", "k2 mxu")
-        tt(v("b2", h), v("k2", h), v("d1", h), OP.is_gt, h, "b2", "k2 d1")
-        tt(v("e1", h), v("sl", h), v("dr", h), OP.mult, h, "e1", "sl dr")
-        tt(v("e2", h), v("sl", h), v("dab", h), OP.mult, h, "e2", "sl dab")
-        tt(v("gs", h), v("g1", h), v("sib", h), OP.mult, h, "gs", "g1 sib")
-        tt(v("bbb", h), v("b1", h), v("b2", h), OP.mult, h, "bbb", "b1 b2")
-        ts(v("m0", h), v("g1", h), -1.0, 1.0, OP.mult, OP.add, tk("g1", h), tk("m0", h))
-        tt(v("e3", h), v("sl", h), v("dz", h), OP.mult, h, "e3", "sl dz")
-        tt(v("go2", h), v("bbb", h), v("gs", h), OP.mult, h, "go2", "bbb gs")
-        tt(v("s2", h, 1, 4), v("s1", h, 2, 4), v("e1", h), OP.add, h, "s2b", "s1c e1")
-        tt(v("s2", h, 2, 4), v("bb", h), v("e2", h), OP.add, h, "s2c", "bb e2")
-        tt(v("s2", h, 3, 4), v("zr1", h), v("e3", h), OP.add, h, "s2d", "zr1 e3")
-        for k in range(4): tt(v("n0", h, k, 4), v("m0", h), pnx(3, h, k, 4), OP.mult, h, "n0" + "abcd"[k], "m0 yd", "pN")
-        tt(v("m1", h), v("g1", h), v("go2", h), OP.subtract, h, "m1", "g1 go2")
-        for k in range(4): tt(v("n2", h, k, 4), v("go2", h), v("s2", h, k, 4), OP.mult, h, "n2" + "abcd"[k], "go2 s2" + "abcd"[k])
-        for k in range(4): tt(v("n1", h, k, 4), v("m1", h), v("s1", h, k, 4), OP.mult, h, "n1" + "abcd"[k], "m1 s1" + "abcd"[k])
-        for j, n in enumerate(("n0", "n2", "n1")):
-            op("P", mm(T["pL%d" % h][:, 128:256], v(n, h), T.idf[:, :], j == 0, j == 2), tk(" ".join(n + x for x in "abcd"), h) + ["idf"],
-               tk("pnn", h), ["pL%d" % h])
-
-    def keep(h):
-        cp(T.ml[:, h * 128:h * 128 + 128], T["pL%d" % h][:, 128:256], tk("pnn", h), tk("ml", h), ["pL%d" % h])
-        cp(T.y[:, h * 128:h * 128 + 128], T["pL%d" % h][:, 128:256], tk("pnn", h), tk("y", h), ["pL%d" % h])
-
-    def m_gather(h, e):
-        if e == "S":
-            op("S", lambda: g.scalar.activation(out=T["mg%d" % h][:, :], in_=T.mwin[:, :].indirect(T.ml[:, h * 128:h * 128 + 128]), func=AF.Copy),
-               ["mwin"] + tk("ml", h), tk("mg", h))
-        else:
-            op("V", lambda: g.vector.tensor_copy(out=T["mg%d" % h][:, :], in_=T.mwin[:, :].indirect(T.ml[:, h * 128:h * 128 + 128])),
-               ["mwin"] + tk("ml", h), tk("mg", h))
-
-    def m_sum(h):
-        op("P", [mm(T["pL%d" % h][:, 256:384], T.idb[:, :], T["mg%d" % h][:, r::16], r == 0, r == 15) for r in range(16)],
-           tk("mg", h) + ["idb"], tk("pms", h), ["pL%d" % h])
-
-    def m_out(h, vis):
-        act(T["ms%d" % vis][:, h * 128:h * 128 + 128], T["pL%d" % h][:, 256:384], AF.Copy, tk("pms", h), ["ms%dh%d" % (vis, h)], ["pL%d" % h])
-
-    def m_send(vis):
-        c = cores[(me - vis) % N]
-        if vis in (1, 2):
-            send(T["ms%d" % vis][:, :], "", [(c, T["rE%d" % vis][:, :])], "aE%d" % vis, ["ms%dh0" % vis, "ms%dh1" % vis])
-        if vis == 3:
-            for h in (0, 1):
-                send(T.ms3[:, h * 128:h * 128 + 128], "", [(c, T.rE3[:, h * 128:h * 128 + 128])], "aE3" + "ab"[h], ["ms3h%d" % h])
-
-    for vis in range(4):
+    def spread(vis):
         b = (me - vis) % N
-        mk = "mk0" if vis == 0 else "rm%d" % b
-        lk = "rl%d" % b
-        op("V", lambda: g.vector.tensor_tensor(out=T.pr[:, :], in0=T.y[:, 0:256].indirect(T[lk][:, 0:64]), in1=T[mk][:, :], op=OP.mult),
-           ["y0", "y1", lk, mk], ["pr"])
-        op("V", lambda: g.vector.tensor_tensor(out=T.a2[:, :], in0=T.pr[:, 0:512], in1=T.pr[:, 512:1024], op=OP.add), ["pr"], ["a2"])
-        for h in (0, 1):
-            op("V", lambda: g.vector.tensor_tensor(out=T.yn[:, h * 128:h * 128 + 128], in0=T.a2[:, h * 128:h * 128 + 128],
-                                                   in1=T.a2[:, 256 + h * 128:384 + h * 128], op=OP.add), ["a2"], ["yn%d" % h])
-        for h in (0, 1):
-            cp(T.cl[:, h * 128:h * 128 + 128], T.yn[:, h * 128:h * 128 + 128], ["yn%d" % h], ["cl%d" % h])
-        for h in (0, 1):
-            op("S", lambda: g.scalar.activation(out=T["gm%d" % h][:, :], in_=T.meta[:, :].indirect(T.cl[:, h * 128:h * 128 + 128]), func=AF.Copy),
-               ["meta", "cl%d" % h], ["gm%d" % h])
-            gather_mul(h, "cl", "cl", vis, "")
-        if vis == 0: dist("ra%d" % ((me + 1) % N), RL, RM)
-        for h in (0, 1):
-            meta_mm(h)
-            dots(h, 0, "ke")
-        for h in (0, 1): s_copies(h)
-        if vis == 0:
-            dist2(RM)
-            spread_g((me - 1) % N, "ax1", range(16))
-            send(T[RM][:, :], RM, [(c, T[RM][:, :]) for c in peers], "aM%d" % me, [RM])
-        if vis > 0:
-            m_gather(0, "S"); m_gather(1, "S")
-        for h in (0, 1):
-            off_a(h); dec1(h)
-        for h in (0, 1):
-            conv(h); gather_mul(h, "l2", "l2", vis, "")
-        for h in (0, 1):
-            dots(h, 128, "f")
-        if vis in (0, 1): spread_g((me - vis - 2) % N, "ax%d" % (vis % 2), range(16))
-        if vis > 0:
-            m_sum(0); m_sum(1)
-        for h in (0, 1): off_b1(h)
-        if vis > 0:
-            m_out(0, vis - 1); m_out(1, vis - 1)
-            m_send(vis - 1)
-        for h in (0, 1):
-            off_b2(h); dec2(h)
-        for h in (0, 1): keep(h)
+        for r in range(16):
+            gsel(A("ax%d" % (vis % 2), S(r, None, 16)), A("ra%d" % b, S(128 * (r // 8), 128 * (r // 8) + 128)), [[0, 128]], 1, 0, OP.is_gt, 0.0)
+    spread(0)
 
-    m_gather(0, "S"); m_gather(1, "V")
-    m_sum(0); m_out(0, 3)
-    for t in range(4): cp(T.wt[:, t * 128 + t:(t + 1) * 128:4], T.b4[:, :], ["b4", "wt"], ["wt%d" % t])
-    cp(T.cf[:, :], T.ml[:, :], ["ml0", "ml1"], ["cf"])
-    m_sum(1); m_out(1, 3); m_send(3)
-    op("V", lambda: g.vector.tensor_tensor(out=T.lby[:, :], in0=T.y[:, :], in1=T.cf[:, :], op=OP.subtract), ["y0", "y1", "cf"], ["lby"])
-    for t in range(4):
-        ts(T.eqt[:, t * 256:t * 256 + 256], T.lby[:, :], (3 - t) / 16.0, None, OP.is_equal, None, ["lby"], ["eqt%d" % t])
-    for t in range(4):
-        op("V", lambda: g.vector.tensor_tensor(out=T.ypt[:, t * 256:t * 256 + 256], in0=T.eqt[:, t * 256:t * 256 + 256], in1=T.cf[:, :], op=OP.mult),
-           ["eqt%d" % t, "cf"], ["ypt%d" % t])
-        op("P", mm(T.pN0[:, 0:256], T.wt[:, t * 128:t * 128 + 128], T.ypt[:, t * 256:t * 256 + 256], t == 0, t == 3), ["wt%d" % t, "ypt%d" % t],
-           ["pyc"], ["pN0"])
-    op("V", lambda: g.vector.tensor_tensor(out=T.acc[:, 0:256], in0=T.ms0[:, :], in1=T.rE1[:, :], op=OP.add), ["ms0h0", "ms0h1", "rE1"], ["acc0"])
-    cp(T.ycs[:, :], T.pN0[:, 0:256], ["pyc"], ["ycs"], ["pN0"])
-    dmag("Y", [(T.yc[:, :], T.ycs[:, :])], "dyc", ["ycs"], ["yc"])
-    op("V", lambda: g.vector.tensor_tensor(out=T.acc[:, 256:512], in0=T.acc[:, 0:256], in1=T.rE2[:, :], op=OP.add), ["acc0", "rE2"], ["acc1"])
+    tag("bytes")
+    SR, AND = OP.arith_shift_right, OP.bitwise_and
+
+    def table(pairs, sem): dma("Y", [(A("meta", rows=S(k, None, 16)), A("db", j)) for k, j in pairs], sem, True)
+    cp(A("db", 1), A("kl")); tt(A("db", 0), A("kl"), A("db", 1), OP.subtract)
+    for j in range(4): cp(A("dp", j), A("db", j % 2, S(j // 2, None, 2)))
+    dma("Y", [(A("cwin", rows=S(8 + j, None, 16)), A("dp", j)) for j in range(4)], "dcw")
+    ms(A("meta"), 0.0)
+    ts(A("db", 8), A("kl"), 0, OP.is_ge)
+    table([(12, 8), (0, 0), (1, 1)], "dm0")
+    ts(A("pn", S(1, 2)), A("pn", S(0, 1)), 15, AND); cp(A("pf"), A("pn", S(1, 2)))
+    act(A("db", 7), A("one"), scale=A("pf"))
+    for b in range(8):
+        cp(A("xk", S(32 * b, 32 * b + 32)), A("ytk", ALL, b))
+    op("V", [lambda: g.vector.transpose(out=T.zk[:, :], in_=T.xk[:, :])], [A("xk")], [A("zk")])
+    for b in range(8):
+        ts(A("lstk", S(b, None, 8)), A("zk", S(32 * b, 32 * b + 32)), 0.5, OP.mult)
+
+    tag("const2")
+    act(A("wi"), A("g16"), scale=A("xv", S(8, 9)))
+    act(A("idb"), A("idf", S(8, 136)))
+    for q in range(4): act(A("sel", q), A("idf"), scale=A("xv", S(9 + q, 10 + q)))
+    cp(A("lku"), A("lki"))
+
+    def choose_a(aw):
+        for k in range(4):
+            tt(A("df", S(256 * k, 256 * k + 256)), IN(A(aw), A("lku", S(16 * k, 16 * k + 16))), A(RA), OP.subtract)
+
+    def choose_p():
+        act(A("dabs"), A("df"), AF.Abs)
+        for q in range(4):
+            mm([(A("pL1", S(256 + 64 * q, 320 + 64 * q)), A("zq", q, S(15 - l, 143 - l)), A("dabs", S(l, None, 16)), l == 0, l == 15) for l in range(16)])
+
+    def choose_b(out):
+        for q in range(4): tt(A("kd", q), A("pL1", S(256 + 64 * q, 320 + 64 * q)), A("lkk"), OP.add)
+        tt(A("km"), A("kd", ALL, S(0, 2)), A("kd", ALL, S(2, 4)), OP.min)
+        tt(A("ki", S(0, 64)), A("km", ALL, 0), A("km", ALL, 1), OP.min)
+        ts(A("ki", S(64, 128)), A("ki", S(0, 64)), 255, AND)
+        cp(A(out), A("ki", S(64, 128)))
+
+    tag("choose0")
+    choose_a("a0b")
+    ms(A("zq"), 0.0)
+    for q in range(4): ts(A("zq", q, S(15, 128, 16)), A("gi"), A("xv", S(9 + q, 10 + q)), OP.mult, 1024.0, OP.mult)
+    tt(A("lkk"), A("lki"), A("kof"), OP.add)
+    choose_p()
+    tag("kk")
+    act(A("kk"), IN(A("cwin"), A("lstk")))
+
+    tag("cut0")
+    ts(A("xh"), A("xc"), 1, SR)
+    for t in range(4): ts(A("xy", t), A("xc", t), (1.5 - t) / 8, OP.add)
+    for k, (i, j) in enumerate(((0, 2), (1, 3), (0, 3), (1, 2))): tt(A("xw", k), A("xh", i), A("xh", j), OP.is_equal)
+    tt(A("xw", 6), A("xy", 2), A("xy", 1), OP.subtract); tt(A("xw", 7), A("xy", 3), A("xy", 1), OP.subtract)
+    tt(A("xw", 4), A("xw", 0), A("xw", 1), OP.max); tt(A("xw", 5), A("xw", 2), A("xw", 3), OP.max)
+    cp(A("xo", 0), A("xy", 0))
+    tt(A("xw", 8), A("xw", 4), A("xw", 6), OP.mult); tt(A("xw", 9), A("xw", 5), A("xw", 7), OP.mult)
+    tt(A("xw", 10), A("xy", 1), A("xw", 8), OP.add)
+    tt(A("xo", 2), A("xy", 2), A("xw", 8), OP.subtract); tt(A("xo", 3), A("xy", 3), A("xw", 9), OP.subtract)
+    tt(A("xo", 1), A("xw", 10), A("xw", 9), OP.add)
+    dma("Y", [(A("y", rows=S(t, None, 4)), A("xo", t)) for t in range(4)], "dy0")
+    tag("bytes")
+    ts(A("di", 0), A("ul"), 1, AND); ts(A("di", 1), A("ul"), 1, SR)
+    cp(A("db", 2), A("di", 0)); cp(A("db", 4), A("di", 1)); tt(A("db", 3), A("di", 1), A("db", 4), OP.subtract)
+    tag("choose0")
+    choose_b("il")
+
+    tag("mask")
+    banks = [A(n + h) for n in ("pK", "pC", "pD") for h in "01"] + [A("pL0"), A("pK0")]
+    for k in range(8):
+        c = S(512 * k, 512 * k + 512)
+        mm([(banks[k], A("wi"), A("meta", c), True, True)])
+        tt(A("swin", c), A("swin", c), banks[k], OP.mult)
+    table([(2, 2), (3, 3), (4, 4), (5, 5), (6, 6), (7, 7), (13, 6), (14, 7)], "dm1")
+    dma("Y", [(A("meta", rows=S(j, None, 16)), A("kk", rows=S(j, None, 16))) for j in range(8, 12)], "dm2", True)
+    dma("Y", [(A("mwin"), H(T.m[:, :]))], "dmm")
+
+    def weights_a():
+        tag("const3")
+        for f in range(4):
+            for t in range(4): act(A("wl", f, ALL, t), A("m32"), scale=A("xv", S(16 + 4 * f + t, 17 + 4 * f + t)))
+        act(A("gh"), A("gi"), scale=0.5)
+        for k in range(8): act(A("wp", ALL, k), A("pt", ALL, S(0, 2)), scale=A("gh", S(k, k + 1)))
+
+    def weights_b():
+        tag("const3")
+        for k, pat in enumerate((P_A, P_B, P_U)): act(A("wz", k), A("pt", ALL, pat), scale=A("xv", S(5 + k, 6 + k)))
+        for f, (pat, j) in enumerate(((P_A, 0), (P_U, 0), (P_T, 1), (P_ID, 2), (P_U, 2), (P_T, 3), (P_T, 4))):
+            act(A("w16", ALL, f), A("pt", ALL, pat), scale=A("xv", S(j, j + 1)))
+        tt(A("wz", 0), A("wz", 0), A("wz", 1), OP.add); tt(A("w16", ALL, 7), A("wz", 0), A("wz", 2), OP.add)
+        for k in range(8): ts(A("wg", ALL, k), A("w16"), A("gi", S(k, k + 1)), OP.mult)
+        ms(A("r4"), 1.0); ms(A("r4", S(0, None, 4)), 0.0)
+        ms(A("r5"), 1.0); ms(A("r5", S(0, None, 5)), 0.0); ms(A("r5", S(3, None, 5)), 0.0)
+        ms(A("kc"), 0.25); ms(A("kc", S(2, None, 5)), 0.5)
+        for h in "01":
+            ms(A("zs" + h), 0.0)
+            ms(A("dn" + h, S(0, None, 4)), 0.0); ms(A("mk" + h, S(0, None, 4)), 0.0); ms(A("dt" + h, S(0, None, 4), 0), 0.0)
+
+    IDF = A("idf", S(8, 136))
+    L3 = S(3, None, 4)
+
+    def X(h, c, n=1): return A("x%d" % h, L3, S(c, c + n) if n > 1 else c)
+
+    def pick(buf, vq): return A(buf, S(32 * vq + 3, 32 * vq + 32, 4))
+
+    def inherit(h, vis):
+        tag("inh%d%d" % (vis, h))
+        lst = "il" if vis == 0 else "ri%d" % ((me - vis) % N)
+        act(A("yg%d" % h), IN(A("y" if vis == 0 else "yw%d" % h), A(lst, S(32 * h, 32 * h + 32))))
+        mm([(A("pL%d" % h, S(0, 128)), A("sel", 2 * h + vq % 2, S(8 - 8 * (vq // 2 - h), 136 - 8 * (vq // 2 - h))),
+             A("yg%d" % h, S(256 * (vq % 2) + 128 * (vq // 2), 256 * (vq % 2) + 128 * (vq // 2) + 128)), vq == 0, vq == 3) for vq in range(4)])
+
+    def lists(h, vis):
+        tag("cl %d%d" % (vis, h))
+        y = A("pL%d" % h, S(0, 128))
+        ts(A("cl%d" % h), y, 0.25, OP.add)
+        ts(A("nr%d" % h), y, RND1, OP.add, -RND1, OP.add)
+        act(A("gm%d" % h), IN(A("meta"), A("cl%d" % h)))
+        tt(A("lam%d" % h), y, A("nr%d" % h), OP.subtract)
+        mm([(A("pK%d" % h), A("lam%d" % h), A("wl"), True, False)])
+
+    def gather1(h, vis):
+        tag("g1 %d%d" % (vis, h))
+        tt(A("p%d" % h), IN(A("swin"), A("cl%d" % h)), A("ax%d" % (vis % 2)), OP.mult)
+
+    def dots1(h, vis):
+        tag("dot1 %d%d" % (vis, h))
+        mm([(A("pK%d" % h, S(0, 2), S(32 * (r // 4), 32 * (r // 4) + 32)), A("p%d" % h, S(r, None, 16)), A("wp", S(2 * (r % 4), 2 * (r % 4) + 2)),
+             False, r == 15) for r in range(16)], True)
+
+    def fields(h, vis, bk):
+        tag("fld%d %d%d" % (bk, vis, h))
+        n = ("pC%d", "pD%d")[bk] % h
+        for vq in range(4):
+            c = S(32 * vq, 32 * vq + 32)
+            mm([(A(n, ALL, c), A("gm%d" % h, S(4 * vq + s, None, 16)), A("wg", S(8 * s + 4 * bk, 8 * s + 4 * bk + 4)), s == 0, False) for s in range(4)]
+               + [(A(n, 3 - 3 * bk, c), A("lam%d" % h), A("wl", bk, S(8 * vq, 8 * vq + 8)), False, True)])
+
+    def decide1(h, vis):
+        tag("d1 %d%d" % (vis, h))
+        x = "x%d" % h; dn = "dn%d" % h; sl = "sl%d" % h
+        scan(A(x, ALL, 0), A("r4"), A("pK%d" % h, 0), OP.max)
+        for t in range(3): tt(A(dn, S(t + 1, None, 4)), A(x, S(t, None, 4), 0), A(x, L3, 0), OP.is_equal)
+        for f in (2, 0, 1): scan(A(sl, ALL, f), A(dn), A("pC%d" % h, f), OP.add)
+        ts(A(sl, L3, 3), A(sl, L3, 2), 1.0, OP.add)
+        scan(A(x, ALL, 1), A(dn), A("pK%d" % h, 1), OP.add)
+        for vq in range(4): cp(A("zl%d" % h, S(vq, None, 4)), pick(sl, vq))
+        mm([(A("pL%d" % h, S(0, 128)), A("zl%d" % h), IDF, True, True)])
+
+    def D(h, k, s): return A("dt%d" % h, S(3 - k, None, 4), s)
+
+    def aside_a(h, vis):
+        tag("offa %d%d" % (vis, h))
+        x = "x%d" % h; dn = A("dn%d" % h); sl = "sl%d" % h
+        for c, f in ((9, 2), (10, 3)): scan(A(x, ALL, c), dn, A("pK%d" % h, f), OP.add)
+        ts(X(h, 6, 2), X(h, 0, 2), RNDH, OP.add, -RNDH, OP.add)
+        tt(X(h, 2), X(h, 9), X(h, 10), OP.max)
+        tt(X(h, 5), X(h, 9), X(h, 10), OP.min)
+        tt(X(h, 4), X(h, 0), X(h, 6), OP.subtract)
+        tt(X(h, 8), X(h, 1), X(h, 7), OP.subtract)
+        tt(X(h, 16), A(sl, L3, 0), X(h, 2), OP.add)
+        tt(X(h, 18, 2), A(sl, L3, S(2, 4)), X(h, 4, 2), OP.add)
+        tt(X(h, 25), X(h, 5), X(h, 4), OP.subtract)
+        tt(X(h, 22), X(h, 2), X(h, 8), OP.max)
+        tt(X(h, 23), X(h, 2), X(h, 8), OP.min)
+        cp(A("dt%d" % h, L3), A("pC%d" % h, 3))
+        tt(X(h, 24), A(sl, L3, 1), X(h, 22), OP.add)
+        tt(X(h, 26), X(h, 23), X(h, 5), OP.subtract)
+        ts(D(h, 3, 1), X(h, 25), 1.0, OP.add)
+        tt(D(h, 2, 0), X(h, 24), X(h, 16), OP.subtract)
+
+    def list2(h, vis):
+        tag("l2 %d%d" % (vis, h))
+        cp(A("l2%d" % h), A("pL%d" % h, S(0, 128)))
+
+    def gather2(h, vis):
+        tag("g2 %d%d" % (vis, h))
+        tt(A("p%d" % h), IN(A("swin"), A("l2%d" % h)), A("ax%d" % (vis % 2)), OP.mult)
+        scan(A("x%d" % h, ALL, 11), A("dn%d" % h), A("pD%d" % h, 3), OP.add)
+        ts(X(h, 3), X(h, 11), 0.0, OP.not_equal, PEN, OP.mult)
+
+    def dots2(h, vis):
+        tag("dot2 %d%d" % (vis, h))
+        k2 = A("pL%d" % h, S(128, 288))
+        mm([(k2, A("idb"), A("kc"), True, False)]
+           + [(A("pL%d" % h, S(129 + 40 * (r // 4) + r % 4, 168 + 40 * (r // 4), 5)), A("p%d" % h, S(r, None, 16)), A("gh"), False, False)
+              for r in range(16)] + [(k2, IDF, X(h, 1, 5), False, True)])
+
+    def aside_b(h, vis):
+        tag("offb %d%d" % (vis, h))
+        tt(X(h, 12), X(h, 11), X(h, 11), OP.mult)
+        for c, f in ((17, 0), (20, 1), (21, 2)): scan(A("x%d" % h, ALL, c), A("dn%d" % h), A("pD%d" % h, f), OP.add)
+        ts(X(h, 13), X(h, 12), 4194304.0, OP.is_gt, -PEN, OP.mult)
+        tt(A("dt%d" % h, S(2, None, 4)), X(h, 16, 4), A("pC%d" % h, 3), OP.subtract)
+        tt(D(h, 2, 1), X(h, 18), X(h, 17), OP.subtract)
+        tt(D(h, 2, 2), X(h, 20), X(h, 25), OP.add)
+        tt(X(h, 14), X(h, 6), X(h, 13), OP.add)
+        tt(D(h, 3, 2), X(h, 21), X(h, 25), OP.subtract)
+        cp(D(h, 3, 3), X(h, 21))
+        tt(D(h, 2, 3), X(h, 20), X(h, 26), OP.add)
+
+    def decide2(h, vis):
+        tag("d2 %d%d" % (vis, h))
+        t5 = "t5%d" % h; mk = "mk%d" % h; st = "st%d" % h; pl = "pL%d" % h
+        scan(A(t5), A("r5"), A(pl, S(128, 288)), OP.max)
+        tt(A(mk, L3), X(h, 14), A(pl, S(129, 288, 5)), OP.is_gt)
+        tt(A(mk, S(1, None, 4)), A(t5, S(3, None, 5)), A(t5, S(4, None, 5)), OP.is_equal)
+        tt(A(mk, S(2, None, 4)), A(t5, S(4, None, 5)), A(t5, S(2, None, 5)), OP.is_gt)
+        for s in range(4): scan(A(st, ALL, s), A(mk), A("dt%d" % h, ALL, s), OP.add)
+        zs = "zs%d" % h
+        for vq in range(4): cp(A(zs, S(2 + vq, 34, 4)), pick(st, vq))
+        mm([(A(pl, S(128 + 128 * h, 256 + 128 * h)), A(zs, S(2, 34)), IDF, True, True)])
+        if vis < 3:
+            mm([(A(pl, S(256 - 128 * h, 384 - 128 * h)), A(zs, S(4 - 4 * h, 36 - 4 * h)), IDF, True, True)])
+            act(A("yw%d" % h), A(pl, S(128, 384)))
+
+    def keep(h, vis):
+        tag("keep%d%d" % (vis, h))
+        ts(A("ml%d" % h), A("pL%d" % h, S(128 + 128 * h, 256 + 128 * h)), 0.25, OP.add)
+
+    def m_gather(h, vis, split=False):
+        tag("mg %d%d" % (vis, h))
+        if split:
+            act(A("mg%d" % h, S(0, 1024)), IN(A("mwin"), A("ml%d" % h, S(0, 64))))
+            cp(A("mg%d" % h, S(1024, 2048)), IN(A("mwin"), A("ml%d" % h, S(64, 128))))
+        else: act(A("mg%d" % h), IN(A("mwin"), A("ml%d" % h)))
+
+    def m_sum(hs, k, pb):
+        tag("msum%d" % k)
+        for vh in range(2):
+            rs = [(h, r) for h in hs for r in range(8 * vh, 8 * vh + 8)]
+            mm([(A(pb, vh), A("idb"), A("mg%d" % h, S(r, None, 16)), i == 0, i == len(rs) - 1) for i, (h, r) in enumerate(rs)])
+
+    def m_out(k, pb):
+        tag("mout%d" % k)
+        act(A("ms%d" % k), A(pb, S(0, 2)))
+        if k: send(A("ms%d" % k), A("rE%d" % k), [cores[(me - min(k, 3)) % N]], "aE%d" % k)
+
+    def places(h):
+        tag("plc%d" % h)
+        so = "so%d" % h; sl = "sl%d" % h; y = A("st%d" % h, L3)
+        ts(A(so, 0), y, RND1, OP.add, -RND1, OP.add)
+        tt(A(so, 1), y, A(so, 0), OP.subtract)
+        ts(A(so, 1), A(so, 1), 32768.0, OP.mult)
+        tt(A(so, 2), A(so, 1), A(so, 0), OP.add)
+
+        def w(k, s): return A(so, k, S(s, None, 4))
+        for i in (0, 2):
+            tt(w(3, i), w(2, i), w(2, i + 1), OP.max); tt(w(3, i + 1), w(2, i), w(2, i + 1), OP.min)
+        tt(A(sl, L3, 0), w(3, 0), w(3, 2), OP.max); tt(w(0, 0), w(3, 0), w(3, 2), OP.min)
+        tt(w(0, 1), w(3, 1), w(3, 3), OP.max); tt(A(sl, L3, 3), w(3, 1), w(3, 3), OP.min)
+        tt(A(sl, L3, 1), w(0, 0), w(0, 1), OP.max); tt(A(sl, L3, 2), w(0, 0), w(0, 1), OP.min)
+        for vq in range(4): cp(A("zp%d" % (vq // 2), S(2 * h + vq % 2, None, 4)), pick(sl, vq))
+
+    steps = [(h, vis) for vis in range(4) for h in (0, 1)]
+    inherit(0, 0); weights_a(); inherit(1, 0)
+    lists(0, 0)
+    for i in range(9):
+        now = steps[i] if i < 8 else None
+        old = steps[i - 1] if i > 0 else None
+        nxt = steps[i + 1] if i < 7 else None
+        if now:
+            gather1(*now)
+            if i == 0:
+                weights_b(); tag("choose1"); choose_a("ra%d" % ((me + 1) % N))
+            fields(*now, 0)
+        if i == 8: places(0)
+        if old: dots2(*old)
+        if now: dots1(*now)
+        if i == 8:
+            m_sum((0,), 3, "pD0"); m_out(3, "pD0")
+        if old:
+            aside_b(*old); decide2(*old)
+        if now: decide1(*now)
+        if i == 0:
+            tag("choose1"); choose_p()
+        if old and nxt: inherit(*nxt)
+        if now:
+            fields(*now, 1); aside_a(*now); list2(*now)
+        if i == 0:
+            tag("choose1"); choose_b("ri%d" % me)
+            send(A("ri%d" % me), A("ri%d" % me), peers, "aI%d" % me)
+            spread(1)
+        if old: keep(*old)
+        if nxt: lists(*nxt)
+        if i >= 3 and i % 2 == 1: m_sum((0, 1), (i - 3) // 2, "pD0")
+        if old and i < 8: m_gather(*old)
+        if i >= 3 and i % 2 == 1: m_out((i - 3) // 2, "pD0")
+        if now: gather2(*now)
+        if i in (1, 3): spread((i + 3) // 2)
+    m_gather(1, 3, True)
+    m_sum((1,), 4, "pD1"); m_out(4, "pD1")
+    places(1)
+    tag("out")
+    for vh in range(2): mm([(A("pK0", vh), A("zp%d" % vh), IDF, True, True)])
+    act(A("ycs"), A("pK0", S(0, 2)), AF.Identity, A("xv", S(13, 14)))
+    dma("Y", [(H(T.yc[:, :]), A("ycs"))], "dyc")
+    tt(A("acc"), A("ms0"), A("rE1"), OP.add)
+    for k in (2, 3): tt(A("acc"), A("acc"), A("rE%d" % k), OP.add)
     for h in (0, 1):
-        c = slice(h * 128, h * 128 + 128)
-        op("V", lambda: g.vector.tensor_tensor(out=T.fin[:, c], in0=T.acc[:, 256 + h * 128:384 + h * 128], in1=T.rE3[:, c], op=OP.add),
-           ["acc1", "rE3h%d" % h], ["fin%d" % h])
-        op("V", lambda: g.vector.tensor_tensor(out=T.yes[:, c], in0=T.fin[:, c], in1=T[RA][:, c], op=OP.mult), ["fin%d" % h, RA], ["yes%d" % h])
-        dmag("Y", [(T.ye[:, c], T.yes[:, c])], "dye%d" % h, ["yes%d" % h], ["ye%d" % h])
+        c = S(h * 128, h * 128 + 128)
+        tt(A("acc", c), A("acc", c), A("rE4", c), OP.add)
+        tt(A("yes", c), A("acc", c), A(RA, c), OP.mult)
+        dma("Y", [(H(T.ye[:, c]), A("yes", c))], "dye%d" % h)
 
     need("G", [(s, cnt[s]) for s in cnt])

@@ -7,12 +7,13 @@ AF = ActivationFunctionType
 RND1 = 12582912.0
 RNDH = 6291456.0
 PEN = 2097152.0
+SPLIT = 88
 TAG = [""]
 
 F32, B16, I32, U16 = "float32", "bfloat16", "int32", "uint16"
-NXV = 32
+NXV = 36
 SCRATCH = {
-    "kl": ("sbuf", [128, 256], I32), "ul": ("sbuf", [128, 256], I32), "pn": ("sbuf", [128, 2], I32), "pf": ("sbuf", [128, 1], F32),
+    "kl": ("sbuf", [128, 256], I32), "ul": ("sbuf", [128, 256], I32),
     "ytk": ("sbuf", [128, 2, 8, 16], I32), "xk": ("sbuf", [128, 256], F32), "zk": ("sbuf", [128, 256], F32),
     "lstk": ("sbuf", [128, 256], U16),
     "di": ("sbuf", [128, 2, 256], I32), "db": ("sbuf", [128, 9, 256], B16), "dp": ("sbuf", [128, 4, 128], B16),
@@ -26,18 +27,19 @@ SCRATCH = {
     "xc": ("sbuf", [128, 4, 64], I32), "xh": ("sbuf", [128, 4, 64], I32), "xy": ("sbuf", [128, 4, 64], F32),
     "xw": ("sbuf", [128, 11, 64], F32), "xo": ("sbuf", [128, 4, 64], F32), "y": ("sbuf", [128, 256], F32),
     "one": ("sbuf", [128, 256], F32), "idf": ("sbuf", [128, 144], F32), "idb": ("sbuf", [128, 128], B16),
-    "gi": ("sbuf", [128, 8], F32), "gh": ("sbuf", [128, 8], F32), "m32": ("sbuf", [128, 32], F32), "g16": ("sbuf", [128, 128], F32),
-    "cf": ("sbuf", [128, 16 * NXV], F32), "xv": ("sbuf", [128, NXV], F32), "pt": ("sbuf", [128, 4, 5, 4], F32),
+    "gi": ("sbuf", [128, 8], F32), "gh": ("sbuf", [128, 8], F32), "m32": ("sbuf", [128, 32], F32),
+    "cf": ("sbuf", [128, 16, NXV], F32), "xv": ("sbuf", [128, NXV], F32), "rl": ("sbuf", [128, 64], U16),
     "w16": ("sbuf", [128, 4, 8, 4], F32), "wz": ("sbuf", [128, 3, 16], F32),
-    "wg": ("sbuf", [128, 32, 8, 4], B16), "wl": ("sbuf", [128, 4, 32, 4], B16), "wp": ("sbuf", [128, 8, 8, 4], F32),
+    "wg": ("sbuf", [128, 32, 8, 4], B16), "wl": ("sbuf", [128, 5, 32, 4], B16), "wp": ("sbuf", [128, 8, 8, 4], F32),
     "sel": ("sbuf", [128, 4, 144], F32), "zq": ("sbuf", [128, 4, 144], B16), "wi": ("sbuf", [128, 128], B16),
+    "inn": ("sbuf", [128, 4096], B16), "hb": ("sbuf", [128, 16], F32), "pn": ("sbuf", [128, 3], I32), "pf": ("sbuf", [128, 3], F32), "nb": ("sbuf", [128, 3, 256], B16),
     "r4": ("sbuf", [128, 128], F32), "r5": ("sbuf", [128, 160], F32), "kc": ("sbuf", [128, 160], B16),
     "ycs": ("sbuf", [128, 256], F32), "acc": ("sbuf", [128, 256], F32), "yes": ("sbuf", [128, 256], F32),
 }
 for _h in "01":
     for _n, _s, _d in (("yw", [256], F32), ("yg", [512], F32), ("cl", [128], U16), ("l2", [128], U16), ("ml", [128], U16), ("nr", [128], F32),
                        ("lam", [128], B16), ("p", [2048], F32), ("gm", [2048], B16), ("mg", [2048], B16), ("x", [128, 28], F32),
-                       ("dn", [128], F32), ("mk", [128], F32), ("sl", [128, 4], F32), ("st", [128, 4], F32), ("zl", [32, 4], F32),
+                       ("dn", [128], F32), ("mk", [128], F32), ("sl", [128, 10], F32), ("st", [128, 4], F32), ("zl", [32, 4], F32),
                        ("zs", [36, 4], F32), ("zp", [32, 4], F32), ("dt", [128, 4], F32), ("t5", [160], F32), ("so", [4, 128], F32)):
         SCRATCH[_n + _h] = ("sbuf", [128] + _s, _d)
     for _n in ("pK", "pC", "pD"): SCRATCH[_n + _h] = ("psum", [128, 4, 128], F32)
@@ -45,12 +47,12 @@ for _h in "01":
 for _k in range(4):
     SCRATCH["ra%d" % _k] = ("sbuf", [128, 256], B16)
     SCRATCH["ri%d" % _k] = ("sbuf", [128, 64], U16)
-for _k in range(5):
-    SCRATCH["ms%d" % _k] = ("sbuf", [128, 256], F32)
-    if _k: SCRATCH["rE%d" % _k] = ("sbuf", [128, 256], F32)
+for _k in range(4):
+    SCRATCH["ms%d" % _k] = ("sbuf", [128, 256], F32 if _k < 3 else U16)
+    if _k: SCRATCH["rE%d" % _k] = ("sbuf", [128, 256], F32 if _k < 3 else U16)
 
 _DS = ["dk", "du", "da", "dl", "da0", "dyk", "dxc", "dss", "dmm", "dxv", "dcw", "dm0", "dm1", "dm2", "dm3", "dy0", "dyc", "dye0", "dye1"]
-SEMAPHORES = ["sv", "ss", "sp", "sg", "rl"] + _DS + ["aA%d" % k for k in range(4)] + ["aI%d" % k for k in range(4)] + ["aE%d" % k for k in range(1, 5)]
+SEMAPHORES = ["sv", "ss", "sp", "sg", "rl", "aL"] + _DS + ["aA%d" % k for k in range(4)] + ["aI%d" % k for k in range(4)] + ["aE%d" % k for k in range(1, 4)]
 
 ALL = slice(None)
 
@@ -66,11 +68,11 @@ def telescoped(slot_of):
     return [(s, t, c) for (s, t), c in sorted(w.items()) if c]
 
 
-PATTERNS = [[(t, t, 1) for t in range(4)], telescoped(lambda t: t ^ 1), telescoped(lambda t: 2 - (t & 2)), telescoped(lambda t: 3 - (t & 2)),
-            telescoped(lambda t: t)]
-P_ID, P_U, P_A, P_B, P_T = range(5)
+PATTERNS = [telescoped(lambda t: t), [(t, t, 1) for t in range(4)], telescoped(lambda t: t ^ 1), telescoped(lambda t: 2 - (t & 2)),
+            telescoped(lambda t: 3 - (t & 2))]
+P_T, P_ID, P_U, P_A, P_B = range(5)
 KID = {0: 1.0, 1: 1.0}; UP = {2: 1.0, 3: 2.0, 4: 2.0}; UPP = {3: 1.0, 4: 1.0}; NODE = {5: 1.0, 6: 2.0, 7: 256.0}; NP = {6: 1.0, 7: 128.0}
-KKL = {8: 1.0, 9: 1.0}; KKR = {10: 1.0, 11: 1.0}; NP2 = {13: 1.0, 14: 128.0}
+KKL = {8: 1.0, 9: 1.0}; KKR = {10: 1.0, 11: 1.0}; NP2 = {14: 1.0, 15: 128.0}
 
 
 def lin(*terms):
@@ -80,7 +82,7 @@ def lin(*terms):
     return d
 
 
-VALUES = [UP, KID, NODE, lin((1, KKR), (-1, KID)), lin((1, KKL), (-1, KKR)), lin((4096, NP2), (1, UPP)), lin((-4096, NP2)), lin((-1, NP)), {12: 1.0}]
+VALUES = [UP, KID, NODE, lin((1, KKR), (-1, KID)), lin((1, KKL), (-1, KKR)), lin((4096, NP2), (1, UPP)), lin((-4096, NP2)), lin((-1, NP))]
 
 
 def rank_program(g, core, T, topo):
@@ -121,7 +123,7 @@ def rank_program(g, core, T, topo):
             evs += [ev for m2, k2, ev in wr.get(n, []) if m & m2]
         for n, m in w:
             evs += [ev for m2, k2, ev in wr.get(n, []) if m & m2 and not (acc and k2[:len(key)] == key)]
-            evs += [ev for (k2, m2), ev in rd.get(n, {}).items() if m & m2 and k2 != key]
+            evs += [ev for (k2, m2), ev in rd.get(n, {}).items() if m & m2]
         for n, m in r + w:
             evs += [ev for k2, ev in bank.get(n, {}).items() if k2 != key]
         need(e, evs)
@@ -202,8 +204,9 @@ def rank_program(g, core, T, topo):
     for k in range(N):
         if k != me:
             wr["ra%d" % k] = [(A("ra%d" % k)[1][0][1], "far", ("aA%d" % k, ne))]
-            wr["ri%d" % k] = [(A("ri%d" % k)[1][0][1], "far", ("aI%d" % k, ne))]
-    for k in range(1, 5): wr["rE%d" % k] = [(A("rE%d" % k)[1][0][1], "far", ("aE%d" % k, ne))]
+            if k != (me - 1) % N: wr["ri%d" % k] = [(A("ri%d" % k)[1][0][1], "far", ("aI%d" % k, ne))]
+    wr["rl"] = [(A("rl")[1][0][1], "far", ("aL", ne))]
+    for k in range(1, 4): wr["rE%d" % k] = [(A("rE%d" % k)[1][0][1], "far", ("aE%d" % k, ne))]
 
     tag("load")
     dma("Y", [(A("kl"), H(T.kid[:, :]))], "dk")
@@ -211,34 +214,39 @@ def rank_program(g, core, T, topo):
     dma("Y", [(A("ytk", k), H(T.kid[k::2, :])) for k in (0, 1)], "dyk")
     dma("S", [(A("lki"), H(T.lk[:, :]))], "dl")
     dma("S", [(A("a0b"), H(T.a0[:, :]))], "da0")
-    dma("Y", [(A("ul"), H(T.up[:, :]))], "du")
-    dma("S", [(A("xc", t), H(T.cut0[t::4, :])) for t in range(4)], "dxc")
 
     tag("const")
-    ms(A("one"), 1.0); ms(A("cf"), 0.0); ms(A("pt"), 0.0)
-    for j, rows in enumerate(VALUES):
-        for k, w in rows.items(): ms(A("cf", S(k * NXV + j, k * NXV + j + 1)), w)
-    for q in range(4):
-        fill(A("cf", S(4 * q * NXV + 9 + q, (4 * q + 4) * NXV, NXV)), 1.0)
-        fill(A("cf", S(q * NXV + 13, None, 4 * NXV)), -32768.0 * (1.5 - q) / 8)
-    for f in range(4):
-        for s, t, c in PATTERNS[f]: fill(A("cf", S(s * NXV + 16 + 4 * f + t, None, 4 * NXV)), c)
-    dma("Y", [(A("xv"), A("cf", rows=S(0, 8)))], "dxv")
-    dma("Y", [(A("swin"), H(T.s[:, :]))], "dss")
-    ms(A("cwin"), 0.0)
     iota(A("pn", S(0, 1)), [[0, 1]], 0, 1, False)
+    iota(A("db", 5), [[0, 128], [1, 2]], 0, 0); iota(A("db", 6), [[1, 128], [0, 2]], 0, 0)
+    ms(A("one"), 1.0); ms(A("cf"), 0.0)
+    ts(A("pn", S(1, 2)), A("pn", S(0, 1)), 15, OP.bitwise_and); ts(A("pn", S(2, 3)), A("pn", S(0, 1)), 7, OP.bitwise_and)
+    for j, rows in enumerate(VALUES):
+        for k, w in rows.items(): ms(A("cf", k, S(j, j + 1)), w)
+    for q in range(4):
+        ms(A("cf", S(4 * q, 4 * q + 4), 9 + q), 1.0)
+        fill(A("cf", S(q, None, 4), 13), -32768.0 * (1.5 - q) / 8)
+    for f in range(5):
+        for s, t, c in PATTERNS[f]: fill(A("cf", S(s, None, 4), 16 + 4 * f + t), c)
+
+    def pt(f, n=1): return A("cf", S(0, 4), S(16 + 4 * f, 16 + 4 * (f + n)))
+    dma("Y", [(A("xv"), A("cf", rows=S(0, 8)))], "dxv")
+    dma("S", [(A("xc", t), H(T.cut0[t::4, :])) for t in range(4)], "dxc")
+    dma("Y", [(A("ul"), H(T.up[:, :]))], "du")
+    iota(A("hb"), [[1, 16]], 0, 0)
+    for j, (c, k) in enumerate(((1, 5), (2, 6), (2, 7))): ts(A("pf", S(j, j + 1)), A("pn", S(c, c + 1)), k, OP.is_equal)
+    act(A("nb", 0), A("db", 5), scale=A("pf", S(0, 1))); act(A("nb", 1), A("db", 6), scale=A("pf", S(1, 2)))
+    act(A("hb"), A("hb"), scale=A("pf", S(2, 3)))
+    ms(A("cwin"), 0.0); ms(A("zq"), 0.0)
+    tt(A("nb", 2), A("nb", 0), A("nb", 1), OP.add)
     gsel(A("gi"), A("one", S(0, 8)), [[-16, 8]], 0, 1, OP.is_ge, 0.0)
     gsel(A("gi"), A("gi"), [[16, 8]], 15, -1, OP.is_ge, 0.0)
-    iota(A("db", 5), [[0, 128], [1, 2]], 0, 0); iota(A("db", 6), [[1, 128], [0, 2]], 0, 0)
     iota(A("kof"), [[256, 4], [0, 16]], 0, 0)
-    send(A(RA), A(RA), peers, "aA%d" % me)
     gsel(A("idf"), A("one", S(0, 144)), [[-1, 144]], 8, 1, OP.is_equal, 0.0)
-    gsel(A("g16"), A("one", S(0, 128)), [[-16, 8], [0, 16]], 0, 1, OP.is_ge, 0.0)
-    gsel(A("g16"), A("g16"), [[16, 8], [0, 16]], 15, -1, OP.is_ge, 0.0)
+    gsel(A("wi"), A("one", S(0, 128)), [[-1, 8], [0, 16]], 0, 1, OP.is_equal, 0.0)
     gsel(A("m32"), A("one", S(0, 32)), [[-4, 4], [-16, 8]], 0, 1, OP.is_ge, 0.0)
     gsel(A("m32"), A("m32"), [[4, 4], [16, 8]], 3, -1, OP.is_ge, 0.0)
-    for f in range(5):
-        for s, t, c in PATTERNS[f]: fill(A("pt", s, f, S(t, t + 1)), c)
+    tag("static")
+    for k in range(16): act(A("meta", S(256 * k, 256 * k + 256)), A("nb", 2), AF.Identity, A("hb", S(k, k + 1)))
 
     def spread(vis):
         b = (me - vis) % N
@@ -253,47 +261,48 @@ def rank_program(g, core, T, topo):
     cp(A("db", 1), A("kl")); tt(A("db", 0), A("kl"), A("db", 1), OP.subtract)
     for j in range(4): cp(A("dp", j), A("db", j % 2, S(j // 2, None, 2)))
     dma("Y", [(A("cwin", rows=S(8 + j, None, 16)), A("dp", j)) for j in range(4)], "dcw")
-    ms(A("meta"), 0.0)
     ts(A("db", 8), A("kl"), 0, OP.is_ge)
-    table([(12, 8), (0, 0), (1, 1)], "dm0")
-    ts(A("pn", S(1, 2)), A("pn", S(0, 1)), 15, AND); cp(A("pf"), A("pn", S(1, 2)))
-    act(A("db", 7), A("one"), scale=A("pf"))
-    for b in range(8):
-        cp(A("xk", S(32 * b, 32 * b + 32)), A("ytk", ALL, b))
-    op("V", [lambda: g.vector.transpose(out=T.zk[:, :], in_=T.xk[:, :])], [A("xk")], [A("zk")])
-    for b in range(8):
-        ts(A("lstk", S(b, None, 8)), A("zk", S(32 * b, 32 * b + 32)), 0.5, OP.mult)
-
-    tag("const2")
-    act(A("wi"), A("g16"), scale=A("xv", S(8, 9)))
-    act(A("idb"), A("idf", S(8, 136)))
-    for q in range(4): act(A("sel", q), A("idf"), scale=A("xv", S(9 + q, 10 + q)))
+    dma("Y", [(A("inn", rows=S(0, 8)), A("db", 8))], "dm0")
+    dma("Y", [(A("swin", S(0, 2048)), H(T.s[:, 0:2048]))], "dss")
     cp(A("lku"), A("lki"))
+    send(A(RA), A(RA), peers, "aA%d" % me)
+    send(A("lku"), A("rl"), [cores[(me + 1) % N]], "aL")
+    gsel(A("r4"), A("one", S(0, 128)), [[0, 32], [1, 4]], 0, 0, OP.is_gt, 0.0)
+    gsel(A("r5"), A("one", S(0, 160)), [[0, 32], [1, 5]], 0, 0, OP.is_gt, 0.0)
+    gsel(A("r5"), A("r5"), [[0, 32], [1, 5]], -3, 0, OP.not_equal, 0.0)
+    for h in "01":
+        iota(A("zs" + h), [[0, 144]], 0, 0)
+        for o in (A("dn" + h, S(0, None, 4)), A("mk" + h, S(0, None, 4)), A("dt" + h, S(0, None, 4), 0)): iota(o, [[0, 32]], 0, 0)
 
-    def choose_a(aw):
+    def choose_a(kept, lk, a):
         for k in range(4):
-            tt(A("df", S(256 * k, 256 * k + 256)), IN(A(aw), A("lku", S(16 * k, 16 * k + 16))), A(RA), OP.subtract)
+            tt(A("df", S(256 * k, 256 * k + 256)), IN(A(kept), A(lk, S(16 * k, 16 * k + 16))), A(a), OP.subtract)
 
     def choose_p():
         act(A("dabs"), A("df"), AF.Abs)
         for q in range(4):
-            mm([(A("pL1", S(256 + 64 * q, 320 + 64 * q)), A("zq", q, S(15 - l, 143 - l)), A("dabs", S(l, None, 16)), l == 0, l == 15) for l in range(16)])
+            mm([(A("pK0", q, S(0, 64)), A("zq", q, S(15 - l, 143 - l)), A("dabs", S(l, None, 16)), l == 0, l == 15) for l in range(16)])
 
     def choose_b(out):
-        for q in range(4): tt(A("kd", q), A("pL1", S(256 + 64 * q, 320 + 64 * q)), A("lkk"), OP.add)
+        for q in range(4): tt(A("kd", q), A("pK0", q, S(0, 64)), A("lkk"), OP.add)
         tt(A("km"), A("kd", ALL, S(0, 2)), A("kd", ALL, S(2, 4)), OP.min)
         tt(A("ki", S(0, 64)), A("km", ALL, 0), A("km", ALL, 1), OP.min)
         ts(A("ki", S(64, 128)), A("ki", S(0, 64)), 255, AND)
         cp(A(out), A("ki", S(64, 128)))
 
     tag("choose0")
-    choose_a("a0b")
-    ms(A("zq"), 0.0)
+    choose_a("a0b", "lku", RA)
     for q in range(4): ts(A("zq", q, S(15, 128, 16)), A("gi"), A("xv", S(9 + q, 10 + q)), OP.mult, 1024.0, OP.mult)
-    tt(A("lkk"), A("lki"), A("kof"), OP.add)
     choose_p()
+    tag("lstk")
+    for b in range(8):
+        cp(A("xk", S(32 * b, 32 * b + 32)), A("ytk", ALL, b))
+    op("V", [lambda: g.vector.transpose(out=T.zk[:, :], in_=T.xk[:, :])], [A("xk")], [A("zk")])
+    for b in range(8):
+        ts(A("lstk", S(b, None, 8)), A("zk", S(32 * b, 32 * b + 32)), 0.5, OP.mult)
     tag("kk")
     act(A("kk"), IN(A("cwin"), A("lstk")))
+    tt(A("lkk"), A("lki"), A("kof"), OP.add)
 
     tag("cut0")
     ts(A("xh"), A("xc"), 1, SR)
@@ -307,49 +316,46 @@ def rank_program(g, core, T, topo):
     tt(A("xo", 2), A("xy", 2), A("xw", 8), OP.subtract); tt(A("xo", 3), A("xy", 3), A("xw", 9), OP.subtract)
     tt(A("xo", 1), A("xw", 10), A("xw", 9), OP.add)
     dma("Y", [(A("y", rows=S(t, None, 4)), A("xo", t)) for t in range(4)], "dy0")
+    dma("Y", [(A("swin", S(2048, 4096)), H(T.s[:, 2048:4096]))], "dm3")
     tag("bytes")
     ts(A("di", 0), A("ul"), 1, AND); ts(A("di", 1), A("ul"), 1, SR)
     cp(A("db", 2), A("di", 0)); cp(A("db", 4), A("di", 1)); tt(A("db", 3), A("di", 1), A("db", 4), OP.subtract)
+    table([(j, j) for j in range(5)], "dm1")
     tag("choose0")
     choose_b("il")
+    for f, (pat, j) in enumerate(((P_A, 0), (P_U, 0), (P_T, 1), (P_ID, 2), (P_U, 2), (P_T, 3), (P_T, 4))):
+        ts(A("w16", ALL, f), pt(pat), A("xv", S(j, j + 1)), OP.mult)
+    for k, pat in enumerate((P_A, P_B, P_U)): ts(A("wz", k), pt(pat), A("xv", S(5 + k, 6 + k)), OP.mult)
+    tt(A("wz", 0), A("wz", 0), A("wz", 1), OP.add); tt(A("w16", ALL, 7), A("wz", 0), A("wz", 2), OP.add)
+    for q in range(4): act(A("sel", q), A("idf"), scale=A("xv", S(9 + q, 10 + q)))
 
     tag("mask")
-    banks = [A(n + h) for n in ("pK", "pC", "pD") for h in "01"] + [A("pL0"), A("pK0")]
+    banks = [A(n + h) for n in ("pK", "pC", "pD") for h in "10"] + [A("pK1"), A("pK0")]
     for k in range(8):
         c = S(512 * k, 512 * k + 512)
-        mm([(banks[k], A("wi"), A("meta", c), True, True)])
+        mm([(banks[k], A("wi", rows=S(0, 8)), A("inn", c, rows=S(0, 8)), True, True)])
         tt(A("swin", c), A("swin", c), banks[k], OP.mult)
-    table([(2, 2), (3, 3), (4, 4), (5, 5), (6, 6), (7, 7), (13, 6), (14, 7)], "dm1")
     dma("Y", [(A("meta", rows=S(j, None, 16)), A("kk", rows=S(j, None, 16))) for j in range(8, 12)], "dm2", True)
     dma("Y", [(A("mwin"), H(T.m[:, :]))], "dmm")
 
     def weights_a():
         tag("const3")
-        for f in range(4):
+        for f in range(5):
             for t in range(4): act(A("wl", f, ALL, t), A("m32"), scale=A("xv", S(16 + 4 * f + t, 17 + 4 * f + t)))
         act(A("gh"), A("gi"), scale=0.5)
-        for k in range(8): act(A("wp", ALL, k), A("pt", ALL, S(0, 2)), scale=A("gh", S(k, k + 1)))
+        for k in range(8): act(A("wp", ALL, k), pt(P_ID, 2), scale=A("gh", S(k, k + 1)))
+        for k in range(8): act(A("wg", ALL, k), A("w16"), scale=A("gi", S(k, k + 1)))
 
     def weights_b():
-        tag("const3")
-        for k, pat in enumerate((P_A, P_B, P_U)): act(A("wz", k), A("pt", ALL, pat), scale=A("xv", S(5 + k, 6 + k)))
-        for f, (pat, j) in enumerate(((P_A, 0), (P_U, 0), (P_T, 1), (P_ID, 2), (P_U, 2), (P_T, 3), (P_T, 4))):
-            act(A("w16", ALL, f), A("pt", ALL, pat), scale=A("xv", S(j, j + 1)))
-        tt(A("wz", 0), A("wz", 0), A("wz", 1), OP.add); tt(A("w16", ALL, 7), A("wz", 0), A("wz", 2), OP.add)
-        for k in range(8): ts(A("wg", ALL, k), A("w16"), A("gi", S(k, k + 1)), OP.mult)
-        ms(A("r4"), 1.0); ms(A("r4", S(0, None, 4)), 0.0)
-        ms(A("r5"), 1.0); ms(A("r5", S(0, None, 5)), 0.0); ms(A("r5", S(3, None, 5)), 0.0)
-        ms(A("kc"), 0.25); ms(A("kc", S(2, None, 5)), 0.5)
-        for h in "01":
-            ms(A("zs" + h), 0.0)
-            ms(A("dn" + h, S(0, None, 4)), 0.0); ms(A("mk" + h, S(0, None, 4)), 0.0); ms(A("dt" + h, S(0, None, 4), 0), 0.0)
+        act(A("idb"), A("idf", S(8, 136)))
+        fill(A("kc"), 0.25); fill(A("kc", S(2, None, 5)), 0.5)
 
     IDF = A("idf", S(8, 136))
     L3 = S(3, None, 4)
 
     def X(h, c, n=1): return A("x%d" % h, L3, S(c, c + n) if n > 1 else c)
 
-    def pick(buf, vq): return A(buf, S(32 * vq + 3, 32 * vq + 32, 4))
+    def pick(buf, vq, c=0): return A(buf, S(32 * vq + 3, 32 * vq + 32, 4), S(c, c + 4))
 
     def inherit(h, vis):
         tag("inh%d%d" % (vis, h))
@@ -361,11 +367,13 @@ def rank_program(g, core, T, topo):
     def lists(h, vis):
         tag("cl %d%d" % (vis, h))
         y = A("pL%d" % h, S(0, 128))
+        if vis:
+            act(A("nr%d" % h), y, AF.Identity, RND1); act(A("nr%d" % h), A("nr%d" % h), AF.Identity, -RND1)
         ts(A("cl%d" % h), y, 0.25, OP.add)
-        ts(A("nr%d" % h), y, RND1, OP.add, -RND1, OP.add)
+        if not vis: ts(A("nr%d" % h), y, RND1, OP.add, -RND1, OP.add)
         act(A("gm%d" % h), IN(A("meta"), A("cl%d" % h)))
         tt(A("lam%d" % h), y, A("nr%d" % h), OP.subtract)
-        mm([(A("pK%d" % h), A("lam%d" % h), A("wl"), True, False)])
+        mm([(A("pK%d" % h), A("lam%d" % h), A("wl", S(P_ID, P_ID + 4)), True, False)])
 
     def gather1(h, vis):
         tag("g1 %d%d" % (vis, h))
@@ -376,71 +384,78 @@ def rank_program(g, core, T, topo):
         mm([(A("pK%d" % h, S(0, 2), S(32 * (r // 4), 32 * (r // 4) + 32)), A("p%d" % h, S(r, None, 16)), A("wp", S(2 * (r % 4), 2 * (r % 4) + 2)),
              False, r == 15) for r in range(16)], True)
 
-    def fields(h, vis, bk):
+    def fields(h, vis, bk, vqs=range(4)):
         tag("fld%d %d%d" % (bk, vis, h))
         n = ("pC%d", "pD%d")[bk] % h
-        for vq in range(4):
+        for vq in vqs:
             c = S(32 * vq, 32 * vq + 32)
             mm([(A(n, ALL, c), A("gm%d" % h, S(4 * vq + s, None, 16)), A("wg", S(8 * s + 4 * bk, 8 * s + 4 * bk + 4)), s == 0, False) for s in range(4)]
-               + [(A(n, 3 - 3 * bk, c), A("lam%d" % h), A("wl", bk, S(8 * vq, 8 * vq + 8)), False, True)])
+               + [(A(n, (S(2, 4), 0)[bk], c), A("lam%d" % h), A("wl", (S(P_T, P_ID + 1), P_U)[bk], S(8 * vq, 8 * vq + 8)), False, True)])
 
     def decide1(h, vis):
         tag("d1 %d%d" % (vis, h))
         x = "x%d" % h; dn = "dn%d" % h; sl = "sl%d" % h
         scan(A(x, ALL, 0), A("r4"), A("pK%d" % h, 0), OP.max)
         for t in range(3): tt(A(dn, S(t + 1, None, 4)), A(x, S(t, None, 4), 0), A(x, L3, 0), OP.is_equal)
-        for f in (2, 0, 1): scan(A(sl, ALL, f), A(dn), A("pC%d" % h, f), OP.add)
-        ts(A(sl, L3, 3), A(sl, L3, 2), 1.0, OP.add)
-        scan(A(x, ALL, 1), A(dn), A("pK%d" % h, 1), OP.add)
-        for vq in range(4): cp(A("zl%d" % h, S(vq, None, 4)), pick(sl, vq))
+        for c, f in ((1, 1), (9, 2), (10, 3)): scan(A(x, ALL, c), A(dn), A("pK%d" % h, f), OP.add)
+        for f in (2, 0, 1): scan(A(sl, ALL, 4 + f), A(dn), A("pC%d" % h, f), OP.add)
+        ts(A(sl, L3, 7), A(sl, L3, 6), 1.0, OP.add)
+        ts(X(h, 6, 2), X(h, 0, 2), RNDH, OP.add, -RNDH, OP.add)
+        for vq in range(4): cp(A("zl%d" % h, S(vq, None, 4)), pick(sl, vq, 4))
         mm([(A("pL%d" % h, S(0, 128)), A("zl%d" % h), IDF, True, True)])
 
     def D(h, k, s): return A("dt%d" % h, S(3 - k, None, 4), s)
 
     def aside_a(h, vis):
         tag("offa %d%d" % (vis, h))
-        x = "x%d" % h; dn = A("dn%d" % h); sl = "sl%d" % h
-        for c, f in ((9, 2), (10, 3)): scan(A(x, ALL, c), dn, A("pK%d" % h, f), OP.add)
-        ts(X(h, 6, 2), X(h, 0, 2), RNDH, OP.add, -RNDH, OP.add)
+        sl = "sl%d" % h
         tt(X(h, 2), X(h, 9), X(h, 10), OP.max)
         tt(X(h, 5), X(h, 9), X(h, 10), OP.min)
         tt(X(h, 4), X(h, 0), X(h, 6), OP.subtract)
         tt(X(h, 8), X(h, 1), X(h, 7), OP.subtract)
-        tt(X(h, 16), A(sl, L3, 0), X(h, 2), OP.add)
-        tt(X(h, 18, 2), A(sl, L3, S(2, 4)), X(h, 4, 2), OP.add)
+        tt(A(sl, L3, 0), A(sl, L3, 4), X(h, 2), OP.add)
         tt(X(h, 25), X(h, 5), X(h, 4), OP.subtract)
         tt(X(h, 22), X(h, 2), X(h, 8), OP.max)
         tt(X(h, 23), X(h, 2), X(h, 8), OP.min)
-        cp(A("dt%d" % h, L3), A("pC%d" % h, 3))
-        tt(X(h, 24), A(sl, L3, 1), X(h, 22), OP.add)
+
+    def aside_c(h, vis):
+        tag("offc %d%d" % (vis, h))
+        sl = "sl%d" % h
+        tt(A(sl, L3, 9), A(sl, L3, 7), X(h, 25), OP.add)
+        tt(X(h, 24), A(sl, L3, 5), X(h, 22), OP.add)
         tt(X(h, 26), X(h, 23), X(h, 5), OP.subtract)
-        ts(D(h, 3, 1), X(h, 25), 1.0, OP.add)
-        tt(D(h, 2, 0), X(h, 24), X(h, 16), OP.subtract)
+        tt(D(h, 2, 0), X(h, 24), A(sl, L3, 0), OP.subtract)
 
     def list2(h, vis):
         tag("l2 %d%d" % (vis, h))
-        cp(A("l2%d" % h), A("pL%d" % h, S(0, 128)))
+        ts(A("l2%d" % h), A("pL%d" % h, S(0, 128)), 0.25, OP.add)
+        act(A("dt%d" % h, L3), A("pC%d" % h, 3))
+        act(D(h, 3, 1), X(h, 25), AF.Identity, 1.0)
 
-    def gather2(h, vis):
+    def gather2(h, vis, a, b):
         tag("g2 %d%d" % (vis, h))
-        tt(A("p%d" % h), IN(A("swin"), A("l2%d" % h)), A("ax%d" % (vis % 2)), OP.mult)
+        c = S(16 * a, 16 * b)
+        tt(A("p%d" % h, c), IN(A("swin"), A("l2%d" % h, S(a, b))), A("ax%d" % (vis % 2), c), OP.mult)
+
+    def sibling(h, vis):
         scan(A("x%d" % h, ALL, 11), A("dn%d" % h), A("pD%d" % h, 3), OP.add)
         ts(X(h, 3), X(h, 11), 0.0, OP.not_equal, PEN, OP.mult)
+        k2 = A("pL%d" % h, S(128, 288))
+        mm([(k2, A("idb"), A("kc"), True, False), (k2, IDF, X(h, 1, 5), False, False)])
 
     def dots2(h, vis):
         tag("dot2 %d%d" % (vis, h))
-        k2 = A("pL%d" % h, S(128, 288))
-        mm([(k2, A("idb"), A("kc"), True, False)]
-           + [(A("pL%d" % h, S(129 + 40 * (r // 4) + r % 4, 168 + 40 * (r // 4), 5)), A("p%d" % h, S(r, None, 16)), A("gh"), False, False)
-              for r in range(16)] + [(k2, IDF, X(h, 1, 5), False, True)])
+        mm([(A("pL%d" % h, S(129 + 40 * (r // 4) + r % 4, 168 + 40 * (r // 4), 5)), A("p%d" % h, S(r, None, 16)), A("gh"), False, r == 15)
+            for r in range(16)], True)
 
     def aside_b(h, vis):
         tag("offb %d%d" % (vis, h))
         tt(X(h, 12), X(h, 11), X(h, 11), OP.mult)
-        for c, f in ((17, 0), (20, 1), (21, 2)): scan(A("x%d" % h, ALL, c), A("dn%d" % h), A("pD%d" % h, f), OP.add)
+        sl = "sl%d" % h
+        for n, c, f in ((sl, 3, 0), ("x%d" % h, 20, 1), ("x%d" % h, 21, 2)): scan(A(n, ALL, c), A("dn%d" % h), A("pD%d" % h, f), OP.add)
         ts(X(h, 13), X(h, 12), 4194304.0, OP.is_gt, -PEN, OP.mult)
-        tt(A("dt%d" % h, S(2, None, 4)), X(h, 16, 4), A("pC%d" % h, 3), OP.subtract)
-        tt(D(h, 2, 1), X(h, 18), X(h, 17), OP.subtract)
+        tt(A("dt%d" % h, S(2, None, 4)), A(sl, L3, S(0, None, 3)), A("pC%d" % h, 3), OP.subtract)
+        tt(D(h, 2, 1), A(sl, L3, 6), A(sl, L3, 3), OP.subtract)
         tt(D(h, 2, 2), X(h, 20), X(h, 25), OP.add)
         tt(X(h, 14), X(h, 6), X(h, 13), OP.add)
         tt(D(h, 3, 2), X(h, 21), X(h, 25), OP.subtract)
@@ -456,7 +471,7 @@ def rank_program(g, core, T, topo):
         tt(A(mk, S(2, None, 4)), A(t5, S(4, None, 5)), A(t5, S(2, None, 5)), OP.is_gt)
         for s in range(4): scan(A(st, ALL, s), A(mk), A("dt%d" % h, ALL, s), OP.add)
         zs = "zs%d" % h
-        for vq in range(4): cp(A(zs, S(2 + vq, 34, 4)), pick(st, vq))
+        for vq in range(4): (cp if (h, vis) == (1, 3) else act)(A(zs, S(2 + vq, 34, 4)), pick(st, vq))
         mm([(A(pl, S(128 + 128 * h, 256 + 128 * h)), A(zs, S(2, 34)), IDF, True, True)])
         if vis < 3:
             mm([(A(pl, S(256 - 128 * h, 384 - 128 * h)), A(zs, S(4 - 4 * h, 36 - 4 * h)), IDF, True, True)])
@@ -473,24 +488,26 @@ def rank_program(g, core, T, topo):
             cp(A("mg%d" % h, S(1024, 2048)), IN(A("mwin"), A("ml%d" % h, S(64, 128))))
         else: act(A("mg%d" % h), IN(A("mwin"), A("ml%d" % h)))
 
-    def m_sum(hs, k, pb):
-        tag("msum%d" % k)
-        for vh in range(2):
-            rs = [(h, r) for h in hs for r in range(8 * vh, 8 * vh + 8)]
-            mm([(A(pb, vh), A("idb"), A("mg%d" % h, S(r, None, 16)), i == 0, i == len(rs) - 1) for i, (h, r) in enumerate(rs)])
+    def m_sum(h, pb, first=True, last=True):
+        tag("msum%d" % h)
+        mm([(A(pb, S(0, 2)), A("idb"), A("mg%d" % h, S(r, None, 8)), first and r == 0, last and r == 7) for r in range(8)], not first)
 
     def m_out(k, pb):
         tag("mout%d" % k)
-        act(A("ms%d" % k), A(pb, S(0, 2)))
-        if k: send(A("ms%d" % k), A("rE%d" % k), [cores[(me - min(k, 3)) % N]], "aE%d" % k)
+        for vh in range(2): (act if k < 3 else cp)(A("ms%d" % k, S(128 * vh, 128 * vh + 128)), A(pb, S(0, 2), S(vh, None, 2)))
+        if k: send(A("ms%d" % k), A("rE%d" % k), [cores[(me - k) % N]], "aE%d" % k)
 
-    def places(h):
+    def places_a(h):
         tag("plc%d" % h)
-        so = "so%d" % h; sl = "sl%d" % h; y = A("st%d" % h, L3)
+        so = "so%d" % h; y = A("st%d" % h, L3)
         ts(A(so, 0), y, RND1, OP.add, -RND1, OP.add)
         tt(A(so, 1), y, A(so, 0), OP.subtract)
         ts(A(so, 1), A(so, 1), 32768.0, OP.mult)
         tt(A(so, 2), A(so, 1), A(so, 0), OP.add)
+
+    def places_b(h):
+        tag("plc%d" % h)
+        so = "so%d" % h; sl = "sl%d" % h
 
         def w(k, s): return A(so, k, S(s, None, 4))
         for i in (0, 2):
@@ -501,54 +518,65 @@ def rank_program(g, core, T, topo):
         for vq in range(4): cp(A("zp%d" % (vq // 2), S(2 * h + vq % 2, None, 4)), pick(sl, vq))
 
     steps = [(h, vis) for vis in range(4) for h in (0, 1)]
-    inherit(0, 0); weights_a(); inherit(1, 0)
-    lists(0, 0)
-    for i in range(9):
+    b1 = (me - 1) % N
+    inherit(0, 0); inherit(1, 0); weights_a()
+    lists(0, 0); gather1(0, 0); weights_b()
+    lists(1, 0); gather1(1, 0)
+    dots1(0, 0); fields(0, 0, 0); decide1(0, 0); dots1(1, 0); fields(0, 0, 1); aside_a(0, 0); list2(0, 0)
+    spread(1)
+    gather2(0, 0, 0, SPLIT); fields(1, 0, 0)
+    tag("choose1"); choose_a(RA, "rl", "ra%d" % b1)
+    cp(A("lkk"), A("rl")); tt(A("lkk"), A("lkk"), A("kof"), OP.add)
+    sibling(0, 0); gather2(0, 0, SPLIT, 128)
+    dots2(0, 0); decide1(1, 0); tag("choose1"); choose_p(); aside_a(1, 0); list2(1, 0)
+    aside_c(0, 0); aside_b(0, 0); decide2(0, 0); fields(1, 0, 1)
+    tag("choose1"); choose_b("ri%d" % b1)
+    send(A("ri%d" % b1), A("ri%d" % b1), [cores[(me + 1) % N], cores[(me + 2) % N]], "aI%d" % b1)
+    inherit(0, 1); gather2(1, 0, 0, SPLIT); lists(0, 1); keep(0, 0); sibling(1, 0); m_gather(0, 0); gather2(1, 0, SPLIT, 128)
+    spread(2)
+    for i in range(2, 9):
         now = steps[i] if i < 8 else None
-        old = steps[i - 1] if i > 0 else None
+        old = steps[i - 1]
         nxt = steps[i + 1] if i < 7 else None
+        if now: gather1(*now)
+        if i == 8: places_a(0)
+        dots2(*old)
         if now:
-            gather1(*now)
-            if i == 0:
-                weights_b(); tag("choose1"); choose_a("ra%d" % ((me + 1) % N))
-            fields(*now, 0)
-        if i == 8: places(0)
-        if old: dots2(*old)
-        if now: dots1(*now)
-        if i == 8:
-            m_sum((0,), 3, "pD0"); m_out(3, "pD0")
-        if old:
-            aside_b(*old); decide2(*old)
-        if now: decide1(*now)
-        if i == 0:
-            tag("choose1"); choose_p()
-        if old and nxt: inherit(*nxt)
+            fields(*now, 0, (0, 1)); dots1(*now); fields(*now, 0, (2, 3))
+        if i == 8: m_sum(0, "pD0", last=False)
+        aside_c(*old); aside_b(*old); decide2(*old)
         if now:
-            fields(*now, 1); aside_a(*now); list2(*now)
-        if i == 0:
-            tag("choose1"); choose_b("ri%d" % me)
-            send(A("ri%d" % me), A("ri%d" % me), peers, "aI%d" % me)
-            spread(1)
-        if old: keep(*old)
+            decide1(*now); fields(*now, 1, (0, 1))
+        if nxt: inherit(*nxt)
+        if now:
+            fields(*now, 1, (2, 3)); aside_a(*now); list2(*now)
+        if i % 2: m_sum(0, "pD0", last=False)
+        if i == 7:
+            keep(*old); m_gather(*old); m_sum(1, "pD0", first=False); m_out(2, "pD0")
+        if now: gather2(*now, 0, SPLIT)
         if nxt: lists(*nxt)
-        if i >= 3 and i % 2 == 1: m_sum((0, 1), (i - 3) // 2, "pD0")
-        if old and i < 8: m_gather(*old)
-        if i >= 3 and i % 2 == 1: m_out((i - 3) // 2, "pD0")
-        if now: gather2(*now)
-        if i in (1, 3): spread((i + 3) // 2)
+        if i != 7: keep(*old)
+        if now: sibling(*now)
+        if i in (3, 5): m_sum(1, "pD0", first=False)
+        if i < 7: m_gather(*old)
+        if i in (3, 5): m_out((i - 3) // 2, "pD0")
+        if now: gather2(*now, SPLIT, 128)
+        if i == 3: spread(3)
     m_gather(1, 3, True)
-    m_sum((1,), 4, "pD1"); m_out(4, "pD1")
-    places(1)
+    m_sum(1, "pD0", first=False); places_a(1); m_out(3, "pD0")
+    places_b(0); places_b(1)
     tag("out")
     for vh in range(2): mm([(A("pK0", vh), A("zp%d" % vh), IDF, True, True)])
     act(A("ycs"), A("pK0", S(0, 2)), AF.Identity, A("xv", S(13, 14)))
     dma("Y", [(H(T.yc[:, :]), A("ycs"))], "dyc")
     tt(A("acc"), A("ms0"), A("rE1"), OP.add)
-    for k in (2, 3): tt(A("acc"), A("acc"), A("rE%d" % k), OP.add)
+    tt(A("acc"), A("acc"), A("rE2"), OP.add)
+    tt(A("pC0", S(0, 2)), A("acc"), A(RA), OP.mult); cp(A("pC1", S(0, 2)), A(RA))
     for h in (0, 1):
         c = S(h * 128, h * 128 + 128)
-        tt(A("acc", c), A("acc", c), A("rE4", c), OP.add)
-        tt(A("yes", c), A("acc", c), A(RA, c), OP.mult)
-        dma("Y", [(H(T.ye[:, c]), A("yes", c))], "dye%d" % h)
+        cp(A("acc", c), A("rE3", c))
+        tt(A("ms0", c), A("acc", c), A("pC1", h), OP.mult)
+        tt(A("yes", c), A("ms0", c), A("pC0", h), OP.add)
+        dma("YS"[h], [(H(T.ye[:, c]), A("yes", c))], "dye%d" % h)
 
     need("G", [(s, cnt[s]) for s in cnt])

@@ -4,54 +4,58 @@ from concourse.mybir import AluOpType, ActivationFunctionType
 
 OP = AluOpType
 AF = ActivationFunctionType
-RND1 = 12582912.0
-RNDH = 6291456.0
+RND = 12582912.0
 PEN = 2097152.0
-SPLIT = 88
+CUTS = (40, 104)
+KCUT = 88
+MSPLIT = 40
+DOTS = (3, 9)
+MASK_V = (0, 1, 2, 3, 4, 5, 6, 7)
 TAG = [""]
 
 F32, B16, I32, U16 = "float32", "bfloat16", "int32", "uint16"
-NXV = 36
 SCRATCH = {
     "kl": ("sbuf", [128, 256], I32), "ul": ("sbuf", [128, 256], I32),
     "ytk": ("sbuf", [128, 2, 8, 16], I32), "xk": ("sbuf", [128, 256], F32), "zk": ("sbuf", [128, 256], F32),
-    "lstk": ("sbuf", [128, 256], U16),
-    "di": ("sbuf", [128, 2, 256], I32), "db": ("sbuf", [128, 9, 256], B16), "dp": ("sbuf", [128, 4, 128], B16),
+    "lstk": ("sbuf", [128, 256], U16), "db": ("sbuf", [128, 5, 256], B16), "dp": ("sbuf", [128, 6, 128], B16),
     "lki": ("sbuf", [128, 64], I32), "lku": ("sbuf", [128, 64], U16), "lkk": ("sbuf", [128, 64], F32), "kof": ("sbuf", [128, 64], F32),
-    "a0b": ("sbuf", [128, 256], B16), "il": ("sbuf", [128, 64], U16),
+    "a0b": ("sbuf", [128, 256], B16), "il": ("sbuf", [128, 64], U16), "rl": ("sbuf", [128, 64], U16),
     "swin": ("sbuf", [128, 4096], B16), "mwin": ("sbuf", [128, 4096], B16), "cwin": ("sbuf", [128, 2048], B16),
-    "meta": ("sbuf", [128, 4096], B16), "kk": ("sbuf", [128, 4096], B16),
+    "meta": ("sbuf", [128, 4096], B16), "inn": ("sbuf", [128, 4096], B16),
     "ax0": ("sbuf", [128, 2048], B16), "ax1": ("sbuf", [128, 2048], B16),
     "df": ("sbuf", [128, 1024], B16), "dabs": ("sbuf", [128, 1024], B16),
+    "yg": ("sbuf", [128, 512], F32), "nr": ("sbuf", [128, 128], F32), "lam": ("sbuf", [128, 128], B16), "rn": ("sbuf", [128, 160, 3], F32),
+    "d0": ("sbuf", [128, 256], F32), "zs": ("sbuf", [128, 32, 4], F32), "sl": ("sbuf", [128, 32, 4], F32), "nu": ("sbuf", [128, 32], F32),
     "kd": ("sbuf", [128, 4, 4, 16], F32), "km": ("sbuf", [128, 4, 2, 16], F32), "ki": ("sbuf", [128, 128], I32),
-    "xc": ("sbuf", [128, 4, 64], I32), "xh": ("sbuf", [128, 4, 64], I32), "xy": ("sbuf", [128, 4, 64], F32),
-    "xw": ("sbuf", [128, 11, 64], F32), "xo": ("sbuf", [128, 4, 64], F32), "y": ("sbuf", [128, 256], F32),
+    "xc": ("sbuf", [128, 4, 64], I32), "xh": ("sbuf", [128, 4, 64], I32), "xy": ("sbuf", [128, 4, 64], F32), "xi": ("sbuf", [128, 4, 64], I32),
+    "xw": ("sbuf", [128, 20, 64], F32), "xo": ("sbuf", [128, 4, 64], F32), "xz": ("sbuf", [128, 4, 64], F32), "xl": ("sbuf", [128, 64], U16),
     "one": ("sbuf", [128, 256], F32), "idf": ("sbuf", [128, 144], F32), "idb": ("sbuf", [128, 128], B16),
-    "gi": ("sbuf", [128, 8], F32), "gh": ("sbuf", [128, 8], F32), "m32": ("sbuf", [128, 32], F32),
-    "cf": ("sbuf", [128, 16, NXV], F32), "xv": ("sbuf", [128, NXV], F32), "rl": ("sbuf", [128, 64], U16),
-    "w16": ("sbuf", [128, 4, 8, 4], F32), "wz": ("sbuf", [128, 3, 16], F32),
-    "wg": ("sbuf", [128, 32, 8, 4], B16), "wl": ("sbuf", [128, 5, 32, 4], B16), "wp": ("sbuf", [128, 8, 8, 4], F32),
-    "sel": ("sbuf", [128, 4, 144], F32), "zq": ("sbuf", [128, 4, 144], B16), "wi": ("sbuf", [128, 128], B16),
-    "inn": ("sbuf", [128, 4096], B16), "hb": ("sbuf", [128, 16], F32), "pn": ("sbuf", [128, 3], I32), "pf": ("sbuf", [128, 3], F32), "nb": ("sbuf", [128, 3, 256], B16),
-    "r4": ("sbuf", [128, 128], F32), "r5": ("sbuf", [128, 160], F32), "kc": ("sbuf", [128, 160], B16),
+    "gi": ("sbuf", [128, 8], F32), "g3": ("sbuf", [128, 8, 3], F32), "gx": ("sbuf", [128, 8, 5, 2], F32), "m32": ("sbuf", [128, 32], F32),
+    "pn": ("sbuf", [128, 4], I32), "pf": ("sbuf", [128, 3], F32), "i16": ("sbuf", [128, 16], F32), "e16": ("sbuf", [128, 16], F32),
+    "e4": ("sbuf", [128, 4], F32), "hm": ("sbuf", [128, 4], F32), "fc": ("sbuf", [128, 8], F32), "bs": ("sbuf", [128, 24], F32),
+    "al": ("sbuf", [128, 8], F32), "mx": ("sbuf", [128, 4, 8, 16], B16),
+    "vg": ("sbuf", [128, 8, 9, 2], F32), "dg": ("sbuf", [128, 8, 8, 2], F32), "wg": ("sbuf", [128, 8, 8, 16], B16),
+    "vm": ("sbuf", [128, 2, 9, 2], F32), "dm": ("sbuf", [128, 48], F32), "wm": ("sbuf", [128, 8, 48], B16),
+    "jj": ("sbuf", [128, 8, 8], F32), "sel": ("sbuf", [128, 4, 8, 16], F32), "sq": ("sbuf", [128, 4, 144], F32),
+    "zq": ("sbuf", [128, 4, 144], B16), "zu": ("sbuf", [128, 144], B16), "zc": ("sbuf", [128, 146], B16), "wi": ("sbuf", [128, 128], B16),
+    "hb": ("sbuf", [128, 16], F32), "nb": ("sbuf", [128, 2, 256], B16), "r5": ("sbuf", [128, 160], F32),
     "ycs": ("sbuf", [128, 256], F32), "acc": ("sbuf", [128, 256], F32), "yes": ("sbuf", [128, 256], F32),
+    "pL": ("psum", [128, 512], F32), "pM": ("psum", [128, 4, 128], F32),
 }
 for _h in "01":
-    for _n, _s, _d in (("yw", [256], F32), ("yg", [512], F32), ("cl", [128], U16), ("l2", [128], U16), ("ml", [128], U16), ("nr", [128], F32),
-                       ("lam", [128], B16), ("p", [2048], F32), ("gm", [2048], B16), ("mg", [2048], B16), ("x", [128, 28], F32),
-                       ("dn", [128], F32), ("mk", [128], F32), ("sl", [128, 10], F32), ("st", [128, 4], F32), ("zl", [32, 4], F32),
-                       ("zs", [36, 4], F32), ("zp", [32, 4], F32), ("dt", [128, 4], F32), ("t5", [160], F32), ("so", [4, 128], F32)):
+    for _n, _s, _d in (("yw", [256], F32), ("cl", [128], U16), ("l2", [128], U16), ("ml", [128], U16), ("stk", [256, 2], B16),
+                       ("p", [2048], F32), ("q", [2048], F32), ("gm", [2048], B16), ("mg", [2048], B16),
+                       ("st", [256, 4], F32), ("zp", [32, 4], F32), ("so", [4, 128], F32)):
         SCRATCH[_n + _h] = ("sbuf", [128] + _s, _d)
-    for _n in ("pK", "pC", "pD"): SCRATCH[_n + _h] = ("psum", [128, 4, 128], F32)
-    SCRATCH["pL" + _h] = ("psum", [128, 512], F32)
+    SCRATCH["pK" + _h] = ("psum", [128, 170, 3], F32)
+    for _n in ("pA", "pB"): SCRATCH[_n + _h] = ("psum", [128, 256, 2], F32)
 for _k in range(4):
     SCRATCH["ra%d" % _k] = ("sbuf", [128, 256], B16)
     SCRATCH["ri%d" % _k] = ("sbuf", [128, 64], U16)
-for _k in range(4):
     SCRATCH["ms%d" % _k] = ("sbuf", [128, 256], F32 if _k < 3 else U16)
     if _k: SCRATCH["rE%d" % _k] = ("sbuf", [128, 256], F32 if _k < 3 else U16)
 
-_DS = ["dk", "du", "da", "dl", "da0", "dyk", "dxc", "dss", "dmm", "dxv", "dcw", "dm0", "dm1", "dm2", "dm3", "dy0", "dyc", "dye0", "dye1"]
+_DS = ["dk", "du", "da", "dl", "da0", "dyk", "dxc", "dss", "dmm", "dcw", "dcu", "dm0", "dm1", "dm2", "dm3", "dyc", "dye0", "dye1"]
 SEMAPHORES = ["sv", "ss", "sp", "sg", "rl", "aL"] + _DS + ["aA%d" % k for k in range(4)] + ["aI%d" % k for k in range(4)] + ["aE%d" % k for k in range(1, 4)]
 
 ALL = slice(None)
@@ -60,29 +64,11 @@ ALL = slice(None)
 def S(a, b=None, c=None): return slice(a, b, c)
 
 
-def telescoped(slot_of):
-    w = {}
-    for t in range(4):
-        w[(slot_of(t), t)] = w.get((slot_of(t), t), 0) + 1
-        if t < 3: w[(slot_of(t + 1), t)] = w.get((slot_of(t + 1), t), 0) - 1
-    return [(s, t, c) for (s, t), c in sorted(w.items()) if c]
-
-
-PATTERNS = [telescoped(lambda t: t), [(t, t, 1) for t in range(4)], telescoped(lambda t: t ^ 1), telescoped(lambda t: 2 - (t & 2)),
-            telescoped(lambda t: 3 - (t & 2))]
-P_T, P_ID, P_U, P_A, P_B = range(5)
-KID = {0: 1.0, 1: 1.0}; UP = {2: 1.0, 3: 2.0, 4: 2.0}; UPP = {3: 1.0, 4: 1.0}; NODE = {5: 1.0, 6: 2.0, 7: 256.0}; NP = {6: 1.0, 7: 128.0}
-KKL = {8: 1.0, 9: 1.0}; KKR = {10: 1.0, 11: 1.0}; NP2 = {14: 1.0, 15: 128.0}
-
-
-def lin(*terms):
-    d = {}
-    for c, rows in terms:
-        for k, w in rows.items(): d[k] = d.get(k, 0.0) + c * w
-    return d
-
-
-VALUES = [UP, KID, NODE, lin((1, KKR), (-1, KID)), lin((1, KKL), (-1, KKR)), lin((4096, NP2), (1, UPP)), lin((-4096, NP2)), lin((-1, NP))]
+KID, UP, NODE, KKL, KKR = 0, 1, 2, 4, 5
+NODES = [(S(0, 2), S(0, 1), 3, KID), (S(0, 2), S(1, 2), 3, KKL), (S(0, 2), S(2, 3), 3, KKR), (S(0, 2), S(4, 8, 3), 2, KID), (S(0, 2), S(5, 6), 0, KID),
+         (S(0, 2), S(6, 7), 1, KID), (S(0, 1), S(3, 4), 0, NODE), (S(1, 2), S(3, 4), 1, NODE),
+         (S(2, 3), S(0, 4, 3), 2, NODE), (S(2, 3), S(1, 3), 3, KID), (S(2, 3), S(4, 5), 3, NODE), (S(2, 3), S(5, 6), 1, NODE), (S(2, 3), S(6, 7), 0, NODE),
+         (S(2, 3), S(7, 8), 0, UP), (S(3, 4), S(0, 8, 4), 0, UP), (S(3, 4), S(1, 3), 2, UP), (S(3, 4), S(5, 7), 2, UP), (S(3, 4), S(3, 8, 4), 3, NODE)]
 
 
 def rank_program(g, core, T, topo):
@@ -184,9 +170,6 @@ def rank_program(g, core, T, topo):
     def act(o, a, f=AF.Copy, bias=0.0, scale=1.0):
         op("S", [lambda: g.scalar.activation(out=o[0], in_=a[0], func=f, bias=val(bias), scale=val(scale))], [a, bias, scale], [o])
 
-    def fill(o, c):
-        act(o, A("one", S(0, int(np.prod(o[0].shape[1:])))), scale=float(c))
-
     def mm(group, acc=False):
         op("P", [(lambda q=q: g.tensor.matmul(out=q[0][0], lhsT=q[1][0], rhs=q[2][0], start=q[3], stop=q[4])) for q in group],
            [q[1] for q in group] + [q[2] for q in group], [q[0] for q in group], acc)
@@ -199,6 +182,11 @@ def rank_program(g, core, T, topo):
 
     def tag(s): TAG[0] = s
 
+    def C(name, j): return A(name, S(j, j + 1))
+    def E(k): return C("e16", k)
+    def spreadcol(o, col): act(o, A("one", S(0, int(np.prod(o[0].shape[1:])))), scale=col)
+    def axpy(o, c, x, y): act(o, x, AF.Identity, y, float(c))
+
     RA = "ra%d" % me
     ne = len(topo.engines(core, peers[0]))
     for k in range(N):
@@ -209,70 +197,133 @@ def rank_program(g, core, T, topo):
     for k in range(1, 4): wr["rE%d" % k] = [(A("rE%d" % k)[1][0][1], "far", ("aE%d" % k, ne))]
 
     tag("load")
+    dma("S", [(A("ul"), H(T.up[:, :]))], "du")
     dma("Y", [(A("kl"), H(T.kid[:, :]))], "dk")
-    dma("S", [(A(RA), H(T.a[:, :]))], "da")
     dma("Y", [(A("ytk", k), H(T.kid[k::2, :])) for k in (0, 1)], "dyk")
-    dma("S", [(A("lki"), H(T.lk[:, :]))], "dl")
-    dma("S", [(A("a0b"), H(T.a0[:, :]))], "da0")
+    dma("S", [(A("xc", t), H(T.cut0[t::4, :])) for t in range(4)], "dxc")
+    dma("Y", [(A(RA), H(T.a[:, :]))], "da")
+    dma("Y", [(A("lki"), H(T.lk[:, :]))], "dl")
+    dma("Y", [(A("a0b"), H(T.a0[:, :]))], "da0")
 
     tag("const")
-    iota(A("pn", S(0, 1)), [[0, 1]], 0, 1, False)
-    iota(A("db", 5), [[0, 128], [1, 2]], 0, 0); iota(A("db", 6), [[1, 128], [0, 2]], 0, 0)
-    ms(A("one"), 1.0); ms(A("cf"), 0.0)
-    ts(A("pn", S(1, 2)), A("pn", S(0, 1)), 15, OP.bitwise_and); ts(A("pn", S(2, 3)), A("pn", S(0, 1)), 7, OP.bitwise_and)
-    for j, rows in enumerate(VALUES):
-        for k, w in rows.items(): ms(A("cf", k, S(j, j + 1)), w)
-    for q in range(4):
-        ms(A("cf", S(4 * q, 4 * q + 4), 9 + q), 1.0)
-        fill(A("cf", S(q, None, 4), 13), -32768.0 * (1.5 - q) / 8)
-    for f in range(5):
-        for s, t, c in PATTERNS[f]: fill(A("cf", S(s, None, 4), 16 + 4 * f + t), c)
-
-    def pt(f, n=1): return A("cf", S(0, 4), S(16 + 4 * f, 16 + 4 * (f + n)))
-    dma("Y", [(A("xv"), A("cf", rows=S(0, 8)))], "dxv")
-    dma("S", [(A("xc", t), H(T.cut0[t::4, :])) for t in range(4)], "dxc")
-    dma("Y", [(A("ul"), H(T.up[:, :]))], "du")
-    iota(A("hb"), [[1, 16]], 0, 0)
-    for j, (c, k) in enumerate(((1, 5), (2, 6), (2, 7))): ts(A("pf", S(j, j + 1)), A("pn", S(c, c + 1)), k, OP.is_equal)
-    act(A("nb", 0), A("db", 5), scale=A("pf", S(0, 1))); act(A("nb", 1), A("db", 6), scale=A("pf", S(1, 2)))
-    act(A("hb"), A("hb"), scale=A("pf", S(2, 3)))
-    ms(A("cwin"), 0.0); ms(A("zq"), 0.0)
-    tt(A("nb", 2), A("nb", 0), A("nb", 1), OP.add)
+    SR, AND = OP.arith_shift_right, OP.bitwise_and
+    iota(C("pn", 0), [[0, 1]], 0, 1, False); iota(A("i16"), [[1, 16]], 0, 0); iota(A("nb", 0), [[1, 256]], 0, 0)
+    ms(A("one"), 1.0)
+    for j, b in enumerate((15, 7, 3)): ts(C("pn", j + 1), C("pn", 0), b, AND)
+    cp(A("pf"), A("pn", S(1, 4)))
+    ts(A("e16"), A("i16"), C("pf", 0), OP.is_equal); ts(A("e4"), A("i16", S(0, 4)), C("pf", 2), OP.is_equal)
+    tt(A("fc"), A("e16", S(0, None, 2)), A("e16", S(1, None, 2)), OP.add)
+    ms(A("cwin"), 0.0)
+    for j, (c, k, f) in enumerate(((1, 4, OP.is_lt), (1, 4, OP.is_ge), (0, 8, OP.is_lt), (0, 8, OP.is_ge))): ts(C("hm", j), C("pf", c), k, f)
+    for n in ("zq", "zu", "zc", "mx", "gx", "sel", "vg", "vm"): ms(A(n), 0.0)
     gsel(A("gi"), A("one", S(0, 8)), [[-16, 8]], 0, 1, OP.is_ge, 0.0)
     gsel(A("gi"), A("gi"), [[16, 8]], 15, -1, OP.is_ge, 0.0)
+    gsel(A("m32"), A("one", S(0, 32)), [[-4, 4], [-16, 8]], 0, 1, OP.is_ge, 0.0)
+    gsel(A("m32"), A("m32"), [[4, 4], [16, 8]], 3, -1, OP.is_ge, 0.0)
     iota(A("kof"), [[256, 4], [0, 16]], 0, 0)
     gsel(A("idf"), A("one", S(0, 144)), [[-1, 144]], 8, 1, OP.is_equal, 0.0)
     gsel(A("wi"), A("one", S(0, 128)), [[-1, 8], [0, 16]], 0, 1, OP.is_equal, 0.0)
-    gsel(A("m32"), A("one", S(0, 32)), [[-4, 4], [-16, 8]], 0, 1, OP.is_ge, 0.0)
-    gsel(A("m32"), A("m32"), [[4, 4], [16, 8]], 3, -1, OP.is_ge, 0.0)
+    gsel(A("jj"), A("one", S(0, 64)), [[-16, 8], [-1, 8]], 0, 1, OP.is_equal, 0.0)
+    gsel(A("jj"), A("jj"), [[-16, 8], [-1, 8]], -8, 1, OP.not_equal, 1.0)
     tag("static")
-    for k in range(16): act(A("meta", S(256 * k, 256 * k + 256)), A("nb", 2), AF.Identity, A("hb", S(k, k + 1)))
+    act(C("hb", 0), C("pf", 0), scale=256.0); spreadcol(A("nb", 1), C("hb", 0))
+    act(A("zq", ALL, S(15, 128, 16)), A("m32"), scale=1024.0)
+    act(A("zu", S(15, 128, 16)), A("gi"), scale=C("fc", UP))
+
+    tag("weights0")
+    def B(j): return C("bs", j)
+    HA, HB, H3, LA, LB, L3, LA1, LB1, L31, T1, HALF, BETA, C2, CN, CT, C3 = range(16)
+    act(C("al", 0), C("e4", 0), AF.Identity, -1.0); act(A("al", S(1, 4)), A("e4", S(1, 4)))
+    axpy(C("al", 5), -1, C("e4", 3), C("e4", 2)); act(C("al", 6), C("e4", 3)); axpy(C("al", 4), -1, C("e4", 1), C("al", 0))
+    axpy(B(BETA), 1, E(0), E(4)); act(B(HALF), E(11), scale=0.5); axpy(B(HA), 1, E(4), E(1)); axpy(B(LA), -1, E(4), E(0))
+    for j, (k, c) in enumerate(((6, -5 / 16), (7, 65), (8, 66), (9, -66), (10, 67), (11, 1))):
+        axpy(B(BETA), c, E(k), B(BETA)); act(A("mx", ALL, ALL, j), A("m32"), scale=C("al", j))
+    act(A("mx", ALL, ALL, 6), A("m32"), scale=C("al", 6))
+    for k, c in ((7, -64), (8, -64), (9, 64), (10, -64)): act(A("mx", ALL, ALL, k), A("m32"), scale=float(c))
+    axpy(C("dm", 3), PEN, E(8), B(HALF)); axpy(C("dm", 7), PEN, E(10), B(HALF)); axpy(C("dm", 8), PEN, E(7), B(HALF))
+    for o, x in ((S(0, 3), E(2)), (S(4, 10, 5), E(3)), (S(5, 6), E(3)), (S(10, 12), E(0)), (S(13, 15), E(1)), (S(6, 7), B(HA)), (S(12, 13), B(LA))):
+        spreadcol(A("dm", o), x)
+    axpy(C("dm", 3), PEN, E(9), C("dm", 3))
+    for j in range(2): act(A("zc", S(15 + j, 130, 16)), A("gi"), scale=C("fc", KID))
+    for j in range(3): act(A("g3", ALL, j), A("gi"))
+    act(A("gx", ALL, 1, 0), A("gi")); act(A("gx", ALL, 2, 1), A("gi"))
+    for k in range(8): act(A("wm", k, S(0, 15)), A("dm", S(0, 15)), scale=C("gi", k))
+    for k in range(4): act(A("sq", k), A("idf"), scale=C("e4", k))
+    act(A("idb"), A("idf", S(8, 136)))
+    for vq in range(4):
+        c = 4 * (vq % 2); act(A("sel", vq, ALL, S(8 * (vq // 2) + c, 8 * (vq // 2) + c + 4)), A("jj", ALL, S(c, c + 4)))
+
+    tag("weights")
+    axpy(B(HB), 1, E(5), E(3)); axpy(B(LB), -1, E(5), E(2))
+    act(B(T1), E(11), scale=7 / 16); act(B(C2), E(11), scale=2 / 64)
+    axpy(B(CN), 3 / 64, E(11), E(0)); axpy(B(CT), 1 / 64, E(11), E(2)); axpy(B(C3), 3 / 64, E(11), E(3))
+    axpy(B(H3), -1, E(6), B(T1)); axpy(B(T1), 1, B(HA), E(2))
+    def V(f, e): return A("vm", f // 2, e, S(f % 2, f % 2 + 1))
+    axpy(V(0, 3), -1 / 64, E(10), B(CN)); axpy(V(0, 4), 1 / 64, E(9), B(CT)); axpy(B(C3), -1 / 64, E(9), B(C3)); axpy(B(L3), -1, B(H3), B(T1))
+    for e, x in ((1, E(3)), (2, B(LA)), (5, E(0)), (6, E(1)), (7, E(2))): axpy(V(0, e), 1, x, B(C2))
+    axpy(B(C3), -2 / 64, E(8), B(C3)); axpy(A("bs", S(LA1, LA1 + 3)), 1, A("bs", S(LA, LA + 3)), E(11))
+    for f, e, s, fld in NODES:
+        spreadcol(A("vg", 2 * s + f.start // 2, e, S(f.start % 2, (f.stop - 1) % 2 + 1)), C("fc", fld))
+    axpy(V(0, 0), 2 / 64, E(7), B(C3))
+    for f, e, x in ((1, S(0, 8, 4), B(LA1)), (1, S(7, 8), B(LA1)), (1, S(1, 3), B(L31)), (1, S(3, 4), E(1)), (1, S(5, 7), B(LB1)),
+                    (2, S(0, 4, 3), E(2)), (2, S(1, 2), B(LA1)), (2, S(2, 5, 2), E(3)), (2, S(5, 6), E(1)), (2, S(6, 7), E(0)), (2, S(7, 8), B(HA)),
+                    (3, S(0, 8, 4), B(HA)), (3, S(1, 3), B(H3)), (3, S(3, 8, 4), E(3)), (3, S(5, 7), B(HB))): spreadcol(V(f, e), x)
+
+    def grandchildren(a, b):
+        tag("kk")
+        act(A("meta", S(16 * a, 16 * b)), IN(A("cwin"), A("lstk", S(a, b))))
 
     def spread(vis):
+        tag("spread")
         b = (me - vis) % N
         for r in range(16):
             gsel(A("ax%d" % (vis % 2), S(r, None, 16)), A("ra%d" % b, S(128 * (r // 8), 128 * (r // 8) + 128)), [[0, 128]], 1, 0, OP.is_gt, 0.0)
-    spread(0)
 
     tag("bytes")
-    SR, AND = OP.arith_shift_right, OP.bitwise_and
-
-    def table(pairs, sem): dma("Y", [(A("meta", rows=S(k, None, 16)), A("db", j)) for k, j in pairs], sem, True)
+    cp(A("db", 3), A("ul")); tt(A("db", 2), A("ul"), A("db", 3), OP.subtract)
+    for j in range(2): cp(A("dp", 4 + j), A("db", 2 + j, S(0, None, 2)))
+    dma("Y", [(A("cwin", rows=S(2 + j, None, 16)), A("dp", 4 + j)) for j in range(2)], "dcu", True)
     cp(A("db", 1), A("kl")); tt(A("db", 0), A("kl"), A("db", 1), OP.subtract)
     for j in range(4): cp(A("dp", j), A("db", j % 2, S(j // 2, None, 2)))
-    dma("Y", [(A("cwin", rows=S(8 + j, None, 16)), A("dp", j)) for j in range(4)], "dcw")
-    ts(A("db", 8), A("kl"), 0, OP.is_ge)
-    dma("Y", [(A("inn", rows=S(0, 8)), A("db", 8))], "dm0")
+    dma("Y", [(A("cwin", rows=S(8 + j, None, 16)), A("dp", j)) for j in range(4)], "dcw", True)
+    ts(A("db", 4), A("kl"), 0, OP.is_lt, -256.0, OP.mult)
+    dma("Y", [(A("inn", rows=S(0, 8)), A("db", 4))], "dm0")
     dma("Y", [(A("swin", S(0, 2048)), H(T.s[:, 0:2048]))], "dss")
+    dma("Y", [(A("swin", S(2048, 4096)), H(T.s[:, 2048:4096]))], "dm3")
+    tag("lstk")
+    for b in range(8):
+        cp(A("xk", S(32 * b, 32 * b + 32)), A("ytk", ALL, b))
+    op("V", [lambda: g.vector.transpose(out=T.zk[:, :], in_=T.xk[:, :])], [A("xk")], [A("zk")])
+    for b in range(8):
+        ts(A("lstk", S(b, None, 8)), A("zk", S(32 * b, 32 * b + 32)), 0.5, OP.mult)
+    grandchildren(0, KCUT)
     cp(A("lku"), A("lki"))
     send(A(RA), A(RA), peers, "aA%d" % me)
     send(A("lku"), A("rl"), [cores[(me + 1) % N]], "aL")
-    gsel(A("r4"), A("one", S(0, 128)), [[0, 32], [1, 4]], 0, 0, OP.is_gt, 0.0)
+    spread(0)
+    tag("const")
     gsel(A("r5"), A("one", S(0, 160)), [[0, 32], [1, 5]], 0, 0, OP.is_gt, 0.0)
-    gsel(A("r5"), A("r5"), [[0, 32], [1, 5]], -3, 0, OP.not_equal, 0.0)
-    for h in "01":
-        iota(A("zs" + h), [[0, 144]], 0, 0)
-        for o in (A("dn" + h, S(0, None, 4)), A("mk" + h, S(0, None, 4)), A("dt" + h, S(0, None, 4), 0)): iota(o, [[0, 32]], 0, 0)
+    iota(A("d0", S(0, None, 8)), [[0, 32]], 0, 0)
+
+    tag("cut0")
+    def W(k, n=1): return A("xw", S(k, k + n))
+    ts(A("xh"), A("xc"), 1, SR)
+    for t in range(4): ts(A("xy", t), A("xc", t), (7 - 2 * t) / 16, OP.add)
+    for k, (i, j) in enumerate(((0, 2), (0, 3), (0, 1), (1, 3), (1, 2), (2, 3))): tt(W(k), A("xh", i), A("xh", j), OP.is_equal)
+    tt(W(6, 2), W(0, 2), W(3, 2), OP.max)
+    tt(W(8), A("xy", 2), A("xy", 1), OP.subtract); tt(W(9), A("xy", 3), A("xy", 1), OP.subtract)
+    tt(W(10), W(0), W(1), OP.max); tt(W(11), W(3), W(4), OP.max)
+    tt(W(8, 2), W(8, 2), W(6, 2), OP.mult)
+    tt(W(10, 2), W(10, 2), A("xw", S(2, 6, 3)), OP.max)
+    cp(A("xo", 0), A("xy", 0)); tt(W(12), A("xy", 1), W(8), OP.add)
+    tt(A("xo", S(2, 4)), A("xy", S(2, 4)), W(8, 2), OP.subtract)
+    tt(A("xo", 1), W(12), W(9), OP.add)
+    tt(W(13), W(11), W(10), OP.is_gt)
+    tt(W(14, 2), A("xo", S(2, 4)), A("xo", S(0, 2)), OP.subtract)
+    for j in range(2): tt(W(14 + j), W(14 + j), W(13), OP.mult)
+    tt(A("xz", S(0, 2)), A("xo", S(0, 2)), W(14, 2), OP.add); tt(A("xz", S(2, 4)), A("xo", S(2, 4)), W(14, 2), OP.subtract)
+    cp(A("xi"), A("xz")); ts(A("xh"), A("xi"), 1, SR); cp(A("xl"), A("xh", 0))
+    act(A("mg0", S(0, 1024)), IN(A("cwin"), A("xl")))
 
     def choose_a(kept, lk, a):
         for k in range(4):
@@ -281,302 +332,268 @@ def rank_program(g, core, T, topo):
     def choose_p():
         act(A("dabs"), A("df"), AF.Abs)
         for q in range(4):
-            mm([(A("pK0", q, S(0, 64)), A("zq", q, S(15 - l, 143 - l)), A("dabs", S(l, None, 16)), l == 0, l == 15) for l in range(16)])
+            mm([(A("pM", q, S(0, 64)), A("zq", q, S(15 - l, 143 - l)), A("dabs", S(l, None, 16)), l == 0, l == 15) for l in range(16)])
 
     def choose_b(out):
-        for q in range(4): tt(A("kd", q), A("pK0", q, S(0, 64)), A("lkk"), OP.add)
+        for q in range(4): tt(A("kd", q), A("pM", q, S(0, 64)), A("lkk"), OP.add)
         tt(A("km"), A("kd", ALL, S(0, 2)), A("kd", ALL, S(2, 4)), OP.min)
         tt(A("ki", S(0, 64)), A("km", ALL, 0), A("km", ALL, 1), OP.min)
         ts(A("ki", S(64, 128)), A("ki", S(0, 64)), 255, AND)
         cp(A(out), A("ki", S(64, 128)))
 
+    def mask_bank(k): return A(("pA0", "pB0", "pA1", "pB1")[k % 4])
+
+    def mask_p(ks):
+        tag("mask")
+        for k in ks:
+            c = S(512 * k, 512 * k + 512)
+            mm([(mask_bank(k), A("wi", rows=S(0, 8)), A("inn", c, rows=S(0, 8)), True, k in MASK_V)]
+               + ([] if k in MASK_V else [(mask_bank(k), A("idb"), A("swin", c), False, True)]))
+
+    def mask(ks):
+        tag("mask")
+        for k in ks:
+            c = S(512 * k, 512 * k + 512)
+            if k in MASK_V: tt(A("swin", c), A("swin", c), mask_bank(k), OP.add)
+            else: act(A("swin", c), mask_bank(k))
+
+    def cut_rows(slots):
+        tag("cut0p")
+        mm([(A("pL", S(256 + 64 * w, 320 + 64 * w)), A("sq", w, S(8 + w - s, 136 + w - s)), A("xz" if s == 1 else "xo", s), (s, w) == (1, 0), (s, w) == (0, 3))
+            for s in slots for w in range(4)], slots[0] != 1)
+
     tag("choose0")
     choose_a("a0b", "lku", RA)
-    for q in range(4): ts(A("zq", q, S(15, 128, 16)), A("gi"), A("xv", S(9 + q, 10 + q)), OP.mult, 1024.0, OP.mult)
-    choose_p()
-    tag("lstk")
-    for b in range(8):
-        cp(A("xk", S(32 * b, 32 * b + 32)), A("ytk", ALL, b))
-    op("V", [lambda: g.vector.transpose(out=T.zk[:, :], in_=T.xk[:, :])], [A("xk")], [A("zk")])
-    for b in range(8):
-        ts(A("lstk", S(b, None, 8)), A("zk", S(32 * b, 32 * b + 32)), 0.5, OP.mult)
-    tag("kk")
-    act(A("kk"), IN(A("cwin"), A("lstk")))
-    tt(A("lkk"), A("lki"), A("kof"), OP.add)
-
+    mask_p(range(4))
     tag("cut0")
-    ts(A("xh"), A("xc"), 1, SR)
-    for t in range(4): ts(A("xy", t), A("xc", t), (1.5 - t) / 8, OP.add)
-    for k, (i, j) in enumerate(((0, 2), (1, 3), (0, 3), (1, 2))): tt(A("xw", k), A("xh", i), A("xh", j), OP.is_equal)
-    tt(A("xw", 6), A("xy", 2), A("xy", 1), OP.subtract); tt(A("xw", 7), A("xy", 3), A("xy", 1), OP.subtract)
-    tt(A("xw", 4), A("xw", 0), A("xw", 1), OP.max); tt(A("xw", 5), A("xw", 2), A("xw", 3), OP.max)
-    cp(A("xo", 0), A("xy", 0))
-    tt(A("xw", 8), A("xw", 4), A("xw", 6), OP.mult); tt(A("xw", 9), A("xw", 5), A("xw", 7), OP.mult)
-    tt(A("xw", 10), A("xy", 1), A("xw", 8), OP.add)
-    tt(A("xo", 2), A("xy", 2), A("xw", 8), OP.subtract); tt(A("xo", 3), A("xy", 3), A("xw", 9), OP.subtract)
-    tt(A("xo", 1), A("xw", 10), A("xw", 9), OP.add)
-    dma("Y", [(A("y", rows=S(t, None, 4)), A("xo", t)) for t in range(4)], "dy0")
-    dma("Y", [(A("swin", S(2048, 4096)), H(T.s[:, 2048:4096]))], "dm3")
-    tag("bytes")
-    ts(A("di", 0), A("ul"), 1, AND); ts(A("di", 1), A("ul"), 1, SR)
-    cp(A("db", 2), A("di", 0)); cp(A("db", 4), A("di", 1)); tt(A("db", 3), A("di", 1), A("db", 4), OP.subtract)
-    table([(j, j) for j in range(5)], "dm1")
+    mm([(A("pL", S(0, 64)), A("zu", S(15 - l, 143 - l)), A("mg0", S(l, 1024, 16)), l == 0, l == 15) for l in range(16)])
+    mask((0, 1))
     tag("choose0")
-    choose_b("il")
-    for f, (pat, j) in enumerate(((P_A, 0), (P_U, 0), (P_T, 1), (P_ID, 2), (P_U, 2), (P_T, 3), (P_T, 4))):
-        ts(A("w16", ALL, f), pt(pat), A("xv", S(j, j + 1)), OP.mult)
-    for k, pat in enumerate((P_A, P_B, P_U)): ts(A("wz", k), pt(pat), A("xv", S(5 + k, 6 + k)), OP.mult)
-    tt(A("wz", 0), A("wz", 0), A("wz", 1), OP.add); tt(A("w16", ALL, 7), A("wz", 0), A("wz", 2), OP.add)
-    for q in range(4): act(A("sel", q), A("idf"), scale=A("xv", S(9 + q, 10 + q)))
-
-    tag("mask")
-    banks = [A(n + h) for n in ("pK", "pC", "pD") for h in "10"] + [A("pK1"), A("pK0")]
-    for k in range(8):
-        c = S(512 * k, 512 * k + 512)
-        mm([(banks[k], A("wi", rows=S(0, 8)), A("inn", c, rows=S(0, 8)), True, True)])
-        tt(A("swin", c), A("swin", c), banks[k], OP.mult)
-    dma("Y", [(A("meta", rows=S(j, None, 16)), A("kk", rows=S(j, None, 16))) for j in range(8, 12)], "dm2", True)
+    choose_p()
+    grandchildren(KCUT, 256)
+    dma("Y", [(A("meta", rows=S(j, None, 16)), A("db", j) if j < 4 else A("nb", j - 4)) for j in range(6)], "dm1")
     dma("Y", [(A("mwin"), H(T.m[:, :]))], "dmm")
 
-    def weights_a():
-        tag("const3")
-        for f in range(5):
-            for t in range(4): act(A("wl", f, ALL, t), A("m32"), scale=A("xv", S(16 + 4 * f + t, 17 + 4 * f + t)))
-        act(A("gh"), A("gi"), scale=0.5)
-        for k in range(8): act(A("wp", ALL, k), pt(P_ID, 2), scale=A("gh", S(k, k + 1)))
-        for k in range(8): act(A("wg", ALL, k), A("w16"), scale=A("gi", S(k, k + 1)))
+    tag("cut0b")
+    cp(A("xi", 0), A("pL", S(0, 64))); ts(A("xi", 1), A("xi", 0), 1, SR)
+    tt(W(0), W(10), W(11), OP.max); tt(W(1), W(10), W(11), OP.mult)
+    tt(W(2), A("xi", 1), A("xh", 2), OP.is_equal); tt(W(3), A("xi", 1), A("xh", 3), OP.is_equal)
+    tt(W(4), A("xz", 3), A("xz", 2), OP.subtract)
+    ts(W(1), W(1), 2.0, OP.mult, 1.0, OP.add)
+    tt(W(5), W(2), W(3), OP.add); tt(W(4), W(4), W(3), OP.mult)
+    tt(W(5), W(5), W(1), OP.add)
+    tt(A("xo", 2), A("xz", 2), W(4), OP.add); tt(A("xo", 3), A("xz", 3), W(4), OP.subtract)
+    tt(W(5), W(5), W(0), OP.mult); ts(W(5), W(5), 1 / 64, OP.mult); tt(A("xo", 0), A("xz", 0), W(5), OP.add)
+    cut_rows((1, 2, 3)); cut_rows((0,))
+    tag("choose0")
+    tt(A("lkk"), A("lki"), A("kof"), OP.add)
+
+    def first_cuts():
+        tag("first")
+        for h in range(2): act(A("yw%d" % h), A("pL", S(256, 512)), scale=C("hm", 2 + h))
 
     def weights_b():
-        act(A("idb"), A("idf", S(8, 136)))
-        fill(A("kc"), 0.25); fill(A("kc", S(2, None, 5)), 0.5)
+        tag("weights")
+        tt(A("vm", 0, ALL, 1), A("vm", 0, ALL, 1), A("vm", 0, ALL, 0), OP.subtract)
+        tt(A("vg", S(0, 4, 2), ALL, 1), A("vg", S(0, 4, 2), ALL, 1), A("vg", S(0, 4, 2), ALL, 0), OP.subtract)
+        tt(A("dm", S(16, 48)), A("vm", ALL, S(0, 8)), A("vm", ALL, S(1, 9)), OP.subtract)
+        tt(A("dg"), A("vg", ALL, S(0, 8)), A("vg", ALL, S(1, 9)), OP.subtract)
+
+    def weights_c():
+        tag("weights")
+        for k in range(8): act(A("wm", k, S(16, 48)), A("dm", S(16, 48)), scale=C("gi", k))
+        for k in range(8): act(A("wg", k), A("dg"), scale=C("gi", k))
 
     IDF = A("idf", S(8, 136))
-    L3 = S(3, None, 4)
-
-    def X(h, c, n=1): return A("x%d" % h, L3, S(c, c + n) if n > 1 else c)
-
-    def pick(buf, vq, c=0): return A(buf, S(32 * vq + 3, 32 * vq + 32, 4), S(c, c + 4))
+    Y, L2, TN = A("pL", S(0, 128)), A("pL", S(128, 256)), A("pL", S(256, 384))
 
     def inherit(h, vis):
         tag("inh%d%d" % (vis, h))
         lst = "il" if vis == 0 else "ri%d" % ((me - vis) % N)
-        act(A("yg%d" % h), IN(A("y" if vis == 0 else "yw%d" % h), A(lst, S(32 * h, 32 * h + 32))))
-        mm([(A("pL%d" % h, S(0, 128)), A("sel", 2 * h + vq % 2, S(8 - 8 * (vq // 2 - h), 136 - 8 * (vq // 2 - h))),
-             A("yg%d" % h, S(256 * (vq % 2) + 128 * (vq // 2), 256 * (vq % 2) + 128 * (vq // 2) + 128)), vq == 0, vq == 3) for vq in range(4)])
+        for q in range(2):
+            act(A("yg", S(256 * q, 256 * q + 256)), IN(A("yw%d" % h), A(lst, S(32 * h + 16 * q, 32 * h + 16 * q + 16))))
+            mm([(Y, A("sel", 2 * vh + q), A("yg", S(256 * q + 128 * vh, 256 * q + 128 * vh + 128)), q + vh == 0, q + vh == 2) for vh in range(2)], q > 0)
 
-    def lists(h, vis):
+    def whole(h, vis):
         tag("cl %d%d" % (vis, h))
-        y = A("pL%d" % h, S(0, 128))
-        if vis:
-            act(A("nr%d" % h), y, AF.Identity, RND1); act(A("nr%d" % h), A("nr%d" % h), AF.Identity, -RND1)
-        ts(A("cl%d" % h), y, 0.25, OP.add)
-        if not vis: ts(A("nr%d" % h), y, RND1, OP.add, -RND1, OP.add)
+        act(A("nr"), Y, AF.Identity, RND); act(A("nr"), A("nr"), AF.Identity, -RND)
+
+    def lists(h, vis, both=True):
+        tag("cl %d%d" % (vis, h))
+        cp(A("cl%d" % h), Y)
+        if both: whole(h, vis)
+
+    def fraction(h, vis):
+        tag("cl %d%d" % (vis, h))
+        tt(A("lam"), Y, A("nr"), OP.subtract)
+
+    def table(h, vis):
+        tag("gm %d%d" % (vis, h))
         act(A("gm%d" % h), IN(A("meta"), A("cl%d" % h)))
-        tt(A("lam%d" % h), y, A("nr%d" % h), OP.subtract)
-        mm([(A("pK%d" % h), A("lam%d" % h), A("wl", S(P_ID, P_ID + 4)), True, False)])
 
-    def gather1(h, vis):
-        tag("g1 %d%d" % (vis, h))
-        tt(A("p%d" % h), IN(A("swin"), A("cl%d" % h)), A("ax%d" % (vis % 2)), OP.mult)
+    def mix(h, vis):
+        tag("mix%d%d" % (vis, h))
+        mm([(A("pB%d" % h, S(128 * (vq % 2), 128 * (vq % 2) + 128), vq // 2), A("mx", vq), A("lam"), True, True) for vq in range(4)])
 
-    def dots1(h, vis):
-        tag("dot1 %d%d" % (vis, h))
-        mm([(A("pK%d" % h, S(0, 2), S(32 * (r // 4), 32 * (r // 4) + 32)), A("p%d" % h, S(r, None, 16)), A("wp", S(2 * (r % 4), 2 * (r % 4) + 2)),
-             False, r == 15) for r in range(16)], True)
+    def stack(h, vis):
+        tag("mix%d%d" % (vis, h))
+        act(A("stk%d" % h), A("pB%d" % h), AF.Relu, C("bs", 11))
 
-    def fields(h, vis, bk, vqs=range(4)):
-        tag("fld%d %d%d" % (bk, vis, h))
-        n = ("pC%d", "pD%d")[bk] % h
-        for vq in vqs:
-            c = S(32 * vq, 32 * vq + 32)
-            mm([(A(n, ALL, c), A("gm%d" % h, S(4 * vq + s, None, 16)), A("wg", S(8 * s + 4 * bk, 8 * s + 4 * bk + 4)), s == 0, False) for s in range(4)]
-               + [(A(n, (S(2, 4), 0)[bk], c), A("lam%d" % h), A("wl", (S(P_T, P_ID + 1), P_U)[bk], S(8 * vq, 8 * vq + 8)), False, True)])
+    def STK(h, vq): return A("stk%d" % h, S(128 * (vq % 2), 128 * (vq % 2) + 128), vq // 2)
 
-    def decide1(h, vis):
-        tag("d1 %d%d" % (vis, h))
-        x = "x%d" % h; dn = "dn%d" % h; sl = "sl%d" % h
-        scan(A(x, ALL, 0), A("r4"), A("pK%d" % h, 0), OP.max)
-        for t in range(3): tt(A(dn, S(t + 1, None, 4)), A(x, S(t, None, 4), 0), A(x, L3, 0), OP.is_equal)
-        for c, f in ((1, 1), (9, 2), (10, 3)): scan(A(x, ALL, c), A(dn), A("pK%d" % h, f), OP.add)
-        for f in (2, 0, 1): scan(A(sl, ALL, 4 + f), A(dn), A("pC%d" % h, f), OP.add)
-        ts(A(sl, L3, 7), A(sl, L3, 6), 1.0, OP.add)
-        ts(X(h, 6, 2), X(h, 0, 2), RNDH, OP.add, -RNDH, OP.add)
-        for vq in range(4): cp(A("zl%d" % h, S(vq, None, 4)), pick(sl, vq, 4))
-        mm([(A("pL%d" % h, S(0, 128)), A("zl%d" % h), IDF, True, True)])
+    def marks(h, vis):
+        tag("mrk%d%d" % (vis, h))
+        mm([(A("pK%d" % h, S(40 * vq, 40 * vq + 40)), STK(h, vq), A("wm", ALL, S(0, 15)), vq == 0, False) for vq in range(4)])
 
-    def D(h, k, s): return A("dt%d" % h, S(3 - k, None, 4), s)
+    def gather(h, vis, k, a=0, b=128):
+        tag("g%d %d%d" % (k, vis, h))
+        c = S(16 * a, 16 * b)
+        tt(A("pq"[k - 1] + str(h), c), IN(A("swin"), A(("cl%d", "l2%d")[k - 1] % h, S(a, b))), A("ax%d" % (vis % 2), c), OP.mult)
 
-    def aside_a(h, vis):
-        tag("offa %d%d" % (vis, h))
-        sl = "sl%d" % h
-        tt(X(h, 2), X(h, 9), X(h, 10), OP.max)
-        tt(X(h, 5), X(h, 9), X(h, 10), OP.min)
-        tt(X(h, 4), X(h, 0), X(h, 6), OP.subtract)
-        tt(X(h, 8), X(h, 1), X(h, 7), OP.subtract)
-        tt(A(sl, L3, 0), A(sl, L3, 4), X(h, 2), OP.add)
-        tt(X(h, 25), X(h, 5), X(h, 4), OP.subtract)
-        tt(X(h, 22), X(h, 2), X(h, 8), OP.max)
-        tt(X(h, 23), X(h, 2), X(h, 8), OP.min)
+    KEYS = (((3, S(1, 3)), (4, S(1, 3)), (0, S(0, 3)), (1, S(1, 3))), ((2, S(0, 3, 2)), None, (3, S(0, 1)), (4, S(0, 1))))
 
-    def aside_c(h, vis):
-        tag("offc %d%d" % (vis, h))
-        sl = "sl%d" % h
-        tt(A(sl, L3, 9), A(sl, L3, 7), X(h, 25), OP.add)
-        tt(X(h, 24), A(sl, L3, 5), X(h, 22), OP.add)
-        tt(X(h, 26), X(h, 23), X(h, 5), OP.subtract)
-        tt(D(h, 2, 0), X(h, 24), A(sl, L3, 0), OP.subtract)
+    def dots(h, vis, k, rs=range(16)):
+        tag("dot%d %d%d" % (k, vis, h))
+        grp = []
+        for r in rs:
+            vq = r // 4; key = KEYS[k - 1][r % 4]
+            if key: o, w = A("pK%d" % h, S(40 * vq + key[0], 40 * vq + 40, 5), key[1]), A("g3", ALL, key[1])
+            else: o, w = A("pK%d" % h, S(40 * vq, 40 * vq + 40), S(0, 2)), A("gx")
+            grp.append((o, A("pq"[k - 1] + str(h), S(r, None, 16)), w, False, k == 2 and r == 15))
+        mm(grp, True)
 
     def list2(h, vis):
         tag("l2 %d%d" % (vis, h))
-        ts(A("l2%d" % h), A("pL%d" % h, S(0, 128)), 0.25, OP.add)
-        act(A("dt%d" % h, L3), A("pC%d" % h, 3))
-        act(D(h, 3, 1), X(h, 25), AF.Identity, 1.0)
+        grp = [(z, 4 * vq + at, 4 * vq + s) for vq in range(4) for z, at, s in (("zu", 0, 0), ("zu", 1, 2), ("zc", 2, 3))]
+        mm([(L2, A(z, S(15 - l, 143 - l)), A("gm%d" % h, S(r, None, 16)), i == 0, i == 11) for i, (z, l, r) in enumerate(grp)])
 
-    def gather2(h, vis, a, b):
-        tag("g2 %d%d" % (vis, h))
-        c = S(16 * a, 16 * b)
-        tt(A("p%d" % h, c), IN(A("swin"), A("l2%d" % h, S(a, b))), A("ax%d" % (vis % 2), c), OP.mult)
+    def list2_v(h, vis):
+        tag("l2 %d%d" % (vis, h))
+        ts(A("l2%d" % h), L2, C("e4", 3), OP.add)
 
-    def sibling(h, vis):
-        scan(A("x%d" % h, ALL, 11), A("dn%d" % h), A("pD%d" % h, 3), OP.add)
-        ts(X(h, 3), X(h, 11), 0.0, OP.not_equal, PEN, OP.mult)
-        k2 = A("pL%d" % h, S(128, 288))
-        mm([(k2, A("idb"), A("kc"), True, False), (k2, IDF, X(h, 1, 5), False, False)])
+    def fields(h, vis, b, vqs=range(4)):
+        tag("fld%d %d%d" % (b, vis, h))
+        n = ("pA%d", "pB%d")[b] % h
+        for vq in vqs:
+            c = S(64 * vq, 64 * vq + 64)
+            grp = [(A(n, c), STK(h, vq), A("wm", ALL, S(16 + 16 * b, 32 + 16 * b)), vq == 0, False)]
+            for s in range(4):
+                f = (0, S(0, None, 2)) if (b, s) in ((0, 2), (0, 3), (1, 1)) else (ALL, ALL)
+                grp.append((A(n, c, f[0]), A("gm%d" % h, S(4 * vq + s, None, 16)), A("wg", ALL, 2 * s + b, f[1]), False, vq == 3 and s == 3))
+            mm(grp, vq > 0)
 
-    def dots2(h, vis):
-        tag("dot2 %d%d" % (vis, h))
-        mm([(A("pL%d" % h, S(129 + 40 * (r // 4) + r % 4, 168 + 40 * (r // 4), 5)), A("p%d" % h, S(r, None, 16)), A("gh"), False, r == 15)
-            for r in range(16)], True)
+    def decide(h, vis):
+        tag("dec%d%d" % (vis, h))
+        k = "pK%d" % h; rn = "rn"; d0 = "d0"; st = "st%d" % h
+        ts(A("nu"), A(k, S(1, 160, 5), 0), PEN, OP.is_ge)
+        for j in (2, 0, 1):
+            c = S(0, 160) if j < 2 else S(159, None, -1)
+            scan(A(rn, c, j), A("r5"), A(k, c, j), OP.max)
+        tt(A(d0, S(4, None, 8)), A(k, S(0, 160, 5), 2), A(rn, S(0, 160, 5), 2), OP.is_lt)
+        tt(A(d0, S(3, None, 8)), A(k, S(1, 160, 5), 2), A(rn, S(1, 160, 5), 2), OP.is_equal)
+        for j in range(2): tt(A(d0, S(1 + j, None, 4)), A(k, S(3 + j, 160, 5), S(0, 2)), A(rn, S(3 + j, 160, 5), S(0, 2)), OP.is_lt)
+        tt(A(d0, S(7, None, 8)), A(d0, S(4, None, 8)), A("nu"), OP.max)
+        for f in range(4):
+            scan(A(st, ALL, f), A(d0), A(("pA%d", "pB%d")[f // 2] % h, ALL, f % 2), OP.add)
+            if f == 2: tt(A(st, S(7, None, 8), 1), A(st, S(7, None, 8), 1), A(st, S(7, None, 8), 0), OP.add)
 
-    def aside_b(h, vis):
-        tag("offb %d%d" % (vis, h))
-        tt(X(h, 12), X(h, 11), X(h, 11), OP.mult)
-        sl = "sl%d" % h
-        for n, c, f in ((sl, 3, 0), ("x%d" % h, 20, 1), ("x%d" % h, 21, 2)): scan(A(n, ALL, c), A("dn%d" % h), A("pD%d" % h, f), OP.add)
-        ts(X(h, 13), X(h, 12), 4194304.0, OP.is_gt, -PEN, OP.mult)
-        tt(A("dt%d" % h, S(2, None, 4)), A(sl, L3, S(0, None, 3)), A("pC%d" % h, 3), OP.subtract)
-        tt(D(h, 2, 1), A(sl, L3, 6), A(sl, L3, 3), OP.subtract)
-        tt(D(h, 2, 2), X(h, 20), X(h, 25), OP.add)
-        tt(X(h, 14), X(h, 6), X(h, 13), OP.add)
-        tt(D(h, 3, 2), X(h, 21), X(h, 25), OP.subtract)
-        cp(D(h, 3, 3), X(h, 21))
-        tt(D(h, 2, 3), X(h, 20), X(h, 26), OP.add)
-
-    def decide2(h, vis):
-        tag("d2 %d%d" % (vis, h))
-        t5 = "t5%d" % h; mk = "mk%d" % h; st = "st%d" % h; pl = "pL%d" % h
-        scan(A(t5), A("r5"), A(pl, S(128, 288)), OP.max)
-        tt(A(mk, L3), X(h, 14), A(pl, S(129, 288, 5)), OP.is_gt)
-        tt(A(mk, S(1, None, 4)), A(t5, S(3, None, 5)), A(t5, S(4, None, 5)), OP.is_equal)
-        tt(A(mk, S(2, None, 4)), A(t5, S(4, None, 5)), A(t5, S(2, None, 5)), OP.is_gt)
-        for s in range(4): scan(A(st, ALL, s), A(mk), A("dt%d" % h, ALL, s), OP.add)
-        zs = "zs%d" % h
-        for vq in range(4): (cp if (h, vis) == (1, 3) else act)(A(zs, S(2 + vq, 34, 4)), pick(st, vq))
-        mm([(A(pl, S(128 + 128 * h, 256 + 128 * h)), A(zs, S(2, 34)), IDF, True, True)])
+    def turn(h, vis):
+        tag("trn%d%d" % (vis, h))
+        for vq in range(4): (cp if (h, vis) == (1, 3) else act)(A("zs", S(vq, None, 4)), A("st%d" % h, S(64 * vq + 7, 64 * vq + 64, 8)))
+        mm([(TN, A("zs"), IDF, True, True)])
         if vis < 3:
-            mm([(A(pl, S(256 - 128 * h, 384 - 128 * h)), A(zs, S(4 - 4 * h, 36 - 4 * h)), IDF, True, True)])
-            act(A("yw%d" % h), A(pl, S(128, 384)))
+            for vh in range(2): act(A("yw%d" % h, S(128 * vh, 128 * vh + 128)), TN, scale=C("hm", 2 + vh))
 
     def keep(h, vis):
         tag("keep%d%d" % (vis, h))
-        ts(A("ml%d" % h), A("pL%d" % h, S(128 + 128 * h, 256 + 128 * h)), 0.25, OP.add)
+        cp(A("ml%d" % h), TN)
 
-    def m_gather(h, vis, split=False):
+    def m_gather(h, vis, a=0, b=128, e=act):
         tag("mg %d%d" % (vis, h))
-        if split:
-            act(A("mg%d" % h, S(0, 1024)), IN(A("mwin"), A("ml%d" % h, S(0, 64))))
-            cp(A("mg%d" % h, S(1024, 2048)), IN(A("mwin"), A("ml%d" % h, S(64, 128))))
-        else: act(A("mg%d" % h), IN(A("mwin"), A("ml%d" % h)))
+        e(A("mg%d" % h, S(16 * a, 16 * b)), IN(A("mwin"), A("ml%d" % h, S(a, b))))
 
-    def m_sum(h, pb, first=True, last=True):
+    def m_sum(h):
         tag("msum%d" % h)
-        mm([(A(pb, S(0, 2)), A("idb"), A("mg%d" % h, S(r, None, 8)), first and r == 0, last and r == 7) for r in range(8)], not first)
+        mm([(A("pM", S(0, 2)), A("idb"), A("mg%d" % h, S(r, None, 8)), h == 0 and r == 0, h == 1 and r == 7) for r in range(8)], h == 1)
 
-    def m_out(k, pb):
+    def m_out(k):
         tag("mout%d" % k)
-        for vh in range(2): (act if k < 3 else cp)(A("ms%d" % k, S(128 * vh, 128 * vh + 128)), A(pb, S(0, 2), S(vh, None, 2)))
+        for vh in range(2): (act if k < 3 else cp)(A("ms%d" % k, S(128 * vh, 128 * vh + 128)), A("pM", S(0, 2), S(vh, None, 2)))
         if k: send(A("ms%d" % k), A("rE%d" % k), [cores[(me - k) % N]], "aE%d" % k)
 
     def places_a(h):
         tag("plc%d" % h)
-        so = "so%d" % h; y = A("st%d" % h, L3)
-        ts(A(so, 0), y, RND1, OP.add, -RND1, OP.add)
+        so = "so%d" % h; y = A("st%d" % h, S(7, None, 8))
+        ts(A(so, 0), y, RND, OP.add, -RND, OP.add)
         tt(A(so, 1), y, A(so, 0), OP.subtract)
-        ts(A(so, 1), A(so, 1), 32768.0, OP.mult)
+        ts(A(so, 1), A(so, 1), 32768.0, OP.mult, -2048.0, OP.add)
+        ts(A(so, 1), A(so, 1), RND * 4096, OP.add, -RND * 4096, OP.add)
         tt(A(so, 2), A(so, 1), A(so, 0), OP.add)
 
     def places_b(h):
         tag("plc%d" % h)
-        so = "so%d" % h; sl = "sl%d" % h
+        so = "so%d" % h; sl = "sl"
 
         def w(k, s): return A(so, k, S(s, None, 4))
         for i in (0, 2):
             tt(w(3, i), w(2, i), w(2, i + 1), OP.max); tt(w(3, i + 1), w(2, i), w(2, i + 1), OP.min)
-        tt(A(sl, L3, 0), w(3, 0), w(3, 2), OP.max); tt(w(0, 0), w(3, 0), w(3, 2), OP.min)
-        tt(w(0, 1), w(3, 1), w(3, 3), OP.max); tt(A(sl, L3, 3), w(3, 1), w(3, 3), OP.min)
-        tt(A(sl, L3, 1), w(0, 0), w(0, 1), OP.max); tt(A(sl, L3, 2), w(0, 0), w(0, 1), OP.min)
-        for vq in range(4): cp(A("zp%d" % (vq // 2), S(2 * h + vq % 2, None, 4)), pick(sl, vq))
+        tt(A(sl, ALL, 0), w(3, 0), w(3, 2), OP.max); tt(w(0, 0), w(3, 0), w(3, 2), OP.min)
+        tt(w(0, 1), w(3, 1), w(3, 3), OP.max); tt(A(sl, ALL, 3), w(3, 1), w(3, 3), OP.min)
+        tt(A(sl, ALL, 1), w(0, 0), w(0, 1), OP.max); tt(A(sl, ALL, 2), w(0, 0), w(0, 1), OP.min)
+        for vq in range(4): cp(A("zp%d" % (vq // 2), S(2 * h + vq % 2, None, 4)), A(sl, S(8 * vq, 8 * vq + 8)))
 
     steps = [(h, vis) for vis in range(4) for h in (0, 1)]
     b1 = (me - 1) % N
-    inherit(0, 0); inherit(1, 0); weights_a()
-    lists(0, 0); gather1(0, 0); weights_b()
-    lists(1, 0); gather1(1, 0)
-    dots1(0, 0); fields(0, 0, 0); decide1(0, 0); dots1(1, 0); fields(0, 0, 1); aside_a(0, 0); list2(0, 0)
-    spread(1)
-    gather2(0, 0, 0, SPLIT); fields(1, 0, 0)
-    tag("choose1"); choose_a(RA, "rl", "ra%d" % b1)
-    cp(A("lkk"), A("rl")); tt(A("lkk"), A("lkk"), A("kof"), OP.add)
-    sibling(0, 0); gather2(0, 0, SPLIT, 128)
-    dots2(0, 0); decide1(1, 0); tag("choose1"); choose_p(); aside_a(1, 0); list2(1, 0)
-    aside_c(0, 0); aside_b(0, 0); decide2(0, 0); fields(1, 0, 1)
-    tag("choose1"); choose_b("ri%d" % b1)
-    send(A("ri%d" % b1), A("ri%d" % b1), [cores[(me + 1) % N], cores[(me + 2) % N]], "aI%d" % b1)
-    inherit(0, 1); gather2(1, 0, 0, SPLIT); lists(0, 1); keep(0, 0); sibling(1, 0); m_gather(0, 0); gather2(1, 0, SPLIT, 128)
-    spread(2)
-    for i in range(2, 9):
+    tag("choose0"); choose_b("il"); first_cuts(); mask((2, 3)); mask_p(range(4, 8))
+    inherit(0, 0); mask((4, 5, 6)); lists(0, 0); mask((7,)); fraction(0, 0); mix(0, 0); inherit(1, 0); stack(0, 0); whole(1, 0); table(0, 0)
+    gather(0, 0, 1); marks(0, 0); spread(1); lists(1, 0, False); fraction(1, 0); weights_b()
+    tag("choose1"); choose_a(RA, "rl", "ra%d" % b1); cp(A("lkk"), A("rl")); tt(A("lkk"), A("lkk"), A("kof"), OP.add)
+    dots(0, 0, 1, range(8)); list2(0, 0); dots(0, 0, 1, range(8, 16)); mix(1, 0); list2_v(0, 0); gather(0, 0, 2)
+    weights_c(); tag("choose1"); choose_p(); table(1, 0); fields(0, 0, 0)
+    for i in range(1, 9):
         now = steps[i] if i < 8 else None
         old = steps[i - 1]
         nxt = steps[i + 1] if i < 7 else None
-        if now: gather1(*now)
-        if i == 8: places_a(0)
-        dots2(*old)
-        if now:
-            fields(*now, 0, (0, 1)); dots1(*now); fields(*now, 0, (2, 3))
-        if i == 8: m_sum(0, "pD0", last=False)
-        aside_c(*old); aside_b(*old); decide2(*old)
-        if now:
-            decide1(*now); fields(*now, 1, (0, 1))
+        if now: gather(*now, 1); stack(*now)
+        else: places_a(0)
+        dots(*old, 2)
+        if now: fields(*old, 1); list2(*now); marks(*now); dots(*now, 1, range(DOTS[0]))
+        if i == 1:
+            tag("choose1"); choose_b("ri%d" % b1)
+            send(A("ri%d" % b1), A("ri%d" % b1), [cores[(me + 1) % N], cores[(me + 2) % N]], "aI%d" % b1)
+        else: m_gather(*steps[i - 2], MSPLIT, 128)
+        if i == 8: m_sum(1); m_out(2); m_sum(0)
+        decide(*old)
+        if now: list2_v(*now)
+        turn(*old)
+        if now: dots(*now, 1, range(DOTS[0], DOTS[1])); gather(*now, 2, 0, CUTS[0])
+        keep(*old)
         if nxt: inherit(*nxt)
-        if now:
-            fields(*now, 1, (2, 3)); aside_a(*now); list2(*now)
-        if i % 2: m_sum(0, "pD0", last=False)
-        if i == 7:
-            keep(*old); m_gather(*old); m_sum(1, "pD0", first=False); m_out(2, "pD0")
-        if now: gather2(*now, 0, SPLIT)
-        if nxt: lists(*nxt)
-        if i != 7: keep(*old)
-        if now: sibling(*now)
-        if i in (3, 5): m_sum(1, "pD0", first=False)
-        if i < 7: m_gather(*old)
-        if i in (3, 5): m_out((i - 3) // 2, "pD0")
-        if now: gather2(*now, SPLIT, 128)
-        if i == 3: spread(3)
-    m_gather(1, 3, True)
-    m_sum(1, "pD0", first=False); places_a(1); m_out(3, "pD0")
+        if now: gather(*now, 2, CUTS[0], CUTS[1]); dots(*now, 1, range(DOTS[1], 16))
+        if i < 8: m_gather(*old, 0, MSPLIT)
+        if nxt: lists(*nxt); table(*nxt)
+        if i == 7: fields(*now, 0); fields(*now, 1)
+        if 2 <= i < 7: m_sum(i % 2)
+        if now: gather(*now, 2, CUTS[1], 128)
+        if nxt: fraction(*nxt); fields(*now, 0); mix(*nxt)
+        if i in (3, 5): m_out((i - 3) // 2)
+        if i in (1, 3): spread(2 + i // 2)
+    m_gather(1, 3, 0, 64); m_gather(1, 3, 64, 128, cp)
+    m_sum(1); places_a(1); m_out(3)
     places_b(0); places_b(1)
     tag("out")
-    for vh in range(2): mm([(A("pK0", vh), A("zp%d" % vh), IDF, True, True)])
-    act(A("ycs"), A("pK0", S(0, 2)), AF.Identity, A("xv", S(13, 14)))
+    for vh in range(2): mm([(A("pL", S(128 * vh, 128 * vh + 128)), A("zp%d" % vh), IDF, True, True)])
+    ts(C("bs", 20), C("pf", 2), 4096.0, OP.mult, -12288.0, OP.add)
+    act(A("ycs"), A("pL", S(0, 256)), AF.Identity, C("bs", 20))
     dma("Y", [(H(T.yc[:, :]), A("ycs"))], "dyc")
     tt(A("acc"), A("ms0"), A("rE1"), OP.add)
     tt(A("acc"), A("acc"), A("rE2"), OP.add)
-    tt(A("pC0", S(0, 2)), A("acc"), A(RA), OP.mult); cp(A("pC1", S(0, 2)), A(RA))
+    tt(A("pA0", ALL, 0), A("acc"), A(RA), OP.mult); cp(A("pA1", ALL, 0), A(RA))
     for h in (0, 1):
         c = S(h * 128, h * 128 + 128)
         cp(A("acc", c), A("rE3", c))
-        tt(A("ms0", c), A("acc", c), A("pC1", h), OP.mult)
-        tt(A("yes", c), A("ms0", c), A("pC0", h), OP.add)
+        tt(A("ms0", c), A("acc", c), A("pA1", c, 0), OP.mult)
+        tt(A("yes", c), A("ms0", c), A("pA0", c, 0), OP.add)
         dma("YS"[h], [(H(T.ye[:, c]), A("yes", c))], "dye%d" % h)
 
     need("G", [(s, cnt[s]) for s in cnt])

@@ -6,26 +6,28 @@ OP = AluOpType
 AF = ActivationFunctionType
 RND = 12582912.0
 PEN = 2097152.0
-CUTS = (40, 104)
+FIRST = 24
+LASTCUT = 56
+MASK_V = range(8)
 KCUT = 88
+CUT = 88
 MSPLIT = 40
-DOTS = (3, 9)
-MASK_V = (0, 1, 2, 3, 4, 5, 6, 7)
+DOTS = 8
 TAG = [""]
 
 F32, B16, I32, U16 = "float32", "bfloat16", "int32", "uint16"
 SCRATCH = {
     "kl": ("sbuf", [128, 256], I32), "ul": ("sbuf", [128, 256], I32),
     "ytk": ("sbuf", [128, 2, 8, 16], I32), "xk": ("sbuf", [128, 256], F32), "zk": ("sbuf", [128, 256], F32),
-    "lstk": ("sbuf", [128, 256], U16), "db": ("sbuf", [128, 5, 256], B16), "dp": ("sbuf", [128, 6, 128], B16),
+    "lstk": ("sbuf", [128, 256], U16), "db": ("sbuf", [128, 5, 256], B16), "dp": ("sbuf", [128, 8, 128], B16),
     "lki": ("sbuf", [128, 64], I32), "lku": ("sbuf", [128, 64], U16), "lkk": ("sbuf", [128, 64], F32), "kof": ("sbuf", [128, 64], F32),
     "a0b": ("sbuf", [128, 256], B16), "il": ("sbuf", [128, 64], U16), "rl": ("sbuf", [128, 64], U16),
     "swin": ("sbuf", [128, 4096], B16), "mwin": ("sbuf", [128, 4096], B16), "cwin": ("sbuf", [128, 2048], B16),
-    "meta": ("sbuf", [128, 4096], B16), "inn": ("sbuf", [128, 4096], B16),
+    "meta": ("sbuf", [128, 4096], B16),
     "ax0": ("sbuf", [128, 2048], B16), "ax1": ("sbuf", [128, 2048], B16),
     "df": ("sbuf", [128, 1024], B16), "dabs": ("sbuf", [128, 1024], B16),
-    "yg": ("sbuf", [128, 512], F32), "nr": ("sbuf", [128, 128], F32), "lam": ("sbuf", [128, 128], B16), "rn": ("sbuf", [128, 160, 3], F32),
-    "d0": ("sbuf", [128, 256], F32), "zs": ("sbuf", [128, 32, 4], F32), "sl": ("sbuf", [128, 32, 4], F32), "nu": ("sbuf", [128, 32], F32),
+    "yg": ("sbuf", [128, 512], F32), "nr": ("sbuf", [128, 128], I32), "lam": ("sbuf", [128, 128], B16), "rn": ("sbuf", [128, 160, 3], F32),
+    "d0": ("sbuf", [128, 256], F32), "zs": ("sbuf", [128, 32, 4], F32), "sl": ("sbuf", [128, 32, 4], F32),
     "kd": ("sbuf", [128, 4, 4, 16], F32), "km": ("sbuf", [128, 4, 2, 16], F32), "ki": ("sbuf", [128, 128], I32),
     "xc": ("sbuf", [128, 4, 64], I32), "xh": ("sbuf", [128, 4, 64], I32), "xy": ("sbuf", [128, 4, 64], F32), "xi": ("sbuf", [128, 4, 64], I32),
     "xw": ("sbuf", [128, 20, 64], F32), "xo": ("sbuf", [128, 4, 64], F32), "xz": ("sbuf", [128, 4, 64], F32), "xl": ("sbuf", [128, 64], U16),
@@ -37,8 +39,9 @@ SCRATCH = {
     "vg": ("sbuf", [128, 8, 9, 2], F32), "dg": ("sbuf", [128, 8, 8, 2], F32), "wg": ("sbuf", [128, 8, 8, 16], B16),
     "vm": ("sbuf", [128, 2, 9, 2], F32), "dm": ("sbuf", [128, 48], F32), "wm": ("sbuf", [128, 8, 48], B16),
     "jj": ("sbuf", [128, 8, 8], F32), "sel": ("sbuf", [128, 4, 8, 16], F32), "sq": ("sbuf", [128, 4, 144], F32),
-    "zq": ("sbuf", [128, 4, 144], B16), "zu": ("sbuf", [128, 144], B16), "zc": ("sbuf", [128, 146], B16), "wi": ("sbuf", [128, 128], B16),
-    "hb": ("sbuf", [128, 16], F32), "nb": ("sbuf", [128, 2, 256], B16), "r5": ("sbuf", [128, 160], F32),
+    "zq": ("sbuf", [128, 4, 144], B16), "zu": ("sbuf", [128, 144], B16), "zc": ("sbuf", [128, 146], B16), "idn": ("sbuf", [128, 128], B16),
+    "wi": ("sbuf", [128, 128], B16), "inn": ("sbuf", [128, 4096], B16), "nu": ("sbuf", [128, 32], F32),
+    "hb": ("sbuf", [128, 16], F32), "nb": ("sbuf", [128, 3, 256], B16), "ds": ("sbuf", [128, 2, 128, 2], B16), "r5": ("sbuf", [128, 160], F32),
     "ycs": ("sbuf", [128, 256], F32), "acc": ("sbuf", [128, 256], F32), "yes": ("sbuf", [128, 256], F32),
     "pL": ("psum", [128, 512], F32), "pM": ("psum", [128, 4, 128], F32),
 }
@@ -64,10 +67,10 @@ ALL = slice(None)
 def S(a, b=None, c=None): return slice(a, b, c)
 
 
-KID, UP, NODE, KKL, KKR = 0, 1, 2, 4, 5
+KID, UP, NODE, SKID, KKL, KKR, SIB = range(7)
 NODES = [(S(0, 2), S(0, 1), 3, KID), (S(0, 2), S(1, 2), 3, KKL), (S(0, 2), S(2, 3), 3, KKR), (S(0, 2), S(4, 8, 3), 2, KID), (S(0, 2), S(5, 6), 0, KID),
-         (S(0, 2), S(6, 7), 1, KID), (S(0, 1), S(3, 4), 0, NODE), (S(1, 2), S(3, 4), 1, NODE),
-         (S(2, 3), S(0, 4, 3), 2, NODE), (S(2, 3), S(1, 3), 3, KID), (S(2, 3), S(4, 5), 3, NODE), (S(2, 3), S(5, 6), 1, NODE), (S(2, 3), S(6, 7), 0, NODE),
+         (S(0, 2), S(6, 7), 0, SKID), (S(0, 1), S(3, 4), 0, NODE), (S(1, 2), S(3, 4), 1, NODE),
+         (S(2, 3), S(0, 4, 3), 2, NODE), (S(2, 3), S(1, 3), 3, KID), (S(2, 3), S(4, 5), 3, NODE), (S(2, 3), S(5, 6), 0, SIB), (S(2, 3), S(6, 7), 0, NODE),
          (S(2, 3), S(7, 8), 0, UP), (S(3, 4), S(0, 8, 4), 0, UP), (S(3, 4), S(1, 3), 2, UP), (S(3, 4), S(5, 7), 2, UP), (S(3, 4), S(3, 8, 4), 3, NODE)]
 
 
@@ -220,13 +223,13 @@ def rank_program(g, core, T, topo):
     gsel(A("gi"), A("gi"), [[16, 8]], 15, -1, OP.is_ge, 0.0)
     gsel(A("m32"), A("one", S(0, 32)), [[-4, 4], [-16, 8]], 0, 1, OP.is_ge, 0.0)
     gsel(A("m32"), A("m32"), [[4, 4], [16, 8]], 3, -1, OP.is_ge, 0.0)
-    iota(A("kof"), [[256, 4], [0, 16]], 0, 0)
+    iota(A("kof"), [[256, 4], [0, 16]], 0, 0); iota(A("nb", 2), [[2, 128], [-1, 2]], 1, 0)
     gsel(A("idf"), A("one", S(0, 144)), [[-1, 144]], 8, 1, OP.is_equal, 0.0)
     gsel(A("wi"), A("one", S(0, 128)), [[-1, 8], [0, 16]], 0, 1, OP.is_equal, 0.0)
     gsel(A("jj"), A("one", S(0, 64)), [[-16, 8], [-1, 8]], 0, 1, OP.is_equal, 0.0)
     gsel(A("jj"), A("jj"), [[-16, 8], [-1, 8]], -8, 1, OP.not_equal, 1.0)
     tag("static")
-    act(C("hb", 0), C("pf", 0), scale=256.0); spreadcol(A("nb", 1), C("hb", 0))
+    act(C("hb", 0), C("pf", 0), scale=256.0); spreadcol(A("nb", 1), C("hb", 0)); axpy(C("fc", SIB), 1, E(12), E(5))
     act(A("zq", ALL, S(15, 128, 16)), A("m32"), scale=1024.0)
     act(A("zu", S(15, 128, 16)), A("gi"), scale=C("fc", UP))
 
@@ -249,29 +252,32 @@ def rank_program(g, core, T, topo):
     act(A("gx", ALL, 1, 0), A("gi")); act(A("gx", ALL, 2, 1), A("gi"))
     for k in range(8): act(A("wm", k, S(0, 15)), A("dm", S(0, 15)), scale=C("gi", k))
     for k in range(4): act(A("sq", k), A("idf"), scale=C("e4", k))
-    act(A("idb"), A("idf", S(8, 136)))
+    act(A("idb"), A("idf", S(8, 136))); act(A("idn"), A("idf", S(8, 136)), scale=-1.0)
     for vq in range(4):
         c = 4 * (vq % 2); act(A("sel", vq, ALL, S(8 * (vq // 2) + c, 8 * (vq // 2) + c + 4)), A("jj", ALL, S(c, c + 4)))
 
-    tag("weights")
-    axpy(B(HB), 1, E(5), E(3)); axpy(B(LB), -1, E(5), E(2))
-    act(B(T1), E(11), scale=7 / 16); act(B(C2), E(11), scale=2 / 64)
-    axpy(B(CN), 3 / 64, E(11), E(0)); axpy(B(CT), 1 / 64, E(11), E(2)); axpy(B(C3), 3 / 64, E(11), E(3))
-    axpy(B(H3), -1, E(6), B(T1)); axpy(B(T1), 1, B(HA), E(2))
     def V(f, e): return A("vm", f // 2, e, S(f % 2, f % 2 + 1))
-    axpy(V(0, 3), -1 / 64, E(10), B(CN)); axpy(V(0, 4), 1 / 64, E(9), B(CT)); axpy(B(C3), -1 / 64, E(9), B(C3)); axpy(B(L3), -1, B(H3), B(T1))
-    for e, x in ((1, E(3)), (2, B(LA)), (5, E(0)), (6, E(1)), (7, E(2))): axpy(V(0, e), 1, x, B(C2))
-    axpy(B(C3), -2 / 64, E(8), B(C3)); axpy(A("bs", S(LA1, LA1 + 3)), 1, A("bs", S(LA, LA + 3)), E(11))
+    tag("weights")
     for f, e, s, fld in NODES:
         spreadcol(A("vg", 2 * s + f.start // 2, e, S(f.start % 2, (f.stop - 1) % 2 + 1)), C("fc", fld))
-    axpy(V(0, 0), 2 / 64, E(7), B(C3))
-    for f, e, x in ((1, S(0, 8, 4), B(LA1)), (1, S(7, 8), B(LA1)), (1, S(1, 3), B(L31)), (1, S(3, 4), E(1)), (1, S(5, 7), B(LB1)),
-                    (2, S(0, 4, 3), E(2)), (2, S(1, 2), B(LA1)), (2, S(2, 5, 2), E(3)), (2, S(5, 6), E(1)), (2, S(6, 7), E(0)), (2, S(7, 8), B(HA)),
-                    (3, S(0, 8, 4), B(HA)), (3, S(1, 3), B(H3)), (3, S(3, 8, 4), E(3)), (3, S(5, 7), B(HB))): spreadcol(V(f, e), x)
 
-    def grandchildren(a, b):
+    def weights_a():
+        tag("weights")
+        axpy(B(HB), 1, E(5), E(3)); axpy(B(LB), -1, E(5), E(2))
+        act(B(T1), E(11), scale=7 / 16); act(B(C2), E(11), scale=2 / 64)
+        axpy(B(CN), 3 / 64, E(11), E(0)); axpy(B(CT), 1 / 64, E(11), E(2)); axpy(B(C3), 3 / 64, E(11), E(3))
+        axpy(B(H3), -1, E(6), B(T1)); axpy(B(T1), 1, B(HA), E(2))
+        axpy(V(0, 3), -1 / 64, E(10), B(CN)); axpy(V(0, 4), 1 / 64, E(9), B(CT)); axpy(B(C3), -1 / 64, E(9), B(C3)); axpy(B(L3), -1, B(H3), B(T1))
+        for e, x in ((1, E(3)), (2, B(LA)), (5, E(0)), (6, E(1)), (7, E(2))): axpy(V(0, e), 1, x, B(C2))
+        axpy(B(C3), -2 / 64, E(8), B(C3)); axpy(A("bs", S(LA1, LA1 + 3)), 1, A("bs", S(LA, LA + 3)), E(11))
+        for f, e, x in ((1, S(3, 4), E(1)), (2, S(0, 4, 3), E(2)), (2, S(2, 5, 2), E(3)), (2, S(5, 6), E(1)), (2, S(6, 7), E(0)), (2, S(7, 8), B(HA)),
+                        (3, S(0, 8, 4), B(HA)), (3, S(1, 3), B(H3)), (3, S(3, 8, 4), E(3)), (3, S(5, 7), B(HB)), (1, S(0, 8, 4), B(LA1)),
+                        (1, S(7, 8), B(LA1)), (1, S(1, 3), B(L31)), (1, S(5, 7), B(LB1)), (2, S(1, 2), B(LA1))): spreadcol(V(f, e), x)
+        axpy(V(0, 0), 2 / 64, E(7), B(C3))
+
+    def grandchildren(a, b, e=act):
         tag("kk")
-        act(A("meta", S(16 * a, 16 * b)), IN(A("cwin"), A("lstk", S(a, b))))
+        e(A("meta", S(16 * a, 16 * b)), IN(A("cwin"), A("lstk", S(a, b))))
 
     def spread(vis):
         tag("spread")
@@ -284,9 +290,9 @@ def rank_program(g, core, T, topo):
     for j in range(2): cp(A("dp", 4 + j), A("db", 2 + j, S(0, None, 2)))
     dma("Y", [(A("cwin", rows=S(2 + j, None, 16)), A("dp", 4 + j)) for j in range(2)], "dcu", True)
     cp(A("db", 1), A("kl")); tt(A("db", 0), A("kl"), A("db", 1), OP.subtract)
+    ts(A("db", 4), A("kl"), 0, OP.is_lt, -256.0, OP.mult)
     for j in range(4): cp(A("dp", j), A("db", j % 2, S(j // 2, None, 2)))
     dma("Y", [(A("cwin", rows=S(8 + j, None, 16)), A("dp", j)) for j in range(4)], "dcw", True)
-    ts(A("db", 4), A("kl"), 0, OP.is_lt, -256.0, OP.mult)
     dma("Y", [(A("inn", rows=S(0, 8)), A("db", 4))], "dm0")
     dma("Y", [(A("swin", S(0, 2048)), H(T.s[:, 0:2048]))], "dss")
     dma("Y", [(A("swin", S(2048, 4096)), H(T.s[:, 2048:4096]))], "dm3")
@@ -294,10 +300,10 @@ def rank_program(g, core, T, topo):
     for b in range(8):
         cp(A("xk", S(32 * b, 32 * b + 32)), A("ytk", ALL, b))
     op("V", [lambda: g.vector.transpose(out=T.zk[:, :], in_=T.xk[:, :])], [A("xk")], [A("zk")])
+    cp(A("lku"), A("lki"))
     for b in range(8):
         ts(A("lstk", S(b, None, 8)), A("zk", S(32 * b, 32 * b + 32)), 0.5, OP.mult)
-    grandchildren(0, KCUT)
-    cp(A("lku"), A("lki"))
+    tt(A("lkk"), A("lki"), A("kof"), OP.add)
     send(A(RA), A(RA), peers, "aA%d" % me)
     send(A("lku"), A("rl"), [cores[(me + 1) % N]], "aL")
     spread(0)
@@ -305,32 +311,47 @@ def rank_program(g, core, T, topo):
     gsel(A("r5"), A("one", S(0, 160)), [[0, 32], [1, 5]], 0, 0, OP.is_gt, 0.0)
     iota(A("d0", S(0, None, 8)), [[0, 32]], 0, 0)
 
-    tag("cut0")
     def W(k, n=1): return A("xw", S(k, k + n))
-    ts(A("xh"), A("xc"), 1, SR)
-    for t in range(4): ts(A("xy", t), A("xc", t), (7 - 2 * t) / 16, OP.add)
-    for k, (i, j) in enumerate(((0, 2), (0, 3), (0, 1), (1, 3), (1, 2), (2, 3))): tt(W(k), A("xh", i), A("xh", j), OP.is_equal)
-    tt(W(6, 2), W(0, 2), W(3, 2), OP.max)
-    tt(W(8), A("xy", 2), A("xy", 1), OP.subtract); tt(W(9), A("xy", 3), A("xy", 1), OP.subtract)
-    tt(W(10), W(0), W(1), OP.max); tt(W(11), W(3), W(4), OP.max)
-    tt(W(8, 2), W(8, 2), W(6, 2), OP.mult)
-    tt(W(10, 2), W(10, 2), A("xw", S(2, 6, 3)), OP.max)
-    cp(A("xo", 0), A("xy", 0)); tt(W(12), A("xy", 1), W(8), OP.add)
-    tt(A("xo", S(2, 4)), A("xy", S(2, 4)), W(8, 2), OP.subtract)
-    tt(A("xo", 1), W(12), W(9), OP.add)
-    tt(W(13), W(11), W(10), OP.is_gt)
-    tt(W(14, 2), A("xo", S(2, 4)), A("xo", S(0, 2)), OP.subtract)
-    for j in range(2): tt(W(14 + j), W(14 + j), W(13), OP.mult)
-    tt(A("xz", S(0, 2)), A("xo", S(0, 2)), W(14, 2), OP.add); tt(A("xz", S(2, 4)), A("xo", S(2, 4)), W(14, 2), OP.subtract)
-    cp(A("xi"), A("xz")); ts(A("xh"), A("xi"), 1, SR); cp(A("xl"), A("xh", 0))
-    act(A("mg0", S(0, 1024)), IN(A("cwin"), A("xl")))
+    def P(k, n=1): return A("pB0", S(64 * (k % 4), 64 * (k % 4 + n)), k // 4)
+
+    def pairs_first():
+        tag("cut0")
+        ts(A("xh"), A("xc"), 1, SR)
+        for t in range(4): ts(A("xy", t), A("xc", t), (7 - 2 * t) / 16, OP.add)
+        for o, i, j in ((P(0), 0, 2), (P(1), 0, 3), (P(2), 2, 3), (W(0), 1, 3), (W(1), 1, 2), (W(2), 0, 1)): tt(o, A("xh", i), A("xh", j), OP.is_equal)
+        tt(W(8), A("xy", 2), A("xy", 1), OP.subtract); tt(W(9), A("xy", 3), A("xy", 1), OP.subtract)
+        tt(P(4, 2), P(0, 2), W(0, 2), OP.max)
+        tt(W(3), W(2), P(0), OP.max); tt(P(3), P(2), W(0), OP.max)
+        tt(P(6, 2), W(8, 2), P(4, 2), OP.mult)
+        tt(W(10), W(3), P(1), OP.max); tt(P(2), P(3), W(1), OP.max)
+        tt(W(12), A("xy", 1), P(6), OP.add); tt(A("xo", S(2, 4)), A("xy", S(2, 4)), P(6, 2), OP.subtract)
+        tt(P(0), P(2), W(10), OP.is_gt)
+        tt(A("xy", 1), W(12), P(7), OP.add)
+        tt(W(14), A("xo", 2), A("xy", 0), OP.subtract); tt(W(15), A("xo", 3), A("xy", 1), OP.subtract)
+        for j in range(2): tt(P(4 + j), W(14 + j), P(0), OP.mult)
+        tt(P(3), P(2), W(10), OP.max); tt(W(11), P(2), W(10), OP.mult)
+        tt(A("xz", S(0, 2)), A("xy", S(0, 2)), P(4, 2), OP.add); tt(A("xz", S(2, 4)), A("xo", S(2, 4)), P(4, 2), OP.subtract)
+        ts(A("xh", 0), A("xz", 0), 0.5, OP.mult, -0.25, OP.add); ts(W(11), W(11), 2 / 64, OP.mult, 1 / 64, OP.add)
+        cp(A("xl"), A("xh", 0)); ts(A("xh", S(2, 4)), A("xz", S(2, 4)), 0.5, OP.mult, -0.25, OP.add)
+        act(A("mg0", S(0, 1024)), IN(A("cwin"), A("xl")))
+        mm([(A("pL", S(0, 64)), A("zu", S(15 - l, 143 - l)), A("mg0", S(l, 1024, 16)), l == 0, l == 15) for l in range(16)])
+
+    def uncle_next():
+        tag("cut0b")
+        ts(A("xi", 1), A("pL", S(0, 64)), 0.5, OP.mult, -0.25, OP.add)
+        tt(W(4), A("xz", 3), A("xz", 2), OP.subtract)
+        tt(P(1), A("xi", 1), A("xh", 3), OP.is_equal); tt(W(2), A("xi", 1), A("xh", 2), OP.is_equal)
+        tt(P(4), W(4), P(1), OP.mult); tt(W(5), W(2), P(1), OP.add)
+        tt(A("xo", 2), A("xz", 2), P(4), OP.add); ts(P(5), W(5), 1 / 64, OP.mult); tt(A("xo", 3), A("xz", 3), P(4), OP.subtract)
+        tt(W(6), W(11), P(5), OP.add); cut_rows((2, 3))
+        tt(P(6), W(6), P(3), OP.mult); tt(A("xo", 0), A("xz", 0), P(6), OP.add); cut_rows((0,))
 
     def choose_a(kept, lk, a):
         for k in range(4):
             tt(A("df", S(256 * k, 256 * k + 256)), IN(A(kept), A(lk, S(16 * k, 16 * k + 16))), A(a), OP.subtract)
+        act(A("dabs"), A("df"), AF.Abs)
 
     def choose_p():
-        act(A("dabs"), A("df"), AF.Abs)
         for q in range(4):
             mm([(A("pM", q, S(0, 64)), A("zq", q, S(15 - l, 143 - l)), A("dabs", S(l, None, 16)), l == 0, l == 15) for l in range(16)])
 
@@ -341,7 +362,16 @@ def rank_program(g, core, T, topo):
         ts(A("ki", S(64, 128)), A("ki", S(0, 64)), 255, AND)
         cp(A(out), A("ki", S(64, 128)))
 
-    def mask_bank(k): return A(("pA0", "pB0", "pA1", "pB1")[k % 4])
+    def choose_s(kept, lk, a):
+        act(A("df"), IN(A(kept), A(lk)))
+        for k in range(4):
+            o = A(("pA1", "pB1")[k // 2], ALL, k % 2)
+            mm([(o, A("idb"), A("df", S(256 * k, 256 * k + 256)), True, False), (o, A("idn"), A(a), False, True)])
+
+    def choose_abs():
+        for k in range(4): act(A("dabs", S(256 * k, 256 * k + 256)), A(("pA1", "pB1")[k // 2], ALL, k % 2), AF.Abs)
+
+    def mask_bank(k): return A(("pA0", "pA1", "pB1")[k % 3])
 
     def mask_p(ks):
         tag("mask")
@@ -362,31 +392,12 @@ def rank_program(g, core, T, topo):
         mm([(A("pL", S(256 + 64 * w, 320 + 64 * w)), A("sq", w, S(8 + w - s, 136 + w - s)), A("xz" if s == 1 else "xo", s), (s, w) == (1, 0), (s, w) == (0, 3))
             for s in slots for w in range(4)], slots[0] != 1)
 
-    tag("choose0")
-    choose_a("a0b", "lku", RA)
-    mask_p(range(4))
-    tag("cut0")
-    mm([(A("pL", S(0, 64)), A("zu", S(15 - l, 143 - l)), A("mg0", S(l, 1024, 16)), l == 0, l == 15) for l in range(16)])
-    mask((0, 1))
-    tag("choose0")
-    choose_p()
-    grandchildren(KCUT, 256)
-    dma("Y", [(A("meta", rows=S(j, None, 16)), A("db", j) if j < 4 else A("nb", j - 4)) for j in range(6)], "dm1")
-    dma("Y", [(A("mwin"), H(T.m[:, :]))], "dmm")
-
-    tag("cut0b")
-    cp(A("xi", 0), A("pL", S(0, 64))); ts(A("xi", 1), A("xi", 0), 1, SR)
-    tt(W(0), W(10), W(11), OP.max); tt(W(1), W(10), W(11), OP.mult)
-    tt(W(2), A("xi", 1), A("xh", 2), OP.is_equal); tt(W(3), A("xi", 1), A("xh", 3), OP.is_equal)
-    tt(W(4), A("xz", 3), A("xz", 2), OP.subtract)
-    ts(W(1), W(1), 2.0, OP.mult, 1.0, OP.add)
-    tt(W(5), W(2), W(3), OP.add); tt(W(4), W(4), W(3), OP.mult)
-    tt(W(5), W(5), W(1), OP.add)
-    tt(A("xo", 2), A("xz", 2), W(4), OP.add); tt(A("xo", 3), A("xz", 3), W(4), OP.subtract)
-    tt(W(5), W(5), W(0), OP.mult); ts(W(5), W(5), 1 / 64, OP.mult); tt(A("xo", 0), A("xz", 0), W(5), OP.add)
-    cut_rows((1, 2, 3)); cut_rows((0,))
-    tag("choose0")
-    tt(A("lkk"), A("lki"), A("kof"), OP.add)
+    def table_rows():
+        tag("kk")
+        for j in range(2): cp(A("ds", j, ALL, S(None, None, -1)), A("db", j))
+        rows = [A("db", j) for j in range(4)] + [A("nb", 0), A("nb", 1), A("ds", 0), A("ds", 1), A("nb", 2)]
+        dma("Y", [(A("meta", rows=S(j if j < 8 else 12, None, 16)), x) for j, x in enumerate(rows)], "dm1")
+        dma("Y", [(A("mwin"), H(T.m[:, :]))], "dmm")
 
     def first_cuts():
         tag("first")
@@ -414,14 +425,9 @@ def rank_program(g, core, T, topo):
             act(A("yg", S(256 * q, 256 * q + 256)), IN(A("yw%d" % h), A(lst, S(32 * h + 16 * q, 32 * h + 16 * q + 16))))
             mm([(Y, A("sel", 2 * vh + q), A("yg", S(256 * q + 128 * vh, 256 * q + 128 * vh + 128)), q + vh == 0, q + vh == 2) for vh in range(2)], q > 0)
 
-    def whole(h, vis):
+    def lists(h, vis):
         tag("cl %d%d" % (vis, h))
-        act(A("nr"), Y, AF.Identity, RND); act(A("nr"), A("nr"), AF.Identity, -RND)
-
-    def lists(h, vis, both=True):
-        tag("cl %d%d" % (vis, h))
-        cp(A("cl%d" % h), Y)
-        if both: whole(h, vis)
+        cp(A("cl%d" % h), Y); cp(A("nr"), Y)
 
     def fraction(h, vis):
         tag("cl %d%d" % (vis, h))
@@ -477,12 +483,12 @@ def rank_program(g, core, T, topo):
         for vq in vqs:
             c = S(64 * vq, 64 * vq + 64)
             grp = [(A(n, c), STK(h, vq), A("wm", ALL, S(16 + 16 * b, 32 + 16 * b)), vq == 0, False)]
-            for s in range(4):
-                f = (0, S(0, None, 2)) if (b, s) in ((0, 2), (0, 3), (1, 1)) else (ALL, ALL)
+            for s in ((0, 1, 2, 3), (0, 2, 3))[b]:
+                f = (ALL, ALL) if b or s == 0 else (1, S(1, None, 2)) if s == 1 else (0, S(0, None, 2))
                 grp.append((A(n, c, f[0]), A("gm%d" % h, S(4 * vq + s, None, 16)), A("wg", ALL, 2 * s + b, f[1]), False, vq == 3 and s == 3))
             mm(grp, vq > 0)
 
-    def decide(h, vis):
+    def decide(h, vis, between=None):
         tag("dec%d%d" % (vis, h))
         k = "pK%d" % h; rn = "rn"; d0 = "d0"; st = "st%d" % h
         ts(A("nu"), A(k, S(1, 160, 5), 0), PEN, OP.is_ge)
@@ -491,8 +497,10 @@ def rank_program(g, core, T, topo):
             scan(A(rn, c, j), A("r5"), A(k, c, j), OP.max)
         tt(A(d0, S(4, None, 8)), A(k, S(0, 160, 5), 2), A(rn, S(0, 160, 5), 2), OP.is_lt)
         tt(A(d0, S(3, None, 8)), A(k, S(1, 160, 5), 2), A(rn, S(1, 160, 5), 2), OP.is_equal)
-        for j in range(2): tt(A(d0, S(1 + j, None, 4)), A(k, S(3 + j, 160, 5), S(0, 2)), A(rn, S(3 + j, 160, 5), S(0, 2)), OP.is_lt)
         tt(A(d0, S(7, None, 8)), A(d0, S(4, None, 8)), A("nu"), OP.max)
+        for j in range(2): tt(A(d0, S(1 + j, None, 4)), A(k, S(3 + j, 160, 5), S(0, 2)), A(rn, S(3 + j, 160, 5), S(0, 2)), OP.is_lt)
+        if between: between()
+        tag("dec%d%d" % (vis, h))
         for f in range(4):
             scan(A(st, ALL, f), A(d0), A(("pA%d", "pB%d")[f // 2] % h, ALL, f % 2), OP.add)
             if f == 2: tt(A(st, S(7, None, 8), 1), A(st, S(7, None, 8), 1), A(st, S(7, None, 8), 0), OP.add)
@@ -501,6 +509,9 @@ def rank_program(g, core, T, topo):
         tag("trn%d%d" % (vis, h))
         for vq in range(4): (cp if (h, vis) == (1, 3) else act)(A("zs", S(vq, None, 4)), A("st%d" % h, S(64 * vq + 7, 64 * vq + 64, 8)))
         mm([(TN, A("zs"), IDF, True, True)])
+
+    def rows_of(h, vis):
+        tag("trn%d%d" % (vis, h))
         if vis < 3:
             for vh in range(2): act(A("yw%d" % h, S(128 * vh, 128 * vh + 128)), TN, scale=C("hm", 2 + vh))
 
@@ -512,9 +523,10 @@ def rank_program(g, core, T, topo):
         tag("mg %d%d" % (vis, h))
         e(A("mg%d" % h, S(16 * a, 16 * b)), IN(A("mwin"), A("ml%d" % h, S(a, b))))
 
-    def m_sum(h):
+    def m_sum(h, a=0, b=128):
         tag("msum%d" % h)
-        mm([(A("pM", S(0, 2)), A("idb"), A("mg%d" % h, S(r, None, 8)), h == 0 and r == 0, h == 1 and r == 7) for r in range(8)], h == 1)
+        mm([(A("pM", S(a // 64, b // 64)), A("idb"), A("mg%d" % h, S(16 * a + r, 16 * b, 8)), h == 0 and r == 0, h == 1 and r == 7 and b == 128)
+            for r in range(8)], h == 1)
 
     def m_out(k):
         tag("mout%d" % k)
@@ -544,42 +556,44 @@ def rank_program(g, core, T, topo):
 
     steps = [(h, vis) for vis in range(4) for h in (0, 1)]
     b1 = (me - 1) % N
-    tag("choose0"); choose_b("il"); first_cuts(); mask((2, 3)); mask_p(range(4, 8))
-    inherit(0, 0); mask((4, 5, 6)); lists(0, 0); mask((7,)); fraction(0, 0); mix(0, 0); inherit(1, 0); stack(0, 0); whole(1, 0); table(0, 0)
-    gather(0, 0, 1); marks(0, 0); spread(1); lists(1, 0, False); fraction(1, 0); weights_b()
-    tag("choose1"); choose_a(RA, "rl", "ra%d" % b1); cp(A("lkk"), A("rl")); tt(A("lkk"), A("lkk"), A("kof"), OP.add)
-    dots(0, 0, 1, range(8)); list2(0, 0); dots(0, 0, 1, range(8, 16)); mix(1, 0); list2_v(0, 0); gather(0, 0, 2)
-    weights_c(); tag("choose1"); choose_p(); table(1, 0); fields(0, 0, 0)
-    for i in range(1, 9):
-        now = steps[i] if i < 8 else None
+    tag("choose0"); choose_s("a0b", "lku", RA); choose_abs(); mask_p(range(3)); tag("choose0"); choose_p(); pairs_first(); cut_rows((1,))
+    grandchildren(0, KCUT, cp); grandchildren(KCUT, 256); table_rows(); mask(range(3)); mask_p(range(3, 6)); uncle_next()
+    tag("choose0"); choose_b("il"); first_cuts(); mask((3, 4)); mask_p((6, 7)); inherit(0, 0); mask((5, 6, 7)); lists(0, 0); fraction(0, 0); mix(0, 0); inherit(1, 0); gather(0, 0, 1)
+    stack(0, 0); marks(0, 0); weights_a(); table(0, 0); spread(1)
+    lists(1, 0); tag("choose1"); cp(A("lkk"), A("rl")); fraction(1, 0); mix(1, 0); gather(1, 0, 1); dots(0, 0, 1); list2(0, 0); table(1, 0); stack(1, 0)
+    tag("choose1"); choose_a(RA, "rl", "ra%d" % b1); weights_b(); weights_c(); tt(A("lkk"), A("lkk"), A("kof"), OP.add)
+    list2_v(0, 0); gather(0, 0, 2); list2(1, 0); marks(1, 0); tag("choose1"); choose_p(); dots(0, 0, 2)
+    list2_v(1, 0); fields(0, 0, 0); fields(0, 0, 1); gather(1, 0, 2, 0, FIRST); tag("choose1"); choose_b("ri%d" % b1)
+    send(A("ri%d" % b1), A("ri%d" % b1), [cores[(me + 1) % N], cores[(me + 2) % N]], "aI%d" % b1)
+    dots(1, 0, 1, range(DOTS))
+    for i in range(1, 8):
+        now = steps[i]
         old = steps[i - 1]
         nxt = steps[i + 1] if i < 7 else None
-        if now: gather(*now, 1); stack(*now)
-        else: places_a(0)
-        dots(*old, 2)
-        if now: fields(*old, 1); list2(*now); marks(*now); dots(*now, 1, range(DOTS[0]))
         if i == 1:
-            tag("choose1"); choose_b("ri%d" % b1)
-            send(A("ri%d" % b1), A("ri%d" % b1), [cores[(me + 1) % N], cores[(me + 2) % N]], "aI%d" % b1)
-        else: m_gather(*steps[i - 2], MSPLIT, 128)
-        if i == 8: m_sum(1); m_out(2); m_sum(0)
-        decide(*old)
-        if now: list2_v(*now)
-        turn(*old)
-        if now: dots(*now, 1, range(DOTS[0], DOTS[1])); gather(*now, 2, 0, CUTS[0])
-        keep(*old)
+            decide(*old); turn(*old); rows_of(*old)
+        else:
+            gather(*now, 1, 0, CUT); dots(*old, 2); mix(*now); fields(*old, 1); stack(*now); list2(*now); marks(*now)
+            if i > 2: m_sum((i - 1) % 2)
+            m_gather(*steps[i - 2], 0, MSPLIT)
+            decide(*old); list2_v(*now); turn(*old); rows_of(*old); gather(*now, 1, CUT, 128)
+        fields(*now, 0)
+        if i > 1: dots(*now, 1, range(DOTS))
         if nxt: inherit(*nxt)
-        if now: gather(*now, 2, CUTS[0], CUTS[1]); dots(*now, 1, range(DOTS[1], 16))
-        if i < 8: m_gather(*old, 0, MSPLIT)
-        if nxt: lists(*nxt); table(*nxt)
-        if i == 7: fields(*now, 0); fields(*now, 1)
-        if 2 <= i < 7: m_sum(i % 2)
-        if now: gather(*now, 2, CUTS[1], 128)
-        if nxt: fraction(*nxt); fields(*now, 0); mix(*nxt)
-        if i in (3, 5): m_out((i - 3) // 2)
+        if i in (4, 6): m_out((i - 4) // 2)
+        dots(*now, 1, range(DOTS, 16))
+        gather(*now, 2, FIRST if i == 1 else 0, 128 if nxt else LASTCUT)
+        if i > 1: m_gather(*steps[i - 2], MSPLIT, 128)
+        if nxt: lists(*nxt)
+        keep(*old)
+        if nxt: table(*nxt); fraction(*nxt)
+        else: m_gather(*old); gather(*now, 2, LASTCUT, 128)
         if i in (1, 3): spread(2 + i // 2)
-    m_gather(1, 3, 0, 64); m_gather(1, 3, 64, 128, cp)
-    m_sum(1); places_a(1); m_out(3)
+    places_a(0); fields(1, 3, 1, (0, 1)); dots(1, 3, 2); fields(1, 3, 1, (2, 3)); m_sum(1); m_out(2)
+    decide(1, 3); turn(1, 3); m_sum(0); keep(1, 3)
+    for a in (0, 64):
+        m_gather(1, 3, a, a + 32); m_gather(1, 3, a + 32, a + 64, cp); m_sum(1, a, a + 64)
+    places_a(1); m_out(3)
     places_b(0); places_b(1)
     tag("out")
     for vh in range(2): mm([(A("pL", S(128 * vh, 128 * vh + 128)), A("zp%d" % vh), IDF, True, True)])

@@ -6,13 +6,13 @@ OP = AluOpType
 AF = ActivationFunctionType
 RND = 12582912.0
 PEN = 2097152.0
-FIRST = 24
+FIRST = 40
 LASTCUT = 56
 MASK_V = range(8)
-KCUT = 88
+KCUT = (72, 110)
 CUT = 88
-MSPLIT = 40
-DOTS = 8
+MSPLIT = (36, 60)
+DOTS = 6
 TAG = [""]
 
 F32, B16, I32, U16 = "float32", "bfloat16", "int32", "uint16"
@@ -20,28 +20,29 @@ SCRATCH = {
     "kl": ("sbuf", [128, 256], I32), "ul": ("sbuf", [128, 256], I32),
     "ytk": ("sbuf", [128, 2, 8, 16], I32), "xk": ("sbuf", [128, 256], F32), "zk": ("sbuf", [128, 256], F32),
     "lstk": ("sbuf", [128, 256], U16), "db": ("sbuf", [128, 5, 256], B16), "dp": ("sbuf", [128, 8, 128], B16),
-    "lki": ("sbuf", [128, 64], I32), "lku": ("sbuf", [128, 64], U16), "lkk": ("sbuf", [128, 64], F32), "kof": ("sbuf", [128, 64], F32),
+    "lki": ("sbuf", [128, 64], I32), "lku": ("sbuf", [128, 64], U16), "lkk": ("sbuf", [128, 64], B16), "kof": ("sbuf", [128, 64], B16),
+    "sh": ("sbuf", [128, 2, 128], B16),
     "a0b": ("sbuf", [128, 256], B16), "il": ("sbuf", [128, 64], U16), "rl": ("sbuf", [128, 64], U16),
     "swin": ("sbuf", [128, 4096], B16), "mwin": ("sbuf", [128, 4096], B16), "cwin": ("sbuf", [128, 2048], B16),
     "meta": ("sbuf", [128, 4096], B16),
     "ax0": ("sbuf", [128, 2048], B16), "ax1": ("sbuf", [128, 2048], B16),
     "df": ("sbuf", [128, 1024], B16), "dabs": ("sbuf", [128, 1024], B16),
     "yg": ("sbuf", [128, 512], F32), "nr": ("sbuf", [128, 128], I32), "lam": ("sbuf", [128, 128], B16), "rn": ("sbuf", [128, 160, 3], F32),
-    "d0": ("sbuf", [128, 256], F32), "zs": ("sbuf", [128, 32, 4], F32), "sl": ("sbuf", [128, 32, 4], F32),
-    "kd": ("sbuf", [128, 4, 4, 16], F32), "km": ("sbuf", [128, 4, 2, 16], F32), "ki": ("sbuf", [128, 128], I32),
+    "d0": ("sbuf", [128, 256], F32), "zs": ("sbuf", [128, 32, 4], F32), "sl0": ("sbuf", [128, 32, 4], F32), "sl1": ("sbuf", [128, 32, 4], F32),
+    "kd": ("sbuf", [128, 4, 32], F32), "km": ("sbuf", [128, 4, 2, 16], F32), "ki": ("sbuf", [128, 4, 16, 2], I32),
     "xc": ("sbuf", [128, 4, 64], I32), "xh": ("sbuf", [128, 4, 64], I32), "xy": ("sbuf", [128, 4, 64], F32), "xi": ("sbuf", [128, 4, 64], I32),
     "xw": ("sbuf", [128, 20, 64], F32), "xo": ("sbuf", [128, 4, 64], F32), "xz": ("sbuf", [128, 4, 64], F32), "xl": ("sbuf", [128, 64], U16),
     "one": ("sbuf", [128, 256], F32), "idf": ("sbuf", [128, 144], F32), "idb": ("sbuf", [128, 128], B16),
-    "gi": ("sbuf", [128, 8], F32), "g3": ("sbuf", [128, 8, 3], F32), "gx": ("sbuf", [128, 8, 5, 2], F32), "m32": ("sbuf", [128, 32], F32),
-    "pn": ("sbuf", [128, 4], I32), "pf": ("sbuf", [128, 3], F32), "i16": ("sbuf", [128, 16], F32), "e16": ("sbuf", [128, 16], F32),
+    "g3": ("sbuf", [128, 8, 3], F32), "gx": ("sbuf", [128, 8, 5, 2], F32), "m32": ("sbuf", [128, 32], F32),
+    "pn": ("sbuf", [128, 4], I32), "pf": ("sbuf", [128, 2], F32), "i16": ("sbuf", [128, 16], F32), "e16": ("sbuf", [128, 16], F32),
     "e4": ("sbuf", [128, 4], F32), "hm": ("sbuf", [128, 4], F32), "fc": ("sbuf", [128, 8], F32), "bs": ("sbuf", [128, 24], F32),
     "al": ("sbuf", [128, 8], F32), "mx": ("sbuf", [128, 4, 8, 16], B16),
     "vg": ("sbuf", [128, 8, 9, 2], F32), "dg": ("sbuf", [128, 8, 8, 2], F32), "wg": ("sbuf", [128, 8, 8, 16], B16),
     "vm": ("sbuf", [128, 2, 9, 2], F32), "dm": ("sbuf", [128, 48], F32), "wm": ("sbuf", [128, 8, 48], B16),
     "jj": ("sbuf", [128, 8, 8], F32), "sel": ("sbuf", [128, 4, 8, 16], F32), "sq": ("sbuf", [128, 4, 144], F32),
-    "zq": ("sbuf", [128, 4, 144], B16), "zu": ("sbuf", [128, 144], B16), "zc": ("sbuf", [128, 146], B16), "idn": ("sbuf", [128, 128], B16),
+    "zq": ("sbuf", [128, 2, 144], B16), "zu": ("sbuf", [128, 144], B16), "zc": ("sbuf", [128, 146], B16), "idn": ("sbuf", [128, 128], B16),
     "wi": ("sbuf", [128, 128], B16), "inn": ("sbuf", [128, 4096], B16), "nu": ("sbuf", [128, 32], F32),
-    "hb": ("sbuf", [128, 16], F32), "nb": ("sbuf", [128, 3, 256], B16), "ds": ("sbuf", [128, 2, 128, 2], B16), "r5": ("sbuf", [128, 160], F32),
+    "nb": ("sbuf", [128, 3, 256], B16), "ds": ("sbuf", [128, 2, 128, 2], B16), "r5": ("sbuf", [128, 160], F32),
     "ycs": ("sbuf", [128, 256], F32), "acc": ("sbuf", [128, 256], F32), "yes": ("sbuf", [128, 256], F32),
     "pL": ("psum", [128, 512], F32), "pM": ("psum", [128, 4, 128], F32),
 }
@@ -55,8 +56,8 @@ for _h in "01":
 for _k in range(4):
     SCRATCH["ra%d" % _k] = ("sbuf", [128, 256], B16)
     SCRATCH["ri%d" % _k] = ("sbuf", [128, 64], U16)
-    SCRATCH["ms%d" % _k] = ("sbuf", [128, 256], F32 if _k < 3 else U16)
-    if _k: SCRATCH["rE%d" % _k] = ("sbuf", [128, 256], F32 if _k < 3 else U16)
+    SCRATCH["ms%d" % _k] = ("sbuf", [128, 256], F32 if _k < 2 else "float16")
+    if _k: SCRATCH["rE%d" % _k] = ("sbuf", [128, 256], F32 if _k < 2 else "float16")
 
 _DS = ["dk", "du", "da", "dl", "da0", "dyk", "dxc", "dss", "dmm", "dcw", "dcu", "dm0", "dm1", "dm2", "dm3", "dyc", "dye0", "dye1"]
 SEMAPHORES = ["sv", "ss", "sp", "sg", "rl", "aL"] + _DS + ["aA%d" % k for k in range(4)] + ["aI%d" % k for k in range(4)] + ["aE%d" % k for k in range(1, 4)]
@@ -128,7 +129,18 @@ def rank_program(g, core, T, topo):
         for n, m in r + w:
             if SCRATCH[n][0] == "psum": bank.setdefault(n, {})[key] = ev
 
+    held = []
+
+    def weave(*parts):
+        runs = []
+        for f in parts:
+            held.append([]); f(); runs.append(held.pop())
+        for k in range(max(len(x) for x in runs)):
+            for x in runs:
+                if k < len(x): op(*x[k])
+
     def op(e, calls, r, w, acc=False):
+        if held: return held[-1].append((e, calls, r, w, acc))
         r = [x for a in r if isinstance(a, tuple) for x in a[1]]; w = [x for a in w for x in a[1]]
         deps(e, e, r, w, acc)
         s = SEM[e]
@@ -210,28 +222,28 @@ def rank_program(g, core, T, topo):
 
     tag("const")
     SR, AND = OP.arith_shift_right, OP.bitwise_and
-    iota(C("pn", 0), [[0, 1]], 0, 1, False); iota(A("i16"), [[1, 16]], 0, 0); iota(A("nb", 0), [[1, 256]], 0, 0)
+    iota(C("pn", 0), [[0, 1]], 0, 1, False); iota(A("i16"), [[1, 16]], 0, 0)
     ms(A("one"), 1.0)
-    for j, b in enumerate((15, 7, 3)): ts(C("pn", j + 1), C("pn", 0), b, AND)
-    cp(A("pf"), A("pn", S(1, 4)))
-    ts(A("e16"), A("i16"), C("pf", 0), OP.is_equal); ts(A("e4"), A("i16", S(0, 4)), C("pf", 2), OP.is_equal)
-    tt(A("fc"), A("e16", S(0, None, 2)), A("e16", S(1, None, 2)), OP.add)
-    ms(A("cwin"), 0.0)
-    for j, (c, k, f) in enumerate(((1, 4, OP.is_lt), (1, 4, OP.is_ge), (0, 8, OP.is_lt), (0, 8, OP.is_ge))): ts(C("hm", j), C("pf", c), k, f)
-    for n in ("zq", "zu", "zc", "mx", "gx", "sel", "vg", "vm"): ms(A(n), 0.0)
-    gsel(A("gi"), A("one", S(0, 8)), [[-16, 8]], 0, 1, OP.is_ge, 0.0)
-    gsel(A("gi"), A("gi"), [[16, 8]], 15, -1, OP.is_ge, 0.0)
+    for j, b in enumerate((15, 3)): ts(C("pn", j + 1), C("pn", 0), b, AND)
+    ms(A("mx"), 0.0); cp(A("pf"), A("pn", S(1, 3))); ms(A("vm"), 0.0)
+    ts(A("e16"), A("i16"), C("pf", 0), OP.is_equal); ts(A("e4"), A("i16", S(0, 4)), C("pf", 1), OP.is_equal)
+    ms(A("zq"), 0.0); tt(A("fc"), A("e16", S(0, None, 2)), A("e16", S(1, None, 2)), OP.add)
+    for n in ("zu", "zc", "gx", "vg", "cwin"): ms(A(n), 0.0)
+    for j, f in enumerate((OP.is_lt, OP.is_ge)): ts(C("hm", j), C("pf", 0), 8, f)
+    ms(A("sel"), 0.0)
     gsel(A("m32"), A("one", S(0, 32)), [[-4, 4], [-16, 8]], 0, 1, OP.is_ge, 0.0)
+    gsel(A("g3"), A("one", S(0, 24)), [[-16, 8], [0, 3]], 0, 1, OP.is_ge, 0.0)
     gsel(A("m32"), A("m32"), [[4, 4], [16, 8]], 3, -1, OP.is_ge, 0.0)
-    iota(A("kof"), [[256, 4], [0, 16]], 0, 0); iota(A("nb", 2), [[2, 128], [-1, 2]], 1, 0)
+    gsel(A("g3"), A("g3"), [[16, 8], [0, 3]], 15, -1, OP.is_ge, 0.0)
     gsel(A("idf"), A("one", S(0, 144)), [[-1, 144]], 8, 1, OP.is_equal, 0.0)
-    gsel(A("wi"), A("one", S(0, 128)), [[-1, 8], [0, 16]], 0, 1, OP.is_equal, 0.0)
+    gsel(A("idb"), A("one", S(0, 128)), [[-1, 128]], 0, 1, OP.is_equal, 0.0)
     gsel(A("jj"), A("one", S(0, 64)), [[-16, 8], [-1, 8]], 0, 1, OP.is_equal, 0.0)
+    iota(A("kof"), [[256, 4], [0, 16]], 0, 0)
+    for y in range(2): gsel(A("sh", y), A("one", S(0, 128)), [[-16, 8], [-1, 8], [0, 2]], -8 * y, 1, OP.is_equal, 0.0)
     gsel(A("jj"), A("jj"), [[-16, 8], [-1, 8]], -8, 1, OP.not_equal, 1.0)
-    tag("static")
-    act(C("hb", 0), C("pf", 0), scale=256.0); spreadcol(A("nb", 1), C("hb", 0)); axpy(C("fc", SIB), 1, E(12), E(5))
-    act(A("zq", ALL, S(15, 128, 16)), A("m32"), scale=1024.0)
-    act(A("zu", S(15, 128, 16)), A("gi"), scale=C("fc", UP))
+    gsel(A("wi"), A("one", S(0, 128)), [[-1, 8], [0, 16]], 0, 1, OP.is_equal, 0.0)
+    GI = A("g3", ALL, 0)
+    def G1(k): return A("g3", k, S(0, 1))
 
     tag("weights0")
     def B(j): return C("bs", j)
@@ -247,12 +259,14 @@ def rank_program(g, core, T, topo):
     for o, x in ((S(0, 3), E(2)), (S(4, 10, 5), E(3)), (S(5, 6), E(3)), (S(10, 12), E(0)), (S(13, 15), E(1)), (S(6, 7), B(HA)), (S(12, 13), B(LA))):
         spreadcol(A("dm", o), x)
     axpy(C("dm", 3), PEN, E(9), C("dm", 3))
-    for j in range(2): act(A("zc", S(15 + j, 130, 16)), A("gi"), scale=C("fc", KID))
-    for j in range(3): act(A("g3", ALL, j), A("gi"))
-    act(A("gx", ALL, 1, 0), A("gi")); act(A("gx", ALL, 2, 1), A("gi"))
-    for k in range(8): act(A("wm", k, S(0, 15)), A("dm", S(0, 15)), scale=C("gi", k))
+    for q in range(4): act(A("zq", q // 2, S(14 + q % 2, 128, 16)), A("m32", S(8 * q, 8 * q + 8)), scale=1024.0)
+    act(A("zu", S(15, 128, 16)), GI, scale=C("fc", UP))
+    for j in range(2): act(A("zc", S(15 + j, 130, 16)), GI, scale=C("fc", KID))
+    act(A("gx", ALL, 1, 0), GI); act(A("gx", ALL, 2, 1), GI)
+    act(C("hm", 2), C("pf", 0), scale=256.0); axpy(C("fc", SIB), 1, E(12), E(5)); spreadcol(A("nb", 1), C("hm", 2))
+    for k in range(8): act(A("wm", k, S(0, 15)), A("dm", S(0, 15)), scale=G1(k))
     for k in range(4): act(A("sq", k), A("idf"), scale=C("e4", k))
-    act(A("idb"), A("idf", S(8, 136))); act(A("idn"), A("idf", S(8, 136)), scale=-1.0)
+    act(A("idn"), A("idf", S(8, 136)), scale=-1.0)
     for vq in range(4):
         c = 4 * (vq % 2); act(A("sel", vq, ALL, S(8 * (vq // 2) + c, 8 * (vq // 2) + c + 4)), A("jj", ALL, S(c, c + 4)))
 
@@ -286,27 +300,27 @@ def rank_program(g, core, T, topo):
             gsel(A("ax%d" % (vis % 2), S(r, None, 16)), A("ra%d" % b, S(128 * (r // 8), 128 * (r // 8) + 128)), [[0, 128]], 1, 0, OP.is_gt, 0.0)
 
     tag("bytes")
-    cp(A("db", 3), A("ul")); tt(A("db", 2), A("ul"), A("db", 3), OP.subtract)
-    for j in range(2): cp(A("dp", 4 + j), A("db", 2 + j, S(0, None, 2)))
-    dma("Y", [(A("cwin", rows=S(2 + j, None, 16)), A("dp", 4 + j)) for j in range(2)], "dcu", True)
-    cp(A("db", 1), A("kl")); tt(A("db", 0), A("kl"), A("db", 1), OP.subtract)
-    ts(A("db", 4), A("kl"), 0, OP.is_lt, -256.0, OP.mult)
-    for j in range(4): cp(A("dp", j), A("db", j % 2, S(j // 2, None, 2)))
+    cp(A("db", 1), A("kl")); cp(A("db", 3), A("ul")); tt(A("db", 0), A("kl"), A("db", 1), OP.subtract)
+    for j in (1, 3, 0, 2): cp(A("dp", j), A("db", j % 2, S(j // 2, None, 2)))
     dma("Y", [(A("cwin", rows=S(8 + j, None, 16)), A("dp", j)) for j in range(4)], "dcw", True)
+    tt(A("db", 2), A("ul"), A("db", 3), OP.subtract); ts(A("db", 4), A("kl"), 0, OP.is_lt, -256.0, OP.mult)
+    for j in (1, 0): cp(A("dp", 4 + j), A("db", 2 + j, S(0, None, 2)))
+    dma("Y", [(A("cwin", rows=S(2 + j, None, 16)), A("dp", 4 + j)) for j in range(2)], "dcu", True)
     dma("Y", [(A("inn", rows=S(0, 8)), A("db", 4))], "dm0")
     dma("Y", [(A("swin", S(0, 2048)), H(T.s[:, 0:2048]))], "dss")
     dma("Y", [(A("swin", S(2048, 4096)), H(T.s[:, 2048:4096]))], "dm3")
     tag("lstk")
     for b in range(8):
         cp(A("xk", S(32 * b, 32 * b + 32)), A("ytk", ALL, b))
-    op("V", [lambda: g.vector.transpose(out=T.zk[:, :], in_=T.xk[:, :])], [A("xk")], [A("zk")])
     cp(A("lku"), A("lki"))
+    op("V", [lambda: g.vector.transpose(out=T.zk[:, :], in_=T.xk[:, :])], [A("xk")], [A("zk")])
+    cp(A("lkk"), A("lki"))
     for b in range(8):
         ts(A("lstk", S(b, None, 8)), A("zk", S(32 * b, 32 * b + 32)), 0.5, OP.mult)
-    tt(A("lkk"), A("lki"), A("kof"), OP.add)
+    iota(A("nb", 0), [[1, 256]], 0, 0); iota(A("nb", 2), [[2, 128], [-1, 2]], 1, 0)
+    spread(0)
     send(A(RA), A(RA), peers, "aA%d" % me)
     send(A("lku"), A("rl"), [cores[(me + 1) % N]], "aL")
-    spread(0)
     tag("const")
     gsel(A("r5"), A("one", S(0, 160)), [[0, 32], [1, 5]], 0, 0, OP.is_gt, 0.0)
     iota(A("d0", S(0, None, 8)), [[0, 32]], 0, 0)
@@ -352,15 +366,17 @@ def rank_program(g, core, T, topo):
         act(A("dabs"), A("df"), AF.Abs)
 
     def choose_p():
-        for q in range(4):
-            mm([(A("pM", q, S(0, 64)), A("zq", q, S(15 - l, 143 - l)), A("dabs", S(l, None, 16)), l == 0, l == 15) for l in range(16)])
+        for j in range(4):
+            h, y = j // 2, j % 2; o = A("pM", j, S(0, 64))
+            mm([(o, A("sh", y), A("lkk"), True, False), (o, A("sh", y), A("kof"), False, False)]
+               + [(o, A("zq", h, S(14 - 2 * x, 142 - 2 * x)), A("dabs", S(8 * y + x, None, 16)), False, x == 7) for x in range(8)])
 
-    def choose_b(out):
-        for q in range(4): tt(A("kd", q), A("pM", q, S(0, 64)), A("lkk"), OP.add)
-        tt(A("km"), A("kd", ALL, S(0, 2)), A("kd", ALL, S(2, 4)), OP.min)
-        tt(A("ki", S(0, 64)), A("km", ALL, 0), A("km", ALL, 1), OP.min)
-        ts(A("ki", S(64, 128)), A("ki", S(0, 64)), 255, AND)
-        cp(A(out), A("ki", S(64, 128)))
+    def choose_b(out, between):
+        for y in range(2): cp(A("kd", S(y, None, 2)), A("pM", S(y, None, 2), S(32, 64)))
+        for y in range(2): tt(A("km", S(y, None, 2)), A("pM", S(y, None, 2), S(0, 32)), A("kd", S(y, None, 2)), OP.min)
+        for y in range(2): tt(A("ki", S(0, 2), ALL, y), A("km", S(y, None, 2), 0), A("km", S(y, None, 2), 1), OP.min)
+        between(0); ts(A("ki", S(2, 4)), A("ki", S(0, 2)), 255, AND)
+        between(1); cp(A(out), A("ki", S(2, 4)))
 
     def choose_s(kept, lk, a):
         act(A("df"), IN(A(kept), A(lk)))
@@ -401,7 +417,7 @@ def rank_program(g, core, T, topo):
 
     def first_cuts():
         tag("first")
-        for h in range(2): act(A("yw%d" % h), A("pL", S(256, 512)), scale=C("hm", 2 + h))
+        for h in range(2): act(A("yw%d" % h), A("pL", S(256, 512)), scale=C("hm", h))
 
     def weights_b():
         tag("weights")
@@ -412,22 +428,22 @@ def rank_program(g, core, T, topo):
 
     def weights_c():
         tag("weights")
-        for k in range(8): act(A("wm", k, S(16, 48)), A("dm", S(16, 48)), scale=C("gi", k))
-        for k in range(8): act(A("wg", k), A("dg"), scale=C("gi", k))
+        for k in range(8): act(A("wm", k, S(16, 48)), A("dm", S(16, 48)), scale=G1(k))
+        for k in range(8): act(A("wg", k), A("dg"), scale=G1(k))
 
     IDF = A("idf", S(8, 136))
-    Y, L2, TN = A("pL", S(0, 128)), A("pL", S(128, 256)), A("pL", S(256, 384))
+    Y, TN = A("pL", S(0, 128)), A("pL", S(256, 384))
 
     def inherit(h, vis):
         tag("inh%d%d" % (vis, h))
         lst = "il" if vis == 0 else "ri%d" % ((me - vis) % N)
-        for q in range(2):
-            act(A("yg", S(256 * q, 256 * q + 256)), IN(A("yw%d" % h), A(lst, S(32 * h + 16 * q, 32 * h + 16 * q + 16))))
-            mm([(Y, A("sel", 2 * vh + q), A("yg", S(256 * q + 128 * vh, 256 * q + 128 * vh + 128)), q + vh == 0, q + vh == 2) for vh in range(2)], q > 0)
+        for vh in range(2):
+            act(A("yg", S(256 * vh, 256 * vh + 256)), IN(A("yw%d" % h), A(lst, S(32 * h + 16 * vh, 32 * h + 16 * vh + 16))))
+            mm([(Y, A("sel", 2 * vh + q), A("yg", S(256 * vh + q, 256 * vh + 256, 2)), q + vh == 0, q + vh == 2) for q in range(2)], vh > 0)
 
     def lists(h, vis):
         tag("cl %d%d" % (vis, h))
-        cp(A("cl%d" % h), Y); cp(A("nr"), Y)
+        cp(A("nr"), Y); cp(A("cl%d" % h), Y)
 
     def fraction(h, vis):
         tag("cl %d%d" % (vis, h))
@@ -458,24 +474,24 @@ def rank_program(g, core, T, topo):
 
     KEYS = (((3, S(1, 3)), (4, S(1, 3)), (0, S(0, 3)), (1, S(1, 3))), ((2, S(0, 3, 2)), None, (3, S(0, 1)), (4, S(0, 1))))
 
-    def dots(h, vis, k, rs=range(16)):
+    def dots(h, vis, k, rs=range(16), a=0, b=128):
         tag("dot%d %d%d" % (k, vis, h))
         grp = []
         for r in rs:
             vq = r // 4; key = KEYS[k - 1][r % 4]
-            if key: o, w = A("pK%d" % h, S(40 * vq + key[0], 40 * vq + 40, 5), key[1]), A("g3", ALL, key[1])
-            else: o, w = A("pK%d" % h, S(40 * vq, 40 * vq + 40), S(0, 2)), A("gx")
-            grp.append((o, A("pq"[k - 1] + str(h), S(r, None, 16)), w, False, k == 2 and r == 15))
+            if key: o, w = A("pK%d" % h, S(40 * vq + key[0], 40 * vq + 40, 5), key[1], rows=S(a, b)), A("g3", ALL, key[1])
+            else: o, w = A("pK%d" % h, S(40 * vq, 40 * vq + 40), S(0, 2), rows=S(a, b)), A("gx")
+            grp.append((o, A("pq"[k - 1] + str(h), S(16 * a + r, 16 * b, 16)), w, False, k == 2 and r == 15 and b == 128))
         mm(grp, True)
 
     def list2(h, vis):
         tag("l2 %d%d" % (vis, h))
         grp = [(z, 4 * vq + at, 4 * vq + s) for vq in range(4) for z, at, s in (("zu", 0, 0), ("zu", 1, 2), ("zc", 2, 3))]
-        mm([(L2, A(z, S(15 - l, 143 - l)), A("gm%d" % h, S(r, None, 16)), i == 0, i == 11) for i, (z, l, r) in enumerate(grp)])
+        mm([(A("pB%d" % h, S(0, 128), 0), A(z, S(15 - l, 143 - l)), A("gm%d" % h, S(r, None, 16)), i == 0, i == 11) for i, (z, l, r) in enumerate(grp)])
 
     def list2_v(h, vis):
         tag("l2 %d%d" % (vis, h))
-        ts(A("l2%d" % h), L2, C("e4", 3), OP.add)
+        ts(A("l2%d" % h), A("pB%d" % h, S(0, 128), 0), C("e4", 3), OP.add)
 
     def fields(h, vis, b, vqs=range(4)):
         tag("fld%d %d%d" % (b, vis, h))
@@ -497,8 +513,9 @@ def rank_program(g, core, T, topo):
             scan(A(rn, c, j), A("r5"), A(k, c, j), OP.max)
         tt(A(d0, S(4, None, 8)), A(k, S(0, 160, 5), 2), A(rn, S(0, 160, 5), 2), OP.is_lt)
         tt(A(d0, S(3, None, 8)), A(k, S(1, 160, 5), 2), A(rn, S(1, 160, 5), 2), OP.is_equal)
-        tt(A(d0, S(7, None, 8)), A(d0, S(4, None, 8)), A("nu"), OP.max)
-        for j in range(2): tt(A(d0, S(1 + j, None, 4)), A(k, S(3 + j, 160, 5), S(0, 2)), A(rn, S(3 + j, 160, 5), S(0, 2)), OP.is_lt)
+        for j in range(2):
+            tt(A(d0, S(1 + j, None, 4)), A(k, S(3 + j, 160, 5), S(0, 2)), A(rn, S(3 + j, 160, 5), S(0, 2)), OP.is_lt)
+            if j == 0: tt(A(d0, S(7, None, 8)), A(d0, S(4, None, 8)), A("nu"), OP.max)
         if between: between()
         tag("dec%d%d" % (vis, h))
         for f in range(4):
@@ -513,7 +530,7 @@ def rank_program(g, core, T, topo):
     def rows_of(h, vis):
         tag("trn%d%d" % (vis, h))
         if vis < 3:
-            for vh in range(2): act(A("yw%d" % h, S(128 * vh, 128 * vh + 128)), TN, scale=C("hm", 2 + vh))
+            for vh in range(2): act(A("yw%d" % h, S(128 * vh, 128 * vh + 128)), TN, scale=C("hm", vh))
 
     def keep(h, vis):
         tag("keep%d%d" % (vis, h))
@@ -521,30 +538,33 @@ def rank_program(g, core, T, topo):
 
     def m_gather(h, vis, a=0, b=128, e=act):
         tag("mg %d%d" % (vis, h))
-        e(A("mg%d" % h, S(16 * a, 16 * b)), IN(A("mwin"), A("ml%d" % h, S(a, b))))
+        e(A(MG(h, vis), S(16 * a, 16 * b)), IN(A("mwin"), A("ml%d" % h, S(a, b))))
 
-    def m_sum(h, a=0, b=128):
+    def MG(h, vis): return ("gm%d" if (h, vis) == (0, 3) else "mg%d") % h
+
+    def m_sum(h, vis=0, a=0, b=128):
         tag("msum%d" % h)
-        mm([(A("pM", S(a // 64, b // 64)), A("idb"), A("mg%d" % h, S(16 * a + r, 16 * b, 8)), h == 0 and r == 0, h == 1 and r == 7 and b == 128)
+        mm([(A("pM", S(a // 64, b // 64)), A("idb"), A(MG(h, vis), S(16 * a + r, 16 * b, 8)), h == 0 and r == 0, h == 1 and r == 7 and b == 128)
             for r in range(8)], h == 1)
 
     def m_out(k):
         tag("mout%d" % k)
-        for vh in range(2): (act if k < 3 else cp)(A("ms%d" % k, S(128 * vh, 128 * vh + 128)), A("pM", S(0, 2), S(vh, None, 2)))
+        for vh in range(2):
+            o, x = A("ms%d" % k, S(128 * vh, 128 * vh + 128)), A("pM", S(0, 2), S(vh, None, 2))
+            if k < 2: act(o, x)
+            else: ts(o, x, -2040.0, OP.add)
         if k: send(A("ms%d" % k), A("rE%d" % k), [cores[(me - k) % N]], "aE%d" % k)
 
-    def places_a(h):
+    def places_a(h, b=5, a=0):
         tag("plc%d" % h)
         so = "so%d" % h; y = A("st%d" % h, S(7, None, 8))
-        ts(A(so, 0), y, RND, OP.add, -RND, OP.add)
-        tt(A(so, 1), y, A(so, 0), OP.subtract)
-        ts(A(so, 1), A(so, 1), 32768.0, OP.mult, -2048.0, OP.add)
-        ts(A(so, 1), A(so, 1), RND * 4096, OP.add, -RND * 4096, OP.add)
-        tt(A(so, 2), A(so, 1), A(so, 0), OP.add)
+        for f in (lambda: ts(A(so, 0), y, RND, OP.add, -RND, OP.add), lambda: tt(A(so, 1), y, A(so, 0), OP.subtract),
+                  lambda: ts(A(so, 1), A(so, 1), 32768.0, OP.mult, -2048.0, OP.add),
+                  lambda: ts(A(so, 1), A(so, 1), RND * 4096, OP.add, -RND * 4096, OP.add), lambda: tt(A(so, 2), A(so, 1), A(so, 0), OP.add))[a:b]: f()
 
     def places_b(h):
         tag("plc%d" % h)
-        so = "so%d" % h; sl = "sl"
+        so = "so%d" % h; sl = "sl%d" % h
 
         def w(k, s): return A(so, k, S(s, None, 4))
         for i in (0, 2):
@@ -556,58 +576,58 @@ def rank_program(g, core, T, topo):
 
     steps = [(h, vis) for vis in range(4) for h in (0, 1)]
     b1 = (me - 1) % N
-    tag("choose0"); choose_s("a0b", "lku", RA); choose_abs(); mask_p(range(3)); tag("choose0"); choose_p(); pairs_first(); cut_rows((1,))
-    grandchildren(0, KCUT, cp); grandchildren(KCUT, 256); table_rows(); mask(range(3)); mask_p(range(3, 6)); uncle_next()
-    tag("choose0"); choose_b("il"); first_cuts(); mask((3, 4)); mask_p((6, 7)); inherit(0, 0); mask((5, 6, 7)); lists(0, 0); fraction(0, 0); mix(0, 0); inherit(1, 0); gather(0, 0, 1)
-    stack(0, 0); marks(0, 0); weights_a(); table(0, 0); spread(1)
-    lists(1, 0); tag("choose1"); cp(A("lkk"), A("rl")); fraction(1, 0); mix(1, 0); gather(1, 0, 1); dots(0, 0, 1); list2(0, 0); table(1, 0); stack(1, 0)
-    tag("choose1"); choose_a(RA, "rl", "ra%d" % b1); weights_b(); weights_c(); tt(A("lkk"), A("lkk"), A("kof"), OP.add)
-    list2_v(0, 0); gather(0, 0, 2); list2(1, 0); marks(1, 0); tag("choose1"); choose_p(); dots(0, 0, 2)
-    list2_v(1, 0); fields(0, 0, 0); fields(0, 0, 1); gather(1, 0, 2, 0, FIRST); tag("choose1"); choose_b("ri%d" % b1)
-    send(A("ri%d" % b1), A("ri%d" % b1), [cores[(me + 1) % N], cores[(me + 2) % N]], "aI%d" % b1)
-    dots(1, 0, 1, range(DOTS))
+    tag("choose0"); choose_s("a0b", "lku", RA); grandchildren(KCUT[0], KCUT[1]); tag("choose0"); choose_abs(); mask_p(range(3)); choose_p()
+    pairs_first(); cut_rows((1,)); grandchildren(0, KCUT[0], cp); grandchildren(KCUT[1], 256); table_rows(); mask(range(3)); mask_p(range(3, 6))
+    uncle_next(); tag("choose0"); choose_b("il", lambda k: mask((3 + k,))); first_cuts(); mask_p((6, 7)); inherit(0, 0); mask((5, 6, 7))
+    lists(0, 0); fraction(0, 0); mix(0, 0); inherit(1, 0); gather(0, 0, 1); stack(0, 0); marks(0, 0); weights_a(); table(0, 0); spread(1)
+    lists(1, 0); fraction(1, 0); mix(1, 0); stack(1, 0); table(1, 0); gather(1, 0, 1); dots(0, 0, 1); list2(0, 0)
+    marks(1, 0); dots(1, 0, 1); weights_b(); weights_c(); list2_v(0, 0)
+    gather(0, 0, 2); list2(1, 0); dots(0, 0, 2); tag("choose1"); cp(A("lkk"), A("rl")); choose_a(RA, "rl", "ra%d" % b1)
+    list2_v(1, 0); fields(0, 0, 0); fields(0, 0, 1); tag("choose1"); choose_p()
     for i in range(1, 8):
         now = steps[i]
         old = steps[i - 1]
         nxt = steps[i + 1] if i < 7 else None
         if i == 1:
-            decide(*old); turn(*old); rows_of(*old)
+            decide(*old); turn(*old); rows_of(*old); gather(1, 0, 2, 0, FIRST)
+            choose_b("ri%d" % b1, lambda k: gather(1, 0, 2, FIRST + 8 * k, FIRST + 8 + 8 * k))
+            send(A("ri%d" % b1), A("ri%d" % b1), [cores[(me + 1) % N], cores[(me + 2) % N]], "aI%d" % b1)
         else:
-            gather(*now, 1, 0, CUT); dots(*old, 2); mix(*now); fields(*old, 1); stack(*now); list2(*now); marks(*now)
-            if i > 2: m_sum((i - 1) % 2)
-            m_gather(*steps[i - 2], 0, MSPLIT)
-            decide(*old); list2_v(*now); turn(*old); rows_of(*old); gather(*now, 1, CUT, 128)
-        fields(*now, 0)
-        if i > 1: dots(*now, 1, range(DOTS))
+            gather(*now, 1, 0, CUT if nxt else 128); dots(*old, 2); mix(*now); fields(*old, 1); stack(*now)
+            decide(*old, lambda: keep(*steps[i - 2])); m_gather(*steps[i - 2], 0, MSPLIT[0]); list2(*now); marks(*now)
+            if not nxt: dots(*now, 1, range(DOTS))
+            elif i > 2: m_sum((i - 1) % 2)
+            turn(*old); m_gather(*steps[i - 2], *MSPLIT); rows_of(*old)
+            if nxt: gather(*now, 1, CUT, 128)
+            list2_v(*now)
+        if nxt: fields(*now, 0)
+        if 1 < i < 7: dots(*now, 1, range(DOTS))
         if nxt: inherit(*nxt)
         if i in (4, 6): m_out((i - 4) // 2)
-        dots(*now, 1, range(DOTS, 16))
-        gather(*now, 2, FIRST if i == 1 else 0, 128 if nxt else LASTCUT)
-        if i > 1: m_gather(*steps[i - 2], MSPLIT, 128)
-        if nxt: lists(*nxt)
-        keep(*old)
-        if nxt: table(*nxt); fraction(*nxt)
-        else: m_gather(*old); gather(*now, 2, LASTCUT, 128)
+        if i > 1: dots(*now, 1, range(DOTS, 16))
+        gather(*now, 2, FIRST + 16 if i == 1 else 0, 128 if nxt else LASTCUT)
+        if i > 1: m_gather(*steps[i - 2], MSPLIT[1], 128)
+        if nxt: lists(*nxt); table(*nxt); fraction(*nxt)
+        else: keep(*old); m_gather(*old); gather(*now, 2, LASTCUT, 128); fields(*now, 0)
         if i in (1, 3): spread(2 + i // 2)
-    places_a(0); fields(1, 3, 1, (0, 1)); dots(1, 3, 2); fields(1, 3, 1, (2, 3)); m_sum(1); m_out(2)
-    decide(1, 3); turn(1, 3); m_sum(0); keep(1, 3)
+    def sums_so_far():
+        tag("out"); tt(A("acc"), A("ms0"), A("rE1"), OP.add); cp(A("pA0", ALL, 1), A(RA))
+        ts(C("bs", 20), C("pf", 1), 4096.0, OP.mult, -12288.0, OP.add); ts(A("pB0", ALL, 0), A("acc"), 4080.0, OP.add)
+    weave(lambda: places_a(0), sums_so_far)
+    fields(1, 3, 1, (0, 1)); dots(1, 3, 2); fields(1, 3, 1, (2, 3)); m_sum(0); m_sum(1)
+    decide(1, 3); turn(1, 3); m_out(2); m_sum(0, 3); keep(1, 3)
     for a in (0, 64):
-        m_gather(1, 3, a, a + 32); m_gather(1, 3, a + 32, a + 64, cp); m_sum(1, a, a + 64)
-    places_a(1); m_out(3)
-    places_b(0); places_b(1)
+        m_gather(1, 3, a, a + 32); m_gather(1, 3, a + 32, a + 64, cp); m_sum(1, 3, a, a + 64)
+    places_a(1, 3); m_out(3); weave(lambda: places_b(0), lambda: (places_a(1, 5, 3), places_b(1)))
     tag("out")
     for vh in range(2): mm([(A("pL", S(128 * vh, 128 * vh + 128)), A("zp%d" % vh), IDF, True, True)])
-    ts(C("bs", 20), C("pf", 2), 4096.0, OP.mult, -12288.0, OP.add)
     act(A("ycs"), A("pL", S(0, 256)), AF.Identity, C("bs", 20))
     dma("Y", [(H(T.yc[:, :]), A("ycs"))], "dyc")
-    tt(A("acc"), A("ms0"), A("rE1"), OP.add)
-    tt(A("acc"), A("acc"), A("rE2"), OP.add)
-    tt(A("pA0", ALL, 0), A("acc"), A(RA), OP.mult); cp(A("pA1", ALL, 0), A(RA))
+    tt(A("pA0", ALL, 0), A("pB0", ALL, 0), A("rE2"), OP.add)
+    for h in (0, 1): tt(A("ms0", S(h * 128, h * 128 + 128)), A("rE3", S(h * 128, h * 128 + 128)), A("pA0", S(h * 128, h * 128 + 128), 0), OP.add)
     for h in (0, 1):
         c = S(h * 128, h * 128 + 128)
-        cp(A("acc", c), A("rE3", c))
-        tt(A("ms0", c), A("acc", c), A("pA1", c, 0), OP.mult)
-        tt(A("yes", c), A("ms0", c), A("pA0", c, 0), OP.add)
+        tt(A("yes", c), A("ms0", c), A("pA0", c, 1), OP.mult)
         dma("YS"[h], [(H(T.ye[:, c]), A("yes", c))], "dye%d" % h)
 
     need("G", [(s, cnt[s]) for s in cnt])

import numpy as np
from concourse.bass import DstId, RemoteDMATransfer
from concourse.mybir import AluOpType, ActivationFunctionType

OP = AluOpType
AF = ActivationFunctionType
RND = 12582912.0
PEN = 2097152.0
FIRST = 40
LASTCUT = 56
MASK_V = range(8)
KCUT = (72, 110)
CUT = 88
MSPLIT = (36, 60)
DOTS = 6
TAG = [""]

F32, B16, I32, U16 = "float32", "bfloat16", "int32", "uint16"
SCRATCH = {
    "kl": ("sbuf", [128, 256], I32), "ul": ("sbuf", [128, 256], I32),
    "ytk": ("sbuf", [128, 2, 8, 16], I32), "xk": ("sbuf", [128, 256], F32), "zk": ("sbuf", [128, 256], F32),
    "lstk": ("sbuf", [128, 256], U16), "db": ("sbuf", [128, 5, 256], B16), "dp": ("sbuf", [128, 8, 128], B16),
    "lki": ("sbuf", [128, 64], I32), "lku": ("sbuf", [128, 64], U16), "lkk": ("sbuf", [128, 64], B16), "kof": ("sbuf", [128, 64], B16),
    "sh": ("sbuf", [128, 2, 128], B16),
    "a0b": ("sbuf", [128, 256], B16), "il": ("sbuf", [128, 64], U16), "rl": ("sbuf", [128, 64], U16),
    "swin": ("sbuf", [128, 4096], B16), "mwin": ("sbuf", [128, 4096], B16), "cwin": ("sbuf", [128, 2048], B16),
    "meta": ("sbuf", [128, 4096], B16),
    "ax0": ("sbuf", [128, 2048], B16), "ax1": ("sbuf", [128, 2048], B16),
    "df": ("sbuf", [128, 1024], B16), "dabs": ("sbuf", [128, 1024], B16),
    "yg": ("sbuf", [128, 512], F32), "nr": ("sbuf", [128, 128], I32), "lam": ("sbuf", [128, 128], B16), "rn": ("sbuf", [128, 160, 3], F32),
    "d0": ("sbuf", [128, 256], F32), "zs": ("sbuf", [128, 32, 4], F32), "sl0": ("sbuf", [128, 32, 4], F32), "sl1": ("sbuf", [128, 32, 4], F32),
    "kd": ("sbuf", [128, 4, 32], F32), "km": ("sbuf", [128, 4, 2, 16], F32), "ki": ("sbuf", [128, 4, 16, 2], I32),
    "xc": ("sbuf", [128, 4, 64], I32), "xh": ("sbuf", [128, 4, 64], I32), "xy": ("sbuf", [128, 4, 64], F32), "xi": ("sbuf", [128, 4, 64], I32),
    "xw": ("sbuf", [128, 20, 64], F32), "xo": ("sbuf", [128, 4, 64], F32), "xz": ("sbuf", [128, 4, 64], F32), "xl": ("sbuf", [128, 64], U16),
    "one": ("sbuf", [128, 256], F32), "idf": ("sbuf", [128, 144], F32), "idb": ("sbuf", [128, 128], B16),
    "g3": ("sbuf", [128, 8, 3], F32), "gx": ("sbuf", [128, 8, 5, 2], F32), "m32": ("sbuf", [128, 32], F32),
    "pn": ("sbuf", [128, 4], I32), "pf": ("sbuf", [128, 2], F32), "i16": ("sbuf", [128, 16], F32), "e16": ("sbuf", [128, 16], F32),
    "e4": ("sbuf", [128, 4], F32), "hm": ("sbuf", [128, 4], F32), "fc": ("sbuf", [128, 8], F32), "bs": ("sbuf", [128, 24], F32),
    "al": ("sbuf", [128, 8], F32), "mx": ("sbuf", [128, 4, 8, 16], B16),
    "vg": ("sbuf", [128, 8, 9, 2], F32), "dg": ("sbuf", [128, 8, 8, 2], F32), "wg": ("sbuf", [128, 8, 8, 16], B16),
    "vm": ("sbuf", [128, 2, 9, 2], F32), "dm": ("sbuf", [128, 48], F32), "wm": ("sbuf", [128, 8, 48], B16),
    "jj": ("sbuf", [128, 8, 8], F32), "sel": ("sbuf", [128, 4, 8, 16], F32), "sq": ("sbuf", [128, 4, 144], F32),
    "zq": ("sbuf", [128, 2, 144], B16), "zu": ("sbuf", [128, 144], B16), "zc": ("sbuf", [128, 146], B16), "idn": ("sbuf", [128, 128], B16),
    "wi": ("sbuf", [128, 128], B16), "inn": ("sbuf", [128, 4096], B16), "nu": ("sbuf", [128, 32], F32),
    "nb": ("sbuf", [128, 3, 256], B16), "ds": ("sbuf", [128, 2, 128, 2], B16), "r5": ("sbuf", [128, 160], F32),
    "ycs": ("sbuf", [128, 256], F32), "acc": ("sbuf", [128, 256], F32), "yes": ("sbuf", [128, 256], F32),
    "pL": ("psum", [128, 512], F32), "pM": ("psum", [128, 4, 128], F32),
}
for _h in "01":
    for _n, _s, _d in (("yw", [256], F32), ("cl", [128], U16), ("l2", [128], U16), ("ml", [128], U16), ("stk", [256, 2], B16),
                       ("p", [2048], F32), ("q", [2048], F32), ("gm", [2048], B16), ("mg", [2048], B16),
                       ("st", [256, 4], F32), ("zp", [32, 4], F32), ("so", [4, 128], F32)):
        SCRATCH[_n + _h] = ("sbuf", [128] + _s, _d)
    SCRATCH["pK" + _h] = ("psum", [128, 170, 3], F32)
    for _n in ("pA", "pB"): SCRATCH[_n + _h] = ("psum", [128, 256, 2], F32)
for _k in range(4):
    SCRATCH["ra%d" % _k] = ("sbuf", [128, 256], B16)
    SCRATCH["ri%d" % _k] = ("sbuf", [128, 64], U16)
    SCRATCH["ms%d" % _k] = ("sbuf", [128, 256], F32 if _k < 2 else "float16")
    if _k: SCRATCH["rE%d" % _k] = ("sbuf", [128, 256], F32 if _k < 2 else "float16")

_DS = ["dk", "du", "da", "dl", "da0", "dyk", "dxc", "dss", "dmm", "dcw", "dcu", "dm0", "dm1", "dm2", "dm3", "dyc", "dye0", "dye1"]
SEMAPHORES = ["sv", "ss", "sp", "sg", "rl", "aL"] + _DS + ["aA%d" % k for k in range(4)] + ["aI%d" % k for k in range(4)] + ["aE%d" % k for k in range(1, 4)]

ALL = slice(None)


def S(a, b=None, c=None): return slice(a, b, c)


KID, UP, NODE, SKID, KKL, KKR, SIB = range(7)
NODES = [(S(0, 2), S(0, 1), 3, KID), (S(0, 2), S(1, 2), 3, KKL), (S(0, 2), S(2, 3), 3, KKR), (S(0, 2), S(4, 8, 3), 2, KID), (S(0, 2), S(5, 6), 0, KID),
         (S(0, 2), S(6, 7), 0, SKID), (S(0, 1), S(3, 4), 0, NODE), (S(1, 2), S(3, 4), 1, NODE),
         (S(2, 3), S(0, 4, 3), 2, NODE), (S(2, 3), S(1, 3), 3, KID), (S(2, 3), S(4, 5), 3, NODE), (S(2, 3), S(5, 6), 0, SIB), (S(2, 3), S(6, 7), 0, NODE),
         (S(2, 3), S(7, 8), 0, UP), (S(3, 4), S(0, 8, 4), 0, UP), (S(3, 4), S(1, 3), 2, UP), (S(3, 4), S(5, 7), 2, UP), (S(3, 4), S(3, 8, 4), 3, NODE)]


def rank_program(g, core, T, topo):
    me = T.rank_of(core)
    if me is None:
        return
    cores = list(T.cores); N = len(cores)
    peers = [c for c in cores if c != core]
    Q = {"V": g.vector, "S": g.scalar, "P": g.tensor, "G": g, "Y": g.sync}
    SEM = {"V": "sv", "S": "ss", "P": "sp", "G": "sg"}
    cnt = {}; known = {e: {} for e in Q}; snap = {}; wr = {}; rd = {}; bank = {}; masks = {}

    def A(name, *ix, rows=ALL):
        shape = SCRATCH[name][1][1:]
        ix = tuple(ix) if ix else (ALL,)
        key = (name, repr(ix))
        if key not in masks:
            m = np.zeros(shape, bool); m[ix] = True
            masks[key] = int("".join("1" if x else "0" for x in m.reshape(-1)), 2)
        return (T[name][(rows,) + ix], [(name, masks[key])])

    def IN(win, off): return (win[0].indirect(off[0]), win[1] + off[1])

    def need(e, evs):
        best = {}
        for s, v in evs: best[s] = max(best.get(s, 0), v)
        for s in sorted(best, key=lambda k: (k in ("sv", "ss", "sp", "sg"), k)):
            v = best[s]; kn = known[e]
            if kn.get(s, 0) >= v: continue
            Q[e].wait_ge(T.sem[s], v)
            for s2, v2 in snap.get((s, v), {}).items():
                if kn.get(s2, 0) < v2: kn[s2] = v2
            kn[s] = v

    def deps(e, key, r, w, acc=False):
        evs = []
        for n, m in r:
            evs += [ev for m2, k2, ev in wr.get(n, []) if m & m2]
        for n, m in w:
            evs += [ev for m2, k2, ev in wr.get(n, []) if m & m2 and not (acc and k2[:len(key)] == key)]
            evs += [ev for (k2, m2), ev in rd.get(n, {}).items() if m & m2]
        for n, m in r + w:
            evs += [ev for k2, ev in bank.get(n, {}).items() if k2 != key]
        need(e, evs)

    def done(e, key, ev, r, w, part=False):
        snap[ev] = dict(known[e])
        for n, m in w:
            if part: wr[n] = wr.get(n, []) + [(m, key, ev)]
            else:
                wr[n] = [(m2 & ~m, k2, v2) for m2, k2, v2 in wr.get(n, []) if m2 & ~m] + [(m, key, ev)]
                rd[n] = {k: v2 for k, v2 in rd.get(n, {}).items() if k[1] & ~m}
        for n, m in r: rd.setdefault(n, {})[(key, m)] = ev
        for n, m in r + w:
            if SCRATCH[n][0] == "psum": bank.setdefault(n, {})[key] = ev

    held = []

    def weave(*parts):
        runs = []
        for f in parts:
            held.append([]); f(); runs.append(held.pop())
        for k in range(max(len(x) for x in runs)):
            for x in runs:
                if k < len(x): op(*x[k])

    def op(e, calls, r, w, acc=False):
        if held: return held[-1].append((e, calls, r, w, acc))
        r = [x for a in r if isinstance(a, tuple) for x in a[1]]; w = [x for a in w for x in a[1]]
        deps(e, e, r, w, acc)
        s = SEM[e]
        for c in calls:
            c().then_inc(T.sem[s], 1); cnt[s] = cnt.get(s, 0) + 1
        done(e, e, (s, cnt[s]), r, w)

    def dma(e, pairs, sem, part=False):
        r = [x for o, i in pairs for x in i[1]]; w = [x for o, i in pairs for x in o[1]]
        deps(e, "dma" if part else "dma" + sem, r, w, part)
        for o, i in pairs:
            Q[e].dma_start(out=o[0], in_=i[0]).then_inc(T.sem[sem], 16)
        cnt[sem] = 16 * len(pairs)
        done(e, "dma" + sem, (sem, cnt[sem]), r, w, part)

    def H(ap): return (ap, [])

    def send(src, dst, to, rsem):
        deps("G", "send", src[1], [])
        ids = []
        for c in to:
            a = topo.addr(c); ids.append(DstId(rid=a[0], pnc=a[1]))
        g.remote_dma_fused([RemoteDMATransfer(dst_ids=ids, dma_engine_mask=topo.mask(core, to[0]), remote_sem=T.sem[rsem],
                                              srcs=[src[0]], dsts=[dst[0] for c in to])], local_sem=T.sem.rl)
        cnt["rl"] = cnt.get("rl", 0) + len(topo.engines(core, to[0]))

    def val(x): return x[0] if isinstance(x, tuple) else x

    def tt(o, a, b, f): op("V", [lambda: g.vector.tensor_tensor(out=o[0], in0=a[0], in1=b[0], op=f)], [a, b], [o])

    def ts(o, a, s1, f0, s2=None, f1=None):
        if f1 is None: op("V", [lambda: g.vector.tensor_scalar(out=o[0], in0=a[0], scalar1=val(s1), scalar2=None, op0=f0)], [a, s1], [o])
        else: op("V", [lambda: g.vector.tensor_scalar(out=o[0], in0=a[0], scalar1=val(s1), scalar2=val(s2), op0=f0, op1=f1)], [a, s1, s2], [o])

    def cp(o, a): op("V", [lambda: g.vector.tensor_copy(out=o[0], in_=a[0])], [a], [o])

    def scan(o, d0, d1, f):
        op("V", [lambda: g.vector.tensor_tensor_scan(out=o[0], data0=d0[0], data1=d1[0], initial=0.0, op0=OP.mult, op1=f)], [d0, d1], [o])

    def ms(o, c): op("V", [lambda: g.vector.memset(o[0], c)], [], [o])

    def act(o, a, f=AF.Copy, bias=0.0, scale=1.0):
        op("S", [lambda: g.scalar.activation(out=o[0], in_=a[0], func=f, bias=val(bias), scale=val(scale))], [a, bias, scale], [o])

    def mm(group, acc=False):
        op("P", [(lambda q=q: g.tensor.matmul(out=q[0][0], lhsT=q[1][0], rhs=q[2][0], start=q[3], stop=q[4])) for q in group],
           [q[1] for q in group] + [q[2] for q in group], [q[0] for q in group], acc)

    def gsel(o, a, pat, base, cm, cmp_, fill_):
        op("G", [lambda: g.affine_select(out=o[0], in_=a[0], pattern=pat, compare_op=cmp_, fill=fill_, base=base, channel_multiplier=cm)], [a], [o])

    def iota(o, pat, base, cm, small=True):
        op("G", [lambda: g.iota(o[0], pat, base, cm, allow_small_or_imprecise_dtypes=small)], [], [o])

    def tag(s): TAG[0] = s

    def C(name, j): return A(name, S(j, j + 1))
    def E(k): return C("e16", k)
    def spreadcol(o, col): act(o, A("one", S(0, int(np.prod(o[0].shape[1:])))), scale=col)
    def axpy(o, c, x, y): act(o, x, AF.Identity, y, float(c))

    RA = "ra%d" % me
    ne = len(topo.engines(core, peers[0]))
    for k in range(N):
        if k != me:
            wr["ra%d" % k] = [(A("ra%d" % k)[1][0][1], "far", ("aA%d" % k, ne))]
            if k != (me - 1) % N: wr["ri%d" % k] = [(A("ri%d" % k)[1][0][1], "far", ("aI%d" % k, ne))]
    wr["rl"] = [(A("rl")[1][0][1], "far", ("aL", ne))]
    for k in range(1, 4): wr["rE%d" % k] = [(A("rE%d" % k)[1][0][1], "far", ("aE%d" % k, ne))]

    tag("load")
    dma("S", [(A("ul"), H(T.up[:, :]))], "du")
    dma("Y", [(A("kl"), H(T.kid[:, :]))], "dk")
    dma("Y", [(A("ytk", k), H(T.kid[k::2, :])) for k in (0, 1)], "dyk")
    dma("S", [(A("xc", t), H(T.cut0[t::4, :])) for t in range(4)], "dxc")
    dma("Y", [(A(RA), H(T.a[:, :]))], "da")
    dma("Y", [(A("lki"), H(T.lk[:, :]))], "dl")
    dma("Y", [(A("a0b"), H(T.a0[:, :]))], "da0")

    tag("const")
    SR, AND = OP.arith_shift_right, OP.bitwise_and
    iota(C("pn", 0), [[0, 1]], 0, 1, False); iota(A("i16"), [[1, 16]], 0, 0)
    ms(A("one"), 1.0)
    for j, b in enumerate((15, 3)): ts(C("pn", j + 1), C("pn", 0), b, AND)
    ms(A("mx"), 0.0); cp(A("pf"), A("pn", S(1, 3))); ms(A("vm"), 0.0)
    ts(A("e16"), A("i16"), C("pf", 0), OP.is_equal); ts(A("e4"), A("i16", S(0, 4)), C("pf", 1), OP.is_equal)
    ms(A("zq"), 0.0); tt(A("fc"), A("e16", S(0, None, 2)), A("e16", S(1, None, 2)), OP.add)
    for n in ("zu", "zc", "gx", "vg", "cwin"): ms(A(n), 0.0)
    for j, f in enumerate((OP.is_lt, OP.is_ge)): ts(C("hm", j), C("pf", 0), 8, f)
    ms(A("sel"), 0.0)
    gsel(A("m32"), A("one", S(0, 32)), [[-4, 4], [-16, 8]], 0, 1, OP.is_ge, 0.0)
    gsel(A("g3"), A("one", S(0, 24)), [[-16, 8], [0, 3]], 0, 1, OP.is_ge, 0.0)
    gsel(A("m32"), A("m32"), [[4, 4], [16, 8]], 3, -1, OP.is_ge, 0.0)
    gsel(A("g3"), A("g3"), [[16, 8], [0, 3]], 15, -1, OP.is_ge, 0.0)
    gsel(A("idf"), A("one", S(0, 144)), [[-1, 144]], 8, 1, OP.is_equal, 0.0)
    gsel(A("idb"), A("one", S(0, 128)), [[-1, 128]], 0, 1, OP.is_equal, 0.0)
    gsel(A("jj"), A("one", S(0, 64)), [[-16, 8], [-1, 8]], 0, 1, OP.is_equal, 0.0)
    iota(A("kof"), [[256, 4], [0, 16]], 0, 0)
    for y in range(2): gsel(A("sh", y), A("one", S(0, 128)), [[-16, 8], [-1, 8], [0, 2]], -8 * y, 1, OP.is_equal, 0.0)
    gsel(A("jj"), A("jj"), [[-16, 8], [-1, 8]], -8, 1, OP.not_equal, 1.0)
    gsel(A("wi"), A("one", S(0, 128)), [[-1, 8], [0, 16]], 0, 1, OP.is_equal, 0.0)
    GI = A("g3", ALL, 0)
    def G1(k): return A("g3", k, S(0, 1))

    tag("weights0")
    def B(j): return C("bs", j)
    HA, HB, H3, LA, LB, L3, LA1, LB1, L31, T1, HALF, BETA, C2, CN, CT, C3 = range(16)
    act(C("al", 0), C("e4", 0), AF.Identity, -1.0); act(A("al", S(1, 4)), A("e4", S(1, 4)))
    axpy(C("al", 5), -1, C("e4", 3), C("e4", 2)); act(C("al", 6), C("e4", 3)); axpy(C("al", 4), -1, C("e4", 1), C("al", 0))
    axpy(B(BETA), 1, E(0), E(4)); act(B(HALF), E(11), scale=0.5); axpy(B(HA), 1, E(4), E(1)); axpy(B(LA), -1, E(4), E(0))
    for j, (k, c) in enumerate(((6, -5 / 16), (7, 65), (8, 66), (9, -66), (10, 67), (11, 1))):
        axpy(B(BETA), c, E(k), B(BETA)); act(A("mx", ALL, ALL, j), A("m32"), scale=C("al", j))
    act(A("mx", ALL, ALL, 6), A("m32"), scale=C("al", 6))
    for k, c in ((7, -64), (8, -64), (9, 64), (10, -64)): act(A("mx", ALL, ALL, k), A("m32"), scale=float(c))
    axpy(C("dm", 3), PEN, E(8), B(HALF)); axpy(C("dm", 7), PEN, E(10), B(HALF)); axpy(C("dm", 8), PEN, E(7), B(HALF))
    for o, x in ((S(0, 3), E(2)), (S(4, 10, 5), E(3)), (S(5, 6), E(3)), (S(10, 12), E(0)), (S(13, 15), E(1)), (S(6, 7), B(HA)), (S(12, 13), B(LA))):
        spreadcol(A("dm", o), x)
    axpy(C("dm", 3), PEN, E(9), C("dm", 3))
    for q in range(4): act(A("zq", q // 2, S(14 + q % 2, 128, 16)), A("m32", S(8 * q, 8 * q + 8)), scale=1024.0)
    act(A("zu", S(15, 128, 16)), GI, scale=C("fc", UP))
    for j in range(2): act(A("zc", S(15 + j, 130, 16)), GI, scale=C("fc", KID))
    act(A("gx", ALL, 1, 0), GI); act(A("gx", ALL, 2, 1), GI)
    act(C("hm", 2), C("pf", 0), scale=256.0); axpy(C("fc", SIB), 1, E(12), E(5)); spreadcol(A("nb", 1), C("hm", 2))
    for k in range(8): act(A("wm", k, S(0, 15)), A("dm", S(0, 15)), scale=G1(k))
    for k in range(4): act(A("sq", k), A("idf"), scale=C("e4", k))
    act(A("idn"), A("idf", S(8, 136)), scale=-1.0)
    for vq in range(4):
        c = 4 * (vq % 2); act(A("sel", vq, ALL, S(8 * (vq // 2) + c, 8 * (vq // 2) + c + 4)), A("jj", ALL, S(c, c + 4)))

    def V(f, e): return A("vm", f // 2, e, S(f % 2, f % 2 + 1))
    tag("weights")
    for f, e, s, fld in NODES:
        spreadcol(A("vg", 2 * s + f.start // 2, e, S(f.start % 2, (f.stop - 1) % 2 + 1)), C("fc", fld))

    def weights_a():
        tag("weights")
        axpy(B(HB), 1, E(5), E(3)); axpy(B(LB), -1, E(5), E(2))
        act(B(T1), E(11), scale=7 / 16); act(B(C2), E(11), scale=2 / 64)
        axpy(B(CN), 3 / 64, E(11), E(0)); axpy(B(CT), 1 / 64, E(11), E(2)); axpy(B(C3), 3 / 64, E(11), E(3))
        axpy(B(H3), -1, E(6), B(T1)); axpy(B(T1), 1, B(HA), E(2))
        axpy(V(0, 3), -1 / 64, E(10), B(CN)); axpy(V(0, 4), 1 / 64, E(9), B(CT)); axpy(B(C3), -1 / 64, E(9), B(C3)); axpy(B(L3), -1, B(H3), B(T1))
        for e, x in ((1, E(3)), (2, B(LA)), (5, E(0)), (6, E(1)), (7, E(2))): axpy(V(0, e), 1, x, B(C2))
        axpy(B(C3), -2 / 64, E(8), B(C3)); axpy(A("bs", S(LA1, LA1 + 3)), 1, A("bs", S(LA, LA + 3)), E(11))
        for f, e, x in ((1, S(3, 4), E(1)), (2, S(0, 4, 3), E(2)), (2, S(2, 5, 2), E(3)), (2, S(5, 6), E(1)), (2, S(6, 7), E(0)), (2, S(7, 8), B(HA)),
                        (3, S(0, 8, 4), B(HA)), (3, S(1, 3), B(H3)), (3, S(3, 8, 4), E(3)), (3, S(5, 7), B(HB)), (1, S(0, 8, 4), B(LA1)),
                        (1, S(7, 8), B(LA1)), (1, S(1, 3), B(L31)), (1, S(5, 7), B(LB1)), (2, S(1, 2), B(LA1))): spreadcol(V(f, e), x)
        axpy(V(0, 0), 2 / 64, E(7), B(C3))

    def grandchildren(a, b, e=act):
        tag("kk")
        e(A("meta", S(16 * a, 16 * b)), IN(A("cwin"), A("lstk", S(a, b))))

    def spread(vis):
        tag("spread")
        b = (me - vis) % N
        for r in range(16):
            gsel(A("ax%d" % (vis % 2), S(r, None, 16)), A("ra%d" % b, S(128 * (r // 8), 128 * (r // 8) + 128)), [[0, 128]], 1, 0, OP.is_gt, 0.0)

    tag("bytes")
    cp(A("db", 1), A("kl")); cp(A("db", 3), A("ul")); tt(A("db", 0), A("kl"), A("db", 1), OP.subtract)
    for j in (1, 3, 0, 2): cp(A("dp", j), A("db", j % 2, S(j // 2, None, 2)))
    dma("Y", [(A("cwin", rows=S(8 + j, None, 16)), A("dp", j)) for j in range(4)], "dcw", True)
    tt(A("db", 2), A("ul"), A("db", 3), OP.subtract); ts(A("db", 4), A("kl"), 0, OP.is_lt, -256.0, OP.mult)
    for j in (1, 0): cp(A("dp", 4 + j), A("db", 2 + j, S(0, None, 2)))
    dma("Y", [(A("cwin", rows=S(2 + j, None, 16)), A("dp", 4 + j)) for j in range(2)], "dcu", True)
    dma("Y", [(A("inn", rows=S(0, 8)), A("db", 4))], "dm0")
    dma("Y", [(A("swin", S(0, 2048)), H(T.s[:, 0:2048]))], "dss")
    dma("Y", [(A("swin", S(2048, 4096)), H(T.s[:, 2048:4096]))], "dm3")
    tag("lstk")
    for b in range(8):
        cp(A("xk", S(32 * b, 32 * b + 32)), A("ytk", ALL, b))
    cp(A("lku"), A("lki"))
    op("V", [lambda: g.vector.transpose(out=T.zk[:, :], in_=T.xk[:, :])], [A("xk")], [A("zk")])
    cp(A("lkk"), A("lki"))
    for b in range(8):
        ts(A("lstk", S(b, None, 8)), A("zk", S(32 * b, 32 * b + 32)), 0.5, OP.mult)
    iota(A("nb", 0), [[1, 256]], 0, 0); iota(A("nb", 2), [[2, 128], [-1, 2]], 1, 0)
    spread(0)
    send(A(RA), A(RA), peers, "aA%d" % me)
    send(A("lku"), A("rl"), [cores[(me + 1) % N]], "aL")
    tag("const")
    gsel(A("r5"), A("one", S(0, 160)), [[0, 32], [1, 5]], 0, 0, OP.is_gt, 0.0)
    iota(A("d0", S(0, None, 8)), [[0, 32]], 0, 0)

    def W(k, n=1): return A("xw", S(k, k + n))
    def P(k, n=1): return A("pB0", S(64 * (k % 4), 64 * (k % 4 + n)), k // 4)

    def pairs_first():
        tag("cut0")
        ts(A("xh"), A("xc"), 1, SR)
        for t in range(4): ts(A("xy", t), A("xc", t), (7 - 2 * t) / 16, OP.add)
        for o, i, j in ((P(0), 0, 2), (P(1), 0, 3), (P(2), 2, 3), (W(0), 1, 3), (W(1), 1, 2), (W(2), 0, 1)): tt(o, A("xh", i), A("xh", j), OP.is_equal)
        tt(W(8), A("xy", 2), A("xy", 1), OP.subtract); tt(W(9), A("xy", 3), A("xy", 1), OP.subtract)
        tt(P(4, 2), P(0, 2), W(0, 2), OP.max)
        tt(W(3), W(2), P(0), OP.max); tt(P(3), P(2), W(0), OP.max)
        tt(P(6, 2), W(8, 2), P(4, 2), OP.mult)
        tt(W(10), W(3), P(1), OP.max); tt(P(2), P(3), W(1), OP.max)
        tt(W(12), A("xy", 1), P(6), OP.add); tt(A("xo", S(2, 4)), A("xy", S(2, 4)), P(6, 2), OP.subtract)
        tt(P(0), P(2), W(10), OP.is_gt)
        tt(A("xy", 1), W(12), P(7), OP.add)
        tt(W(14), A("xo", 2), A("xy", 0), OP.subtract); tt(W(15), A("xo", 3), A("xy", 1), OP.subtract)
        for j in range(2): tt(P(4 + j), W(14 + j), P(0), OP.mult)
        tt(P(3), P(2), W(10), OP.max); tt(W(11), P(2), W(10), OP.mult)
        tt(A("xz", S(0, 2)), A("xy", S(0, 2)), P(4, 2), OP.add); tt(A("xz", S(2, 4)), A("xo", S(2, 4)), P(4, 2), OP.subtract)
        ts(A("xh", 0), A("xz", 0), 0.5, OP.mult, -0.25, OP.add); ts(W(11), W(11), 2 / 64, OP.mult, 1 / 64, OP.add)
        cp(A("xl"), A("xh", 0)); ts(A("xh", S(2, 4)), A("xz", S(2, 4)), 0.5, OP.mult, -0.25, OP.add)
        act(A("mg0", S(0, 1024)), IN(A("cwin"), A("xl")))
        mm([(A("pL", S(0, 64)), A("zu", S(15 - l, 143 - l)), A("mg0", S(l, 1024, 16)), l == 0, l == 15) for l in range(16)])

    def uncle_next():
        tag("cut0b")
        ts(A("xi", 1), A("pL", S(0, 64)), 0.5, OP.mult, -0.25, OP.add)
        tt(W(4), A("xz", 3), A("xz", 2), OP.subtract)
        tt(P(1), A("xi", 1), A("xh", 3), OP.is_equal); tt(W(2), A("xi", 1), A("xh", 2), OP.is_equal)
        tt(P(4), W(4), P(1), OP.mult); tt(W(5), W(2), P(1), OP.add)
        tt(A("xo", 2), A("xz", 2), P(4), OP.add); ts(P(5), W(5), 1 / 64, OP.mult); tt(A("xo", 3), A("xz", 3), P(4), OP.subtract)
        tt(W(6), W(11), P(5), OP.add); cut_rows((2, 3))
        tt(P(6), W(6), P(3), OP.mult); tt(A("xo", 0), A("xz", 0), P(6), OP.add); cut_rows((0,))

    def choose_a(kept, lk, a):
        for k in range(4):
            tt(A("df", S(256 * k, 256 * k + 256)), IN(A(kept), A(lk, S(16 * k, 16 * k + 16))), A(a), OP.subtract)
        act(A("dabs"), A("df"), AF.Abs)

    def choose_p():
        for j in range(4):
            h, y = j // 2, j % 2; o = A("pM", j, S(0, 64))
            mm([(o, A("sh", y), A("lkk"), True, False), (o, A("sh", y), A("kof"), False, False)]
               + [(o, A("zq", h, S(14 - 2 * x, 142 - 2 * x)), A("dabs", S(8 * y + x, None, 16)), False, x == 7) for x in range(8)])

    def choose_b(out, between):
        for y in range(2): cp(A("kd", S(y, None, 2)), A("pM", S(y, None, 2), S(32, 64)))
        for y in range(2): tt(A("km", S(y, None, 2)), A("pM", S(y, None, 2), S(0, 32)), A("kd", S(y, None, 2)), OP.min)
        for y in range(2): tt(A("ki", S(0, 2), ALL, y), A("km", S(y, None, 2), 0), A("km", S(y, None, 2), 1), OP.min)
        between(0); ts(A("ki", S(2, 4)), A("ki", S(0, 2)), 255, AND)
        between(1); cp(A(out), A("ki", S(2, 4)))

    def choose_s(kept, lk, a):
        act(A("df"), IN(A(kept), A(lk)))
        for k in range(4):
            o = A(("pA1", "pB1")[k // 2], ALL, k % 2)
            mm([(o, A("idb"), A("df", S(256 * k, 256 * k + 256)), True, False), (o, A("idn"), A(a), False, True)])

    def choose_abs():
        for k in range(4): act(A("dabs", S(256 * k, 256 * k + 256)), A(("pA1", "pB1")[k // 2], ALL, k % 2), AF.Abs)

    def mask_bank(k): return A(("pA0", "pA1", "pB1")[k % 3])

    def mask_p(ks):
        tag("mask")
        for k in ks:
            c = S(512 * k, 512 * k + 512)
            mm([(mask_bank(k), A("wi", rows=S(0, 8)), A("inn", c, rows=S(0, 8)), True, k in MASK_V)]
               + ([] if k in MASK_V else [(mask_bank(k), A("idb"), A("swin", c), False, True)]))

    def mask(ks):
        tag("mask")
        for k in ks:
            c = S(512 * k, 512 * k + 512)
            if k in MASK_V: tt(A("swin", c), A("swin", c), mask_bank(k), OP.add)
            else: act(A("swin", c), mask_bank(k))

    def cut_rows(slots):
        tag("cut0p")
        mm([(A("pL", S(256 + 64 * w, 320 + 64 * w)), A("sq", w, S(8 + w - s, 136 + w - s)), A("xz" if s == 1 else "xo", s), (s, w) == (1, 0), (s, w) == (0, 3))
            for s in slots for w in range(4)], slots[0] != 1)

    def table_rows():
        tag("kk")
        for j in range(2): cp(A("ds", j, ALL, S(None, None, -1)), A("db", j))
        rows = [A("db", j) for j in range(4)] + [A("nb", 0), A("nb", 1), A("ds", 0), A("ds", 1), A("nb", 2)]
        dma("Y", [(A("meta", rows=S(j if j < 8 else 12, None, 16)), x) for j, x in enumerate(rows)], "dm1")
        dma("Y", [(A("mwin"), H(T.m[:, :]))], "dmm")

    def first_cuts():
        tag("first")
        for h in range(2): act(A("yw%d" % h), A("pL", S(256, 512)), scale=C("hm", h))

    def weights_b():
        tag("weights")
        tt(A("vm", 0, ALL, 1), A("vm", 0, ALL, 1), A("vm", 0, ALL, 0), OP.subtract)
        tt(A("vg", S(0, 4, 2), ALL, 1), A("vg", S(0, 4, 2), ALL, 1), A("vg", S(0, 4, 2), ALL, 0), OP.subtract)
        tt(A("dm", S(16, 48)), A("vm", ALL, S(0, 8)), A("vm", ALL, S(1, 9)), OP.subtract)
        tt(A("dg"), A("vg", ALL, S(0, 8)), A("vg", ALL, S(1, 9)), OP.subtract)

    def weights_c():
        tag("weights")
        for k in range(8): act(A("wm", k, S(16, 48)), A("dm", S(16, 48)), scale=G1(k))
        for k in range(8): act(A("wg", k), A("dg"), scale=G1(k))

    IDF = A("idf", S(8, 136))
    Y, TN = A("pL", S(0, 128)), A("pL", S(256, 384))

    def inherit(h, vis):
        tag("inh%d%d" % (vis, h))
        lst = "il" if vis == 0 else "ri%d" % ((me - vis) % N)
        for vh in range(2):
            act(A("yg", S(256 * vh, 256 * vh + 256)), IN(A("yw%d" % h), A(lst, S(32 * h + 16 * vh, 32 * h + 16 * vh + 16))))
            mm([(Y, A("sel", 2 * vh + q), A("yg", S(256 * vh + q, 256 * vh + 256, 2)), q + vh == 0, q + vh == 2) for q in range(2)], vh > 0)

    def lists(h, vis):
        tag("cl %d%d" % (vis, h))
        cp(A("nr"), Y); cp(A("cl%d" % h), Y)

    def fraction(h, vis):
        tag("cl %d%d" % (vis, h))
        tt(A("lam"), Y, A("nr"), OP.subtract)

    def table(h, vis):
        tag("gm %d%d" % (vis, h))
        act(A("gm%d" % h), IN(A("meta"), A("cl%d" % h)))

    def mix(h, vis):
        tag("mix%d%d" % (vis, h))
        mm([(A("pB%d" % h, S(128 * (vq % 2), 128 * (vq % 2) + 128), vq // 2), A("mx", vq), A("lam"), True, True) for vq in range(4)])

    def stack(h, vis):
        tag("mix%d%d" % (vis, h))
        act(A("stk%d" % h), A("pB%d" % h), AF.Relu, C("bs", 11))

    def STK(h, vq): return A("stk%d" % h, S(128 * (vq % 2), 128 * (vq % 2) + 128), vq // 2)

    def marks(h, vis):
        tag("mrk%d%d" % (vis, h))
        mm([(A("pK%d" % h, S(40 * vq, 40 * vq + 40)), STK(h, vq), A("wm", ALL, S(0, 15)), vq == 0, False) for vq in range(4)])

    def gather(h, vis, k, a=0, b=128):
        tag("g%d %d%d" % (k, vis, h))
        c = S(16 * a, 16 * b)
        tt(A("pq"[k - 1] + str(h), c), IN(A("swin"), A(("cl%d", "l2%d")[k - 1] % h, S(a, b))), A("ax%d" % (vis % 2), c), OP.mult)

    KEYS = (((3, S(1, 3)), (4, S(1, 3)), (0, S(0, 3)), (1, S(1, 3))), ((2, S(0, 3, 2)), None, (3, S(0, 1)), (4, S(0, 1))))

    def dots(h, vis, k, rs=range(16), a=0, b=128):
        tag("dot%d %d%d" % (k, vis, h))
        grp = []
        for r in rs:
            vq = r // 4; key = KEYS[k - 1][r % 4]
            if key: o, w = A("pK%d" % h, S(40 * vq + key[0], 40 * vq + 40, 5), key[1], rows=S(a, b)), A("g3", ALL, key[1])
            else: o, w = A("pK%d" % h, S(40 * vq, 40 * vq + 40), S(0, 2), rows=S(a, b)), A("gx")
            grp.append((o, A("pq"[k - 1] + str(h), S(16 * a + r, 16 * b, 16)), w, False, k == 2 and r == 15 and b == 128))
        mm(grp, True)

    def list2(h, vis):
        tag("l2 %d%d" % (vis, h))
        grp = [(z, 4 * vq + at, 4 * vq + s) for vq in range(4) for z, at, s in (("zu", 0, 0), ("zu", 1, 2), ("zc", 2, 3))]
        mm([(A("pB%d" % h, S(0, 128), 0), A(z, S(15 - l, 143 - l)), A("gm%d" % h, S(r, None, 16)), i == 0, i == 11) for i, (z, l, r) in enumerate(grp)])

    def list2_v(h, vis):
        tag("l2 %d%d" % (vis, h))
        ts(A("l2%d" % h), A("pB%d" % h, S(0, 128), 0), C("e4", 3), OP.add)

    def fields(h, vis, b, vqs=range(4)):
        tag("fld%d %d%d" % (b, vis, h))
        n = ("pA%d", "pB%d")[b] % h
        for vq in vqs:
            c = S(64 * vq, 64 * vq + 64)
            grp = [(A(n, c), STK(h, vq), A("wm", ALL, S(16 + 16 * b, 32 + 16 * b)), vq == 0, False)]
            for s in ((0, 1, 2, 3), (0, 2, 3))[b]:
                f = (ALL, ALL) if b or s == 0 else (1, S(1, None, 2)) if s == 1 else (0, S(0, None, 2))
                grp.append((A(n, c, f[0]), A("gm%d" % h, S(4 * vq + s, None, 16)), A("wg", ALL, 2 * s + b, f[1]), False, vq == 3 and s == 3))
            mm(grp, vq > 0)

    def decide(h, vis, between=None):
        tag("dec%d%d" % (vis, h))
        k = "pK%d" % h; rn = "rn"; d0 = "d0"; st = "st%d" % h
        ts(A("nu"), A(k, S(1, 160, 5), 0), PEN, OP.is_ge)
        for j in (2, 0, 1):
            c = S(0, 160) if j < 2 else S(159, None, -1)
            scan(A(rn, c, j), A("r5"), A(k, c, j), OP.max)
        tt(A(d0, S(4, None, 8)), A(k, S(0, 160, 5), 2), A(rn, S(0, 160, 5), 2), OP.is_lt)
        tt(A(d0, S(3, None, 8)), A(k, S(1, 160, 5), 2), A(rn, S(1, 160, 5), 2), OP.is_equal)
        for j in range(2):
            tt(A(d0, S(1 + j, None, 4)), A(k, S(3 + j, 160, 5), S(0, 2)), A(rn, S(3 + j, 160, 5), S(0, 2)), OP.is_lt)
            if j == 0: tt(A(d0, S(7, None, 8)), A(d0, S(4, None, 8)), A("nu"), OP.max)
        if between: between()
        tag("dec%d%d" % (vis, h))
        for f in range(4):
            scan(A(st, ALL, f), A(d0), A(("pA%d", "pB%d")[f // 2] % h, ALL, f % 2), OP.add)
            if f == 2: tt(A(st, S(7, None, 8), 1), A(st, S(7, None, 8), 1), A(st, S(7, None, 8), 0), OP.add)

    def turn(h, vis):
        tag("trn%d%d" % (vis, h))
        for vq in range(4): (cp if (h, vis) == (1, 3) else act)(A("zs", S(vq, None, 4)), A("st%d" % h, S(64 * vq + 7, 64 * vq + 64, 8)))
        mm([(TN, A("zs"), IDF, True, True)])

    def rows_of(h, vis):
        tag("trn%d%d" % (vis, h))
        if vis < 3:
            for vh in range(2): act(A("yw%d" % h, S(128 * vh, 128 * vh + 128)), TN, scale=C("hm", vh))

    def keep(h, vis):
        tag("keep%d%d" % (vis, h))
        cp(A("ml%d" % h), TN)

    def m_gather(h, vis, a=0, b=128, e=act):
        tag("mg %d%d" % (vis, h))
        e(A(MG(h, vis), S(16 * a, 16 * b)), IN(A("mwin"), A("ml%d" % h, S(a, b))))

    def MG(h, vis): return ("gm%d" if (h, vis) == (0, 3) else "mg%d") % h

    def m_sum(h, vis=0, a=0, b=128):
        tag("msum%d" % h)
        mm([(A("pM", S(a // 64, b // 64)), A("idb"), A(MG(h, vis), S(16 * a + r, 16 * b, 8)), h == 0 and r == 0, h == 1 and r == 7 and b == 128)
            for r in range(8)], h == 1)

    def m_out(k):
        tag("mout%d" % k)
        for vh in range(2):
            o, x = A("ms%d" % k, S(128 * vh, 128 * vh + 128)), A("pM", S(0, 2), S(vh, None, 2))
            if k < 2: act(o, x)
            else: ts(o, x, -2040.0, OP.add)
        if k: send(A("ms%d" % k), A("rE%d" % k), [cores[(me - k) % N]], "aE%d" % k)

    def places_a(h, b=5, a=0):
        tag("plc%d" % h)
        so = "so%d" % h; y = A("st%d" % h, S(7, None, 8))
        for f in (lambda: ts(A(so, 0), y, RND, OP.add, -RND, OP.add), lambda: tt(A(so, 1), y, A(so, 0), OP.subtract),
                  lambda: ts(A(so, 1), A(so, 1), 32768.0, OP.mult, -2048.0, OP.add),
                  lambda: ts(A(so, 1), A(so, 1), RND * 4096, OP.add, -RND * 4096, OP.add), lambda: tt(A(so, 2), A(so, 1), A(so, 0), OP.add))[a:b]: f()

    def places_b(h):
        tag("plc%d" % h)
        so = "so%d" % h; sl = "sl%d" % h

        def w(k, s): return A(so, k, S(s, None, 4))
        for i in (0, 2):
            tt(w(3, i), w(2, i), w(2, i + 1), OP.max); tt(w(3, i + 1), w(2, i), w(2, i + 1), OP.min)
        tt(A(sl, ALL, 0), w(3, 0), w(3, 2), OP.max); tt(w(0, 0), w(3, 0), w(3, 2), OP.min)
        tt(w(0, 1), w(3, 1), w(3, 3), OP.max); tt(A(sl, ALL, 3), w(3, 1), w(3, 3), OP.min)
        tt(A(sl, ALL, 1), w(0, 0), w(0, 1), OP.max); tt(A(sl, ALL, 2), w(0, 0), w(0, 1), OP.min)
        for vq in range(4): cp(A("zp%d" % (vq // 2), S(2 * h + vq % 2, None, 4)), A(sl, S(8 * vq, 8 * vq + 8)))

    steps = [(h, vis) for vis in range(4) for h in (0, 1)]
    b1 = (me - 1) % N
    tag("choose0"); choose_s("a0b", "lku", RA); grandchildren(KCUT[0], KCUT[1]); tag("choose0"); choose_abs(); mask_p(range(3)); choose_p()
    pairs_first(); cut_rows((1,)); grandchildren(0, KCUT[0], cp); grandchildren(KCUT[1], 256); table_rows(); mask(range(3)); mask_p(range(3, 6))
    uncle_next(); tag("choose0"); choose_b("il", lambda k: mask((3 + k,))); first_cuts(); mask_p((6, 7)); inherit(0, 0); mask((5, 6, 7))
    lists(0, 0); fraction(0, 0); mix(0, 0); inherit(1, 0); gather(0, 0, 1); stack(0, 0); marks(0, 0); weights_a(); table(0, 0); spread(1)
    lists(1, 0); fraction(1, 0); mix(1, 0); stack(1, 0); table(1, 0); gather(1, 0, 1); dots(0, 0, 1); list2(0, 0)
    marks(1, 0); dots(1, 0, 1); weights_b(); weights_c(); list2_v(0, 0)
    gather(0, 0, 2); list2(1, 0); dots(0, 0, 2); tag("choose1"); cp(A("lkk"), A("rl")); choose_a(RA, "rl", "ra%d" % b1)
    list2_v(1, 0); fields(0, 0, 0); fields(0, 0, 1); tag("choose1"); choose_p()
    for i in range(1, 8):
        now = steps[i]
        old = steps[i - 1]
        nxt = steps[i + 1] if i < 7 else None
        if i == 1:
            decide(*old); turn(*old); rows_of(*old); gather(1, 0, 2, 0, FIRST)
            choose_b("ri%d" % b1, lambda k: gather(1, 0, 2, FIRST + 8 * k, FIRST + 8 + 8 * k))
            send(A("ri%d" % b1), A("ri%d" % b1), [cores[(me + 1) % N], cores[(me + 2) % N]], "aI%d" % b1)
        else:
            gather(*now, 1, 0, CUT if nxt else 128); dots(*old, 2); mix(*now); fields(*old, 1); stack(*now)
            decide(*old, lambda: keep(*steps[i - 2])); m_gather(*steps[i - 2], 0, MSPLIT[0]); list2(*now); marks(*now)
            if not nxt: dots(*now, 1, range(DOTS))
            elif i > 2: m_sum((i - 1) % 2)
            turn(*old); m_gather(*steps[i - 2], *MSPLIT); rows_of(*old)
            if nxt: gather(*now, 1, CUT, 128)
            list2_v(*now)
        if nxt: fields(*now, 0)
        if 1 < i < 7: dots(*now, 1, range(DOTS))
        if nxt: inherit(*nxt)
        if i in (4, 6): m_out((i - 4) // 2)
        if i > 1: dots(*now, 1, range(DOTS, 16))
        gather(*now, 2, FIRST + 16 if i == 1 else 0, 128 if nxt else LASTCUT)
        if i > 1: m_gather(*steps[i - 2], MSPLIT[1], 128)
        if nxt: lists(*nxt); table(*nxt); fraction(*nxt)
        else: keep(*old); m_gather(*old); gather(*now, 2, LASTCUT, 128); fields(*now, 0)
        if i in (1, 3): spread(2 + i // 2)
    def sums_so_far():
        tag("out"); tt(A("acc"), A("ms0"), A("rE1"), OP.add); cp(A("pA0", ALL, 1), A(RA))
        ts(C("bs", 20), C("pf", 1), 4096.0, OP.mult, -12288.0, OP.add); ts(A("pB0", ALL, 0), A("acc"), 4080.0, OP.add)
    weave(lambda: places_a(0), sums_so_far)
    fields(1, 3, 1, (0, 1)); dots(1, 3, 2); fields(1, 3, 1, (2, 3)); m_sum(0); m_sum(1)
    decide(1, 3); turn(1, 3); m_out(2); m_sum(0, 3); keep(1, 3)
    for a in (0, 64):
        m_gather(1, 3, a, a + 32); m_gather(1, 3, a + 32, a + 64, cp); m_sum(1, 3, a, a + 64)
    places_a(1, 3); m_out(3); weave(lambda: places_b(0), lambda: (places_a(1, 5, 3), places_b(1)))
    tag("out")
    for vh in range(2): mm([(A("pL", S(128 * vh, 128 * vh + 128)), A("zp%d" % vh), IDF, True, True)])
    act(A("ycs"), A("pL", S(0, 256)), AF.Identity, C("bs", 20))
    dma("Y", [(H(T.yc[:, :]), A("ycs"))], "dyc")
    tt(A("pA0", ALL, 0), A("pB0", ALL, 0), A("rE2"), OP.add)
    for h in (0, 1): tt(A("ms0", S(h * 128, h * 128 + 128)), A("rE3", S(h * 128, h * 128 + 128)), A("pA0", S(h * 128, h * 128 + 128), 0), OP.add)
    for h in (0, 1):
        c = S(h * 128, h * 128 + 128)
        tt(A("yes", c), A("ms0", c), A("pA0", c, 1), OP.mult)
        dma("YS"[h], [(H(T.ye[:, c]), A("yes", c))], "dye%d" % h)

    need("G", [(s, cnt[s]) for s in cnt])
